import numpy as np, ml_dtypes
CORES = [40,64,80,88,96,104,120,144]
N = 8
BF = ml_dtypes.bfloat16
C, T, S, DQ = 1024, 128, 3, 7
PL = N * C; FREE = 31
RANGES = (("mem", 0, 63), ("h", 0, 63), ("pnd", 0, PL - 1), ("due", 0, FREE), ("val", 0, 63), ("w", 0, 255), ("kap", 0, 255), ("th", 0, 1008))
def parts(rng):
    tops = rng.integers(24, 64, (1, 8, 16))
    nm = np.add.accumulate(rng.integers(1, PL // 16, (N, 8, T, 16)), axis=3) + rng.integers(0, PL, (N, 8, T, 1))
    nm = rng.permuted(nm & (PL - 1), axis=3)
    du = np.where(rng.random((N, 8, T, 16)) < 0.2, FREE, rng.integers(0, 9, (N, 8, T, 16))); du[..., :S] = FREE
    return {"mem": (rng.random((N, 8, 16, C)) * (tops[..., None] + 1)).astype(np.int64), "h": rng.integers(0, 64, (N, 8, 16, T)),
            "val": (rng.random((N, 8, 16, T, 16)) * (tops[..., None, None] + 1)).astype(np.int64), "nm": nm, "du": du,
            "w": rng.integers(0, 256, (N, 8, 16)), "kap": rng.integers(0, 256, (N, 8, 16)),
            "th": (np.sum(tops, axis=2) * (0.8 + 0.13 * rng.random((N, 8)))).astype(np.int64)}
def pack(p):
    bf = lambda a: np.ascontiguousarray(a).astype(np.float32).astype(BF)
    i4 = lambda a: np.ascontiguousarray(a).astype(np.int32)
    return {"mem": bf(p["mem"].reshape(N, 128, C)), "h": bf(p["h"].reshape(N, 128, T)),
            "pnd": i4(p["nm"].transpose(0, 1, 3, 2).reshape(N, 128, T)), "due": i4(p["du"].transpose(0, 1, 3, 2).reshape(N, 128, T)),
            "val": bf(p["val"].reshape(N, 128, 16 * T)), "w": i4(p["w"].reshape(N, 128, 1)), "kap": i4(p["kap"].reshape(N, 128, 1)),
            "th": i4(np.repeat(p["th"].reshape(N, 8, 1), 16, axis=2).reshape(N, 128, 1))}
def setup_inputs(rng):
    return pack(parts(rng))
def setup_inputs_corners(rng):
    p = parts(rng); s = np.arange(16); own = p["nm"]; mode = rng.integers(0, 7, (N, 8, T, 1)); mode[..., T - 1, 0] = 4; mode[..., 0, 0] = 1
    e = rng.integers(0, S + 1, (N, 8, T, 1)); q = rng.choice(np.array([0, 1, S - 1, S, 30]), (N, 8, T, 16))
    late = 30 - (rng.random((N, 8, T, 16)) * rng.integers(2, 16, (N, 8, T, 1))).astype(np.int64)
    border = C * rng.integers(0, N, (N, 8, T, 1)) - 8; border[..., T - 1, 0] = -8
    du = np.where(mode == 3, np.where(s == 15, 0, FREE), q); du = np.where(mode == 6, late, du)
    du = np.where(mode == 2, np.where(s == 15, e, 30), du); du = np.where(mode == 1, e, du); du = np.where(mode == 0, FREE, du)
    du[..., :S] = FREE
    nm = np.where(mode == 4, (border + s) & (PL - 1), own)
    nm = np.where(mode == 0, (PL - 1) * rng.integers(0, 2, (N, 8, T, 16)), nm)
    p["w"][:, 2] = 0; p["w"][:, 5] = 255; p["kap"][:, 3] = 0; p["kap"][:, 4] = 255; p["th"][:, 1] = 0; p["th"][:, 6] = 1008
    p["th"][1:3] = 1008
    z = slice(T - 8, T); nm[2, 2, z] = own[2, 2, z]; du[2, 2, z] = FREE; du[2, 2, z, 13] = 30; du[2, 2, z, 15] = 0
    p["val"][2, 2, :, z, 13] = 63; p["val"][2, 2, :, z, 15] = 0
    nm[1, 5] = own[1, 5]; du[1, 5, :, S:] = 30
    p["th"][0, 0] = 0; du[0, 0] = FREE
    for r in (0, N - 1):
        p["th"][r, 4] = 0; nm[r, 4] = own[0, 4]; du[r, 4] = FREE; du[r, 4, :, 15] = 0
    du[0, 4, :, 14] = 1
    p["nm"] = nm; p["du"] = du
    return pack(p)
def setup_inputs_crowd(rng):
    p = parts(rng); s = np.arange(16); i = np.arange(T).reshape(1, 1, T, 1); r = np.arange(N).reshape(N, 1, 1, 1)
    owner = rng.integers(0, N, (N, 8, 1, 1)); owner[:, 2] = 0; owner[:, 5] = N - 1; owner[N - 1] = 0
    col = np.broadcast_to(64 + i + 17 * s, (N, 8, T, 16)).copy(); far = (T * (r + 1) + i + 17 * s) % C
    col[:, 2] = far[:, 0]; col[:, 5] = far[:, 0]
    p["nm"] = C * owner + col
    du = np.zeros((N, 8, T, 16), np.int64); du[..., :S] = FREE; du[:, 2, :, 1::2] = FREE; du[N - 1, :, :, 1::2] = FREE; p["du"] = du
    p["w"][:, 2] = 0; p["w"][N - 1] = 0; p["th"][:] = 0
    return pack(p)
def edge(rng, a, b):
    k = rng.integers(0, 3, a)
    return 63 * np.where(k == 2, rng.integers(0, 2, b), k)
def setup_inputs_ends(rng):
    p = parts(rng); s = np.arange(16)
    mem = edge(rng, (N, 8, 1, C), (N, 8, 16, C)); mem[..., 0] = 0; mem[..., C - 1] = 63
    h = edge(rng, (N, 8, 1, T), (N, 8, 16, T)); val = edge(rng, (N, 8, 1, T, 16), (N, 8, 16, T, 16))
    for g in (1, 5, 7): mem[:, g, 3] = 0
    for g in (1, 5): val[:, g, 3] = 0
    w = 255 * rng.integers(0, 2, (N, 8, 16)); w[:, 1::2, 15] = 65; w[:, 6] = 255
    kap = 255 * rng.integers(0, 2, (N, 8, 16)); kap[:, 1::2, 15] = 255; kap[:, 1::2, 0] = 0
    th = 1008 * rng.integers(0, 2, (N, 8)); th[:, 0] = 0; th[:, 4] = 1008; th[:, 1::2] = 1008; th[0::2, 6] = 1008
    h[:, 1::2, :, T - 1] = 0; h[:, 1::2, 15, T - 1] = 63
    h[:, 6, :, T - 1] = 63; h[:, 0::4, :, T - 1] = 0
    few = rng.random((N, 8, T, 1)) < 0.7
    s1 = rng.integers(S, 16, (N, 8, T, 1)); s2 = S + (s1 - S + rng.integers(1, 16 - S, (N, 8, T, 1))) % (16 - S)
    nm = np.where(s == s1, 0, np.where(s == s2, PL - 1, (PL - 1) * rng.integers(0, 2, (N, 8, T, 16))))
    du = np.where(((s == s1) | (s == s2)) & (rng.random((N, 8, T, 16)) < 0.75), 0, FREE)
    nm = np.where(few, nm, p["nm"]); du = np.where(few, du, np.where((s >= S) & (rng.random((N, 8, T, 16)) < 0.6), 0, FREE))
    nm[:, 0::4, T - 1] = 0; du[:, 0::4, T - 1] = FREE
    u = (16 * 255 * 63) & 4095; e0 = ((u * u) >> 4) & (PL - 1); e1 = (((u * u) >> 4) + 255 * u) & (PL - 1)
    mem[e0 // C, 6, :, e0 % C] = 63; mem[e1 // C, 6, :, e1 % C] = 63
    nm[:, 6, T - 1] = e0; du[:, 6, T - 1] = FREE
    return pack({"mem": mem, "h": h, "val": val, "nm": nm, "du": du, "w": w, "kap": kap, "th": th})
def setup_inputs_meet(rng):
    p = parts(rng); b = np.array([0, 3, 4, 7]); e = np.array([1, 2, 5, 6]); gi = np.arange(8)[None, :, None]; s = np.arange(16)
    pool = p["nm"][0, :, 0].copy()
    nm = rng.permuted(np.broadcast_to(pool[None, :, None, :], (N, 8, T, 16)).copy(), axis=3); nm[:, 4] = pool[4]
    p["nm"][:, b] = nm[:, b]
    du = rng.integers(0, 3, (N, 8, T, 16)); dt = np.where(rng.random((N, 8, T, 16)) < 0.3, FREE, rng.integers(0, 2, (N, 8, T, 16)))
    du[:, e] = dt[:, e]; du[:, 4] = np.where((rng.random((N, T, 1)) < 0.2) & (s > S), FREE, 0); du[..., :S] = FREE; p["du"] = du
    pat = rng.integers(0, 4, (8, 6, 16)) * rng.choice(np.array([1, 3, 20]), (8, 1, 1))
    mem = pat[gi, rng.integers(0, 6, (N, 8, C))].transpose(0, 1, 3, 2)
    h = pat[gi, rng.integers(0, 6, (N, 8, T))].transpose(0, 1, 3, 2)
    val = pat[gi[..., None], rng.integers(0, 6, (N, 8, T, 16))].transpose(0, 1, 4, 2, 3)
    p["mem"][:, e] = mem[:, e]; p["h"][:, e] = h[:, e]; p["val"][:, e] = val[:, e]
    full = np.sum(np.max(pat, axis=1) - np.min(pat, axis=1), axis=1)
    off = rng.permuted(np.resize(np.array([0, 0, 1, -1, -3]), N * 4)).reshape(N, 4)
    p["th"][:, e] = np.maximum(full[e][None, :] + off, 0)
    p["th"][:, 0] = 0; p["th"][:, 4] = 0
    p["h"][:, 3] = p["h"][:1, 3, :, :1].copy(); p["w"][:, 3] = p["w"][:1, 3].copy(); p["kap"][:, 3] = p["kap"][:1, 3].copy()
    return pack(p)
def setup_inputs_spread(rng):
    p = parts(rng)
    p["mem"] = np.minimum((np.exp2(6 * rng.random((N, 8, 1, C))) * rng.random((N, 8, 16, C))).astype(np.int64), 63)
    p["h"] = np.minimum((np.exp2(6 * rng.random((N, 8, 1, T))) * rng.random((N, 8, 16, T))).astype(np.int64), 63)
    p["val"] = np.minimum((np.exp2(6 * rng.random((N, 8, 1, T, 16))) * rng.random((N, 8, 16, T, 16))).astype(np.int64), 63)
    p["w"] = np.minimum(np.exp2(8 * rng.random((N, 8, 16))).astype(np.int64), 255)
    p["th"] = rng.integers(0, 1009, (N, 8))
    du = np.where(rng.random((N, 8, T, 16)) < 0.5, rng.integers(0, 4, (N, 8, T, 16)), rng.integers(0, FREE + 1, (N, 8, T, 16))); du[..., :S] = FREE; p["du"] = du
    return pack(p)
def check_inputs(d):
    bad = []
    for k, lo, hi in RANGES:
        v = np.asarray(d[k]).astype(np.float64)
        if not (np.all(v >= lo) and np.all(v <= hi) and np.all(v == np.floor(v))): bad.append("range of " + k)
    du = np.asarray(d["due"]).astype(np.int64).reshape(N, 8, 16, T); nm = np.asarray(d["pnd"]).astype(np.int64).reshape(N, 8, 16, T)
    if np.any(du[:, :, :S] != FREE): bad.append("slots that start free")
    k = np.sort(np.where(du != FREE, nm, -1 - np.arange(16).reshape(1, 1, 16, 1)), axis=2)
    if np.any(k[:, :, 1:] == k[:, :, :-1]): bad.append("pending names of a thread differ")
    t = np.asarray(d["th"]).reshape(N, 8, 16)
    if np.any(t != t[:, :, :1]): bad.append("th alike in a group")
    return bad
def reference(mem, h, pnd, due, val, w, kap, th):
    whole = lambda a: a.astype(np.float32).astype(np.int64)
    mt = np.ascontiguousarray(whole(mem).reshape(N, 8, 16, C).transpose(1, 0, 3, 2)).reshape(8, PL, 16)
    hh = whole(h).reshape(N, 8, 16, T).transpose(0, 1, 3, 2)
    nm = pnd.astype(np.int64).reshape(N, 8, 16, T).transpose(0, 1, 3, 2).copy()
    du = due.astype(np.int64).reshape(N, 8, 16, T).transpose(0, 1, 3, 2).copy()
    vl = whole(val).reshape(N, 8, 16, T, 16).transpose(0, 1, 3, 4, 2).copy()
    ww = w.astype(np.int64).reshape(N, 8, 1, 16); kk = kap.astype(np.int64).reshape(N, 8, 1, 16); tt = th.astype(np.int64).reshape(N, 8, 16)[:, :, :1]
    A = np.zeros((N, 1, 1, 1), np.int64); s16 = np.arange(16); gi = np.arange(8).reshape(1, 8, 1, 1)
    for t in range(S):
        u = (np.sum(ww * hh, axis=3) & 4095)[..., None]
        z = ((u * u) >> 4) + kk * u + A
        a = np.where((s16 & 1) == 0, z, np.where(((z >> 3) & 1) == 1, nm + z, nm)) & (PL - 1)
        pend = du != FREE
        hit = (a[..., :, None] == nm[..., None, :]) & pend[..., None, :]
        x = np.where(np.any(hit, axis=4)[..., None], np.take_along_axis(vl, np.argmax(hit, axis=4)[..., None], 3), mt[gi, a])
        hi = np.max(x, axis=3); lo = np.min(x, axis=3); y = (hi + lo) >> 1
        score = np.sum(np.abs(x - hh[..., None, :]), axis=4)
        b = np.take_along_axis(a, np.argmax(score, axis=3)[..., None], 3)
        fence = np.sum(hi - lo, axis=3) >= tt
        same = (nm == b) & pend; had = np.any(same, axis=3)
        put = np.where(had[..., None], same, s16 == t) & ~fence[..., None]
        vl = np.where(put[..., None], y[..., None, :], vl); nm = np.where(put, b, nm)
        du[..., t] = np.where(~had & ~fence, t + 1 + (np.sum(y, axis=3) & DQ), du[..., t])
        sl = np.argmin(du, axis=3)[..., None]; least = np.take_along_axis(du, sl, 3)[..., 0]
        go = (least != FREE) & (fence | (least <= t))
        place = np.take_along_axis(nm, sl, 3)[..., 0]; value = np.take_along_axis(vl, sl[..., None], 3)[..., 0, :]
        du = np.where(go[..., None] & (s16 == sl), FREE, du)
        for g in range(8):
            m = go[:, g].reshape(-1); v = value[:, g].reshape(-1, 16)[m]
            first, at = np.unique(place[:, g].reshape(-1)[m], return_index=True)
            mt[g, first] = v[at]
        hh = np.abs(y - hh); A = (np.sum(fence, axis=(1, 2)) & 63).reshape(N, 1, 1, 1)
    bf = lambda e: np.ascontiguousarray(e).astype(np.float32).astype(BF)
    return {"ymem": bf(mt.reshape(8, N, C, 16).transpose(1, 0, 3, 2).reshape(N, 128, C)), "yh": bf(hh.transpose(0, 1, 3, 2).reshape(N, 128, T)),
            "ypnd": np.ascontiguousarray(nm.transpose(0, 1, 3, 2).reshape(N, 128, T)).astype(np.float32),
            "ydue": np.ascontiguousarray(du.transpose(0, 1, 3, 2).reshape(N, 128, T)).astype(np.float32),
            "yval": bf(vl.transpose(0, 1, 4, 2, 3).reshape(N, 128, 16 * T))}

@@ -1,0 +1,599 @@
+from concourse.mybir import dt, AluOpType as O, AxisListType, ActivationFunctionType as F
+from concourse.bass import DstId, RemoteDMATransfer
+
+NR, C, TH, STEPS = 8, 1024, 128, 3
+DUMP = NR * C
+VB = DUMP + TH
+VD = VB + 16 * TH
+WEND = VD + 16 * TH
+PW = 144
+MAGIC = 12582912.0
+POS = [2, 1, 0] + list(range(3, 16))
+NB = 48
+TA = TH - NB
+
+S, P = "sbuf", "psum"
+SCRATCH = {
+    "W": (S, [128, WEND], "bfloat16"), "vv": (S, [128, 16 * TH], "bfloat16"),
+    "hb": (S, [128, 256], "bfloat16"),
+    "pI": (S, [128, 1], "int32"), "mI": (S, [128, 128], "int32"), "dI": (S, [128, 128], "int32"),
+    "ci1": (S, [128, 4], "int32"), "cols": (S, [128, 16], "float32"), "cT": (S, [128, 3], "float32"),
+    "md": (S, [128, 128], "int32"), "mm": (S, [128, 128], "int32"),
+    "I32": (S, [128, 128], "float32"), "Ib": (S, [128, 128], "bfloat16"), "nI": (S, [128, 128], "bfloat16"),
+    "I2": (S, [128, 128], "bfloat16"), "oddI": (S, [128, 128], "bfloat16"), "I8k": (S, [128, 128], "bfloat16"),
+    "I16k": (S, [128, 128], "bfloat16"),
+    "B": (S, [128, 128], "bfloat16"), "nB": (S, [128, 128], "bfloat16"), "dl": (S, [128, 128], "bfloat16"),
+    "ofd": (S, [128, 128], "bfloat16"), "dc": (S, [128, 8], "float32"), "B8th": (S, [128, 8], "bfloat16"),
+    "Bm32": (S, [128, 8], "bfloat16"), "c716": (S, [128, 8], "bfloat16"), "c960": (S, [128, 24], "bfloat16"),
+    "B16": (S, [128, 8], "bfloat16"), "dc128": (S, [128, 8], "bfloat16"), "Cl": (S, [128, 8], "bfloat16"),
+    "Cd": (S, [128, 8], "float32"), "rh2": (S, [128, 8], "float32"), "oh16": (S, [128, 16], "float32"),
+    "Sel": (S, [128, 2048], "bfloat16"), "KZ": (S, [128, 2048], "bfloat16"),
+    "TK": (S, [128, 128], "bfloat16"), "RS": (S, [128, 128], "float32"),
+    "xl": (S, [128, 8], "uint16"), "hl": (S, [128, 128], "uint16"),
+    "r1": (S, [128, 2048], "bfloat16"), "r2": (S, [128, 2048], "bfloat16"),
+    "tri": (S, [128, 128], "bfloat16"), "on1": (S, [128, 1024], "bfloat16"), "Sel0": (S, [128, 1024], "bfloat16"),
+    "nn": (S, [128, 8], "float32"), "on32": (S, [128, 128], "float32"), "t8k": (S, [128, 128], "bfloat16"),
+    "mh": (S, [128, 128], "bfloat16"), "ib": (S, [128, 128], "bfloat16"),
+    "wI": (S, [128, 1], "int32"), "kI": (S, [128, 1], "int32"), "tI": (S, [128, 1], "int32"),
+    "Wb": (S, [128, 128], "bfloat16"), "thd": (S, [128, 128], "float32"), "thE": (S, [128, 128], "float32"),
+    "th2": (S, [128, 128], "float32"),
+    "L1": (S, [128, 128], "int32"), "L2": (S, [128, 128], "int32"), "f1": (S, [128, 128], "float32"),
+    "f2": (S, [128, 128], "float32"),
+    "h0": (S, [128, 128], "bfloat16"), "h1": (S, [128, 128], "bfloat16"),
+    "nm": (S, [128, 128], "float32"), "pri": (S, [128, 128], "float32"),
+    "fr": (S, [128, 128], "bfloat16"), "qh": (S, [128, 128], "bfloat16"), "ql": (S, [128, 128], "bfloat16"),
+    "i1": (S, [128, 128], "int32"), "i2": (S, [128, 128], "int32"), "i3": (S, [128, 128], "int32"),
+    "i4": (S, [128, 128], "int32"), "i5": (S, [128, 128], "int32"), "i6": (S, [128, 128], "int32"),
+    "aI": (S, [128, 128], "int32"), "hit": (S, [128, 2048], "bfloat16"), "off": (S, [128, 128], "float32"),
+    "lst": (S, [128, 128], "uint16"), "hr": (S, [128, 2048], "bfloat16"), "d": (S, [128, 2048], "bfloat16"),
+    "ad": (S, [128, 2048], "bfloat16"), "sh": (S, [128, 2048], "bfloat16"), "sl": (S, [128, 2048], "bfloat16"),
+    "M0": (S, [128, 128], "float32"), "eq0": (S, [128, 128], "bfloat16"), "e1k": (S, [128, 128], "bfloat16"),
+    "N0": (S, [128, 128], "float32"), "n0c": (S, [128, 128], "float32"),
+    "sI": (S, [128, 128], "int32"), "sd": (S, [128, 128], "bfloat16"), "vl": (S, [128, 8], "uint16"),
+    "x1": (S, [128, 128], "bfloat16"), "x2": (S, [128, 128], "bfloat16"), "An": (S, [128, 128], "float32"),
+    "nh": (S, [128, 128], "bfloat16"), "nl": (S, [128, 128], "bfloat16"), "dab": (S, [128, 1024], "bfloat16"),
+    "eq": (S, [128, 1024], "bfloat16"), "y1": (S, [128, 128], "float32"), "yb": (S, [128, 128], "bfloat16"),
+    "ME": (S, [128, 128], "float32"), "oh": (S, [128, 128], "float32"), "no": (S, [128, 128], "float32"),
+    "PS": (S, [128, 128], "float32"), "SE": (S, [128, 128], "float32"), "go": (S, [128, 128], "bfloat16"),
+    "Fd": (S, [128, 128], "float32"), "r8": (S, [128, 16], "float32"),
+    "tg": (S, [128, 128], "float32"), "l1": (S, [128, 128], "float32"), "l2": (S, [128, 128], "float32"),
+    "sl16": (S, [128, 8], "uint16"), "sm": (S, [128, 64], "float32"),
+    "Ac": (S, [128, 8], "float32"), "rv": (S, [128, STEPS, NR, PW], "bfloat16"), "dcd": (S, [128, 64], "float32"),
+    "dL": (S, [128, 64], "uint16"),
+    "pn": (P, [128, 2048], "float32"), "pk": (P, [128, 512], "float32"), "p5": (P, [128, 512], "float32"),
+    "p6": (P, [128, 512], "float32"), "p7": (P, [128, 512], "float32"),
+}
+SEMAPHORES = ["qg", "qv", "qs", "qt", "ag", "lsA", "lsD", "hin", "hout"] + ["dr%d" % t for t in range(STEPS)] \
+    + ["rl%d" % t for t in range(STEPS)] + ["dm%d" % k for k in range(16)]
+
+
+def dst(topo, d, src):
+    rid, pid = topo.addr(d, src)
+    return DstId(rid=rid, pnc=pid)
+
+
+def bits(es):
+    m = 0
+    for e in es:
+        m |= 1 << e
+    return m
+
+
+def roles(T, topo, r):
+    me = T.cores[r]
+    near = [q for q in range(NR) if q != r and topo.may_write(me, T.cores[q])]
+    far = [q for q in range(NR) if q != r and q not in near]
+    chip = [c for c in topo.cores_of(me) if c != me]
+    car = [c for c in chip if topo.may_write(c, T.cores[far[0]])]
+    car = sorted(car, key=lambda c: (topo.die(c) != topo.die(me), c))
+    plain = [c for c in chip if c not in car]
+    a = sum(q < r for q in near)
+    relay = [(car[(a + b) % 2 * 2 + b // 2], q) for b, q in enumerate(far)]
+    return near, far, car, plain, relay
+
+
+def helper_program(g, core, T, topo):
+    for r in range(NR):
+        me = T.cores[r]
+        if core not in topo.cores_of(me):
+            continue
+        near, far, car, plain, relay = roles(T, topo, r)
+        n = 0
+        if core in car or core in plain:
+            serve = far if core in car else near
+            lo = r * C + 256 * (car.index(core) if core in car else 1 + plain.index(core))
+            es = topo.engines(core, T.cores[serve[0]])
+            g.wait_ge(T.sem.hin, 2)
+            g.remote_dma_fused([RemoteDMATransfer(dst_ids=[dst(topo, T.cores[q], core) for q in serve], dma_engine_mask=bits(es),
+                                                  remote_sem=T.sem.ag, srcs=[T.hb[:]],
+                                                  dsts=[T.W[:, lo:lo + 256] for q in serve])], local_sem=T.sem.hout)
+            n += len(es)
+        for c, q in relay:
+            if c != core:
+                continue
+            es = topo.engines(core, T.cores[q])
+            for t in range(STEPS):
+                g.wait_ge(T.sem["rl%d" % t], 4)
+                g.remote_dma_fused([RemoteDMATransfer(dst_ids=[dst(topo, T.cores[q], core)], dma_engine_mask=bits(es),
+                                                      remote_sem=T.sem["dr%d" % t], srcs=[T.rv[:, t, r, :]],
+                                                      dsts=[T.rv[:, t, r, :]])], local_sem=T.sem.hout)
+                n += len(es)
+        if n:
+            g.wait_ge(T.sem.hout, n)
+
+
+def rank_program(g, core, T, topo):
+    rank = T.rank_of(core)
+    if rank is None:
+        helper_program(g, core, T, topo)
+        return
+    near, far, car, plain, relay = roles(T, topo, rank)
+
+    Q = {"g": g, "v": g.vector, "s": g.scalar, "t": g.tensor, "y": g.sync}
+    cnt, seen, log, ndma = {}, {q: {} for q in Q}, {}, [0]
+
+    def A(name, *idx):
+        ap = T[name]
+        shape = [int(x) for x in ap.shape][1:]
+        idx = idx + (slice(None),) * (len(shape) - len(idx))
+        lo = hi = 0
+        for n, i in zip(shape, idx):
+            if isinstance(i, slice):
+                a, b, st = i.indices(n)
+                last = a + (b - 1 - a) // st * st
+            else:
+                a = last = i
+            lo, hi = lo * n + a, hi * n + last
+        return {"ap": ap[(slice(None),) + idx], "n": name, "r": (lo, hi + 1), "ind": None}
+
+    def ind(win, offs):
+        return {"ap": win["ap"].indirect(offs["ap"]), "n": win["n"], "r": win["r"], "ind": offs}
+
+    def spans(v):
+        lo, hi = v["r"]
+        if v["n"] in SCRATCH and SCRATCH[v["n"]][0] == P:
+            return True, lo // 512 * 512, (hi + 511) // 512 * 512
+        return False, lo, hi
+
+    def need(q, v, write, acc):
+        ps, lo, hi = spans(v)
+        for e in log.get(v["n"], []):
+            if e["lo"] < hi and lo < e["hi"]:
+                same = e["q"] == q
+                if same and (ps and q == "t" or not e["w"]):
+                    continue
+                if e["w"] or write or ps and not same:
+                    acc.append(e["tok"])
+
+    def note(q, v, write, tok):
+        ps, lo, hi = spans(v)
+        L = log.setdefault(v["n"], [])
+        if write:
+            L[:] = [e for e in L if not (lo <= e["lo"] and e["hi"] <= hi and not ps)]
+        if ps:
+            L[:] = [e for e in L if not (e["q"] == q and e["w"] == write and e["lo"] == lo and e["hi"] == hi)]
+        L.append({"lo": lo, "hi": hi, "w": write, "q": q, "tok": tok})
+
+    def settle(q, toks):
+        best = {}
+        for s, n, snap in toks:
+            if seen[q].get(s, 0) < n and best.get(s, (0, 0))[0] < n:
+                best[s] = (n, snap)
+        for s in list(best):
+            if any(o != s and best[o][1].get(s, 0) >= best[s][0] for o in best):
+                del best[s]
+        for s in best:
+            n, snap = best[s]
+            Q[q].wait_ge(T.sem[s], n)
+            for k in snap:
+                seen[q][k] = max(seen[q].get(k, 0), snap[k])
+            seen[q][s] = n
+
+    calls = {"t": {"matmul": g.tensor.matmul, "transpose": g.tensor.transpose},
+             "s": {"activation": g.scalar.activation, "dma_start": g.scalar.dma_start},
+             "y": {"dma_start": g.sync.dma_start}, "g": {"iota": g.iota, "affine_select": g.affine_select},
+             "v": {"tensor_copy": g.vector.tensor_copy, "tensor_tensor": g.vector.tensor_tensor, "memset": g.vector.memset,
+                   "tensor_scalar": g.vector.tensor_scalar, "tensor_tensor_scan": g.vector.tensor_tensor_scan}}
+
+    def E(q, meth, _pos=(), **kw):
+        wr, rd = [], []
+        for k, v in list(kw.items()) + [("ap", p) for p in _pos]:
+            if isinstance(v, dict):
+                (wr if k in ("out", "ap", "accum_out") else rd).append(v)
+                if v["ind"]:
+                    rd.append(v["ind"])
+        toks = []
+        for v in rd:
+            need(q, v, False, toks)
+        for v in wr:
+            need(q, v, True, toks)
+        settle(q, toks)
+        un = lambda v: v["ap"] if isinstance(v, dict) else v
+        ins = calls[q][meth](*[un(p) for p in _pos], **{k: un(v) for k, v in kw.items()})
+        if meth == "dma_start":
+            s, n = "dm%d" % ndma[0], 16
+            ndma[0] += 1
+            ins.then_inc(T.sem[s], 16)
+        else:
+            s = "q" + q
+            cnt[s] = n = cnt.get(s, 0) + 1
+            ins.then_inc(T.sem[s], 1)
+        tok = (s, n, dict(seen[q]))
+        dq = q if meth != "dma_start" else "dma"
+        for v in rd:
+            note(dq, v, False, tok)
+        for v in wr:
+            note(dq, v, True, tok)
+
+    def cp(out, in_):
+        E("v", "tensor_copy", out=out, in_=in_)
+
+    def tt(out, a, b, op):
+        E("v", "tensor_tensor", out=out, in0=a, in1=b, op=op)
+
+    def ts(out, a, s1, op0, s2=None, op1=None):
+        if op1 is None:
+            E("v", "tensor_scalar", out=out, in0=a, scalar1=s1, scalar2=None, op0=op0)
+        else:
+            E("v", "tensor_scalar", out=out, in0=a, scalar1=s1, scalar2=s2, op0=op0, op1=op1)
+
+    def act(out, in_, func=F.Identity, **kw):
+        E("s", "activation", out=out, in_=in_, func=func, **kw)
+
+    def mm(out, lhsT, rhs, start, stop):
+        E("t", "matmul", out=out, lhsT=lhsT, rhs=rhs, start=start, stop=stop)
+
+    def tr(out, in_):
+        E("t", "transpose", out=out, in_=in_, identity=A("I32"))
+
+    def group(out, pairs):
+        for k, (a, b) in enumerate(pairs):
+            mm(out, a, b, k == 0, k == len(pairs) - 1)
+
+    def scan(out, d0, d1, op0, op1, init):
+        E("v", "tensor_tensor_scan", out=out, data0=d0, data1=d1, initial=init, op0=op0, op1=op1)
+
+    def fill(v, x):
+        E("v", "memset", (v, x))
+
+    def ext(name):
+        return {"ap": T[name][:], "n": name, "r": (0, 1), "ind": None}
+
+    c = slice
+    COLS = ["pdf", "pmf", "pf", "odd", "ev8", "nbc", "key", "wf", "k16", "tf"]
+    K_ = lambda n: A("cols", c(COLS.index(n), COLS.index(n) + 1))
+    blk = lambda n, k: A(n, c(128 * k, 128 * k + 128))
+    spread = lambda n: ind(A(n), A("xl"))
+    vslot = lambda s: A("W", c(VB + 128 * POS[s], VB + 128 * POS[s] + 128))
+    H = ["h0", "h1"]
+
+    def slots(t):
+        return [s for s in range(16) if s >= STEPS or s < t]
+
+    E("y", "dma_start", out=A("W", c(rank * C, rank * C + C)), in_=ext("mem"))
+    E("s", "dma_start", out=A("L1"), in_=ext("pnd"))
+    E("s", "dma_start", out=A("L2"), in_=ext("due"))
+    E("y", "dma_start", out=A("h0"), in_=ext("h"))
+    E("s", "dma_start", out=A("wI"), in_=ext("w"))
+    E("y", "dma_start", out=A("kI"), in_=ext("kap"))
+    E("y", "dma_start", out=A("tI"), in_=ext("th"))
+    E("g", "iota", out=A("pI"), pattern=[[0, 1]], base=0, channel_multiplier=1)
+    E("g", "iota", out=A("mI"), pattern=[[1, 128]], base=0, channel_multiplier=0)
+    E("g", "iota", out=A("dI"), pattern=[[-1, 128]], base=0, channel_multiplier=1)
+
+    toks = []
+    own = A("W", c(rank * C, rank * C + C))
+    need("g", own, False, toks)
+    settle("g", toks)
+    sub = lambda a, b: T.W[:, rank * C + a:rank * C + b]
+    e8 = topo.engines(core, T.cores[near[0]])
+    loc = [e for e in topo.engines(core, car[0]) if e not in e8]
+    parts = [(k, j, loc[2 * j:2 * j + 2]) for j, k in enumerate(car)] + [(k, j + 1, e8[2 * j:2 * j + 2]) for j, k in enumerate(plain)]
+    g.remote_dma_fused([RemoteDMATransfer(dst_ids=[dst(topo, k, core)], dma_engine_mask=bits(es), remote_sem=T.sem.hin,
+                                          srcs=[sub(256 * j, 256 * j + 256)], dsts=[T.hb[:]]) for k, j, es in parts],
+                       local_sem=T.sem.lsA)
+    g.remote_dma_fused([RemoteDMATransfer(dst_ids=[dst(topo, T.cores[q], core) for q in near], dma_engine_mask=bits(e8),
+                                          remote_sem=T.sem.ag, srcs=[sub(0, 256)], dsts=[sub(0, 256) for q in near])],
+                       local_sem=T.sem.lsA)
+    nown = 2 * len(parts) + len(e8)
+    note("rem", own, False, ("lsA", nown, {}))
+    nag = len(e8) * 4 * (NR - 1)
+    for q in range(NR):
+        if q != rank:
+            note("rem", A("W", c(q * C, q * C + C)), True, ("ag", nag, {}))
+    small = {"channel_multiplier": 0, "allow_small_or_imprecise_dtypes": True}
+    E("g", "iota", out=A("RS"), pattern=[[0, 8], [32767, 16]], base=0, **small)
+    settle("y", [("qg", cnt["qg"], {})])
+    E("y", "dma_start", out=A("vv"), in_=ext("val"))
+    E("g", "iota", out=A("on1"), pattern=[[0, 1024]], base=1, **small)
+    E("g", "affine_select", out=A("Sel0"), in_=A("on1"), pattern=[[-16, 8], [0, 128]], compare_op=O.is_equal, fill=0.0, base=0,
+      channel_multiplier=1)
+    E("g", "iota", out=A("TK"), pattern=[[0, 8], [-1, 16]], base=15, **small)
+    E("g", "iota", out=A("r1"), pattern=[[0, 128], [256, 16]], base=-128, **small)
+    E("g", "iota", out=A("r2"), pattern=[[0, 128], [-256, 16]], base=128, **small)
+
+    cI = lambda k: A("ci1", c(k, k + 1))
+    ts(A("I32"), A("dI"), 0, O.is_equal)
+    ts(A("Ib"), A("dI"), 0, O.is_equal)
+    cp(A("hl"), A("mI"))
+    ts(cI(0), A("pI"), 4, O.arith_shift_right)
+    ts(cI(1), A("pI"), 15, O.bitwise_and)
+    ts(cI(2), A("pI"), 1, O.bitwise_and)
+    ts(A("md"), A("mI"), 4, O.arith_shift_right)
+    cp(K_("pdf"), cI(0))
+    cp(K_("pmf"), cI(1))
+    cp(K_("odd"), cI(2))
+    cp(K_("pf"), A("pI"))
+    ts(A("B"), A("md"), K_("pdf"), O.is_equal)
+    ts(A("oh16"), A("mI", c(0, 16)), K_("pmf"), O.is_equal)
+    ts(K_("key"), A("oh16", c(0, 1)), 14.0, O.mult, 1008.0, O.add)
+    tt(K_("key"), K_("key"), K_("pmf"), O.subtract)
+    fill(A("t8k"), 8192.0)
+    cp(A("f1"), A("L1"))
+    ts(A("f2"), A("L2"), -32.0, O.mult, K_("key"), O.add)
+    tr(A("p5", c(0, 128)), A("f1"))
+    tr(A("p6", c(0, 128)), A("f2"))
+    act(A("I8k"), A("Ib"), scale=8192.0)
+    act(A("I16k"), A("Ib"), scale=16384.0)
+    act(A("nI"), A("Ib"), scale=-1.0)
+    act(A("hr"), ind(A("h0"), A("hl")))
+    act(A("nm"), A("p5", c(0, 128)))
+    act(A("pri"), A("p6", c(0, 128)))
+    cp(K_("wf"), A("wI"))
+    ts(A("Wb"), A("B"), K_("wf"), O.mult)
+    for s in range(3, 9):
+        act(blk("Sel", s), A("B"), scale=A("oh16", c(s, s + 1)))
+    for s in range(9, 16):
+        ts(blk("Sel", s), A("B"), A("oh16", c(s, s + 1)), O.mult)
+    ts(K_("k16"), A("kI"), 16.0, O.mult)
+    ts(K_("ev8"), K_("odd"), -8.0, O.mult, 8.0, O.add)
+    ts(A("oddI"), A("Ib"), K_("odd"), O.mult)
+    ts(A("ib"), A("mI"), -128.0, O.add)
+
+    def twin_sums(b):
+        for k in range(4 * b, 4 * b + 4):
+            mm(blk("pn", k), A("Ib"), A("tri"), k == 4 * b, False)
+            mm(blk("pn", k), blk("Sel0", k), A("nh"), False, False)
+            mm(blk("pn", k), blk("Sel0", k), A("nl"), False, k == 4 * b + 3)
+
+    def twin_flags(b):
+        for k in range(4 * b, 4 * b + 4):
+            act(blk("dab", k), blk("pn", k), F.Abs, bias=A("nn", c(k, k + 1)))
+        half = c(512 * b, 512 * b + 512)
+        act(A("eq", half), A("dab", half), F.Relu, scale=-1.0, bias=1.0)
+
+    def prepare(t, h):
+        L = slots(t)
+        mm(A("p6", c(384, 512)), A("Wb"), A(h), True, True)
+        act(A("fr"), A("pri"), F.Sign, scale=-1.0, bias=32.5)
+        group(A("p7", c(0, 128)), [(A("nm"), A("I32")), (A("Ib"), A("t8k")), (A("fr"), A("I8k"))])
+        act(A("qh"), A("p7", c(0, 128)))
+        if t == 0:
+            for s in range(3, 16):
+                act(blk("KZ", s), A("Ib"), scale=float(VB + 128 * (POS[s] + 1)))
+        cp(A("i1"), A("p6", c(384, 512)))
+        scan(A("M0"), A("RS"), A("pri"), O.min, O.max, 0.0)
+        ts(A("i2"), A("i1"), 4095, O.bitwise_and)
+        tt(A("eq0"), spread("M0"), A("pri"), O.is_equal)
+        ts(A("i3"), A("i2"), K_("k16"), O.add)
+        group(A("pk", c(128, 256)), [(A("I32"), A("nm")), (A("I16k"), A("eq0"))])
+        tt(A("ql"), A("p7", c(0, 128)), A("qh"), O.subtract)
+        group(A("p6", c(0, 128)), [(A("oddI"), A("qh")), (A("oddI"), A("ql"))])
+        tt(A("i4"), A("i2"), A("i3"), O.mult)
+        scan(A("N0"), A("RS"), A("pk", c(128, 256)), O.min, O.max, 0.0)
+        act(A("n0c"), spread("N0"), bias=-16384.0)
+        tr(A("p7", c(256, 384)), A("n0c"))
+        act(A("nh"), A("p7", c(256, 384)))
+        for j, s in enumerate(L):
+            group(blk("pn", j), [(blk("Sel", s), A("qh")), (blk("Sel", s), A("ql"))])
+        ts(A("i5"), A("i4"), 4, O.arith_shift_right)
+        act(A("An"), spread("N0"), bias=K_("nbc"))
+        act(A("nn"), A("N0", c(15, 128, 16)), scale=-1.0, bias=16384.0)
+        act(A("e1k"), A("eq0"), scale=1024.0)
+        act(A("x1"), spread("M0"), F.Relu, scale=-2048.0, bias=2048.0 * 33)
+        act(A("x2"), spread("M0"), F.Relu, scale=2048.0, bias=-2048.0 * (1024 - 32 * (t + 1)))
+        if t:
+            act(A("hr"), ind(A(h), A("hl")))
+        else:
+            for s in range(16):
+                act(vslot(s), A("vv", c(s, None, 16)))
+        ts(A("sI"), spread("M0"), -1.0, O.mult, 1024.0, O.add)
+        if t:
+            ts(A("i6"), A("i5"), K_("odd"), O.mult, A("Ac", c(1, 2)), O.add)
+            ts(A("i1"), A("i5"), A("Ac", c(0, 1)), O.add)
+            z = "i1"
+        else:
+            ts(A("i6"), A("i5"), K_("odd"), O.mult, K_("ev8"), O.add)
+            z = "i5"
+        ts(A("sI"), A("sI"), 15, O.bitwise_and)
+        ts(A("i3"), A("i6"), 3, O.arith_shift_right, 1, O.bitwise_and)
+        tt(A("sd"), A("sI"), A("dl"), O.mult)
+        group(A("pk", c(480, 488)), [(A("sd"), A("dc128")), (A("Ib"), A("Cl"))])
+        tt(A("i4"), A(z), A("i3"), O.mult)
+        tt(A("i6"), A("i4"), A("p6", c(0, 128)), O.add)
+        ts(A("aI"), A("i6"), 8191, O.bitwise_and)
+        for j in range(len(L)):
+            tt(blk("hit", j), A("aI"), blk("pn", j), O.is_equal)
+        tt(A("nl"), A("p7", c(256, 384)), A("nh"), O.subtract)
+        group(A("p5", c(0, 128)), [(A("Ib"), A("ib"))] + [(blk("KZ", s), blk("hit", j)) for j, s in enumerate(L)])
+        tt(A("off"), A("aI"), A("p5", c(0, 128)), O.max)
+        cp(A("lst"), A("off"))
+        tr(A("p6", c(128, 256)), A("off"))
+        twin_sums(0)
+        if t:
+            twin_sums(1)
+            twin_flags(0)
+            twin_flags(1)
+
+    def reads(t, h):
+        win = A("W", c(0, VD))
+        A2 = TA // 4 * 2
+        act(A("d", c(16 * TA, 2048)), ind(win, A("lst", c(TA, TH))))
+        for a, b in ((0, A2), (A2, TA)):
+            part = c(16 * a, 16 * b)
+            E("v", "tensor_tensor", out=A("d", part), in0=ind(win, A("lst", c(a, b))), in1=A("hr", part), op=O.subtract)
+        cp(A("vl"), A("pk", c(480, 488)))
+        for a in range(TA, TH, 32):
+            b = min(a + 32, TH)
+            out = A("pn", c(1024 + 16 * (a - TA), 1024 + 16 * (b - TA)))
+            mm(out, A("nI"), A("hr", c(16 * a, 16 * b)), True, False)
+            mm(out, A("Ib"), A("d", c(16 * a, 16 * b)), False, True)
+        if t == 0:
+            twin_sums(1)
+        for a, b in ((0, A2), (A2, TA)):
+            act(A("ad", c(16 * a, 16 * b)), A("d", c(16 * a, 16 * b)), F.Abs)
+        act(A("ad", c(16 * TA, 2048)), A("pn", c(1024, 1024 + 16 * NB)), F.Abs)
+        key = A("pk", c(0, 128))
+        mm(key, A("Ib"), A("TK"), True, False)
+        for k in range(16):
+            mm(A("pk", c(k, 128, 16)), A("ad", c(k, None, 16)), A("B16"), False, k == 15)
+        if t == 0:
+            twin_flags(0)
+            twin_flags(1)
+        scan(A("sh"), A("r1"), A("d"), O.min, O.max, -128.0)
+        scan(A("sl"), A("r2"), A("d"), O.max, O.min, 128.0)
+        hi, lo = A("sh", c(15, None, 16)), A("sl", c(15, None, 16))
+        scan(A("ME"), A("RS"), key, O.min, O.max, 0.0)
+        group(A("p5", c(128, 256)), [(A("nI"), A("x1")), (A("Ib"), A("x2")), (hi, A("B")), (lo, A("nB"))])
+        group(A("p5", c(0, 128)), [(hi, A("B")), (lo, A("nB"))])
+        mm(A("pn", c(1536, 1664)), A("Ib"), A("mh"), True, False)
+        mm(A("pn", c(1536, 1536 + TA)), A("I2"), A(h, c(0, TA)), False, False)
+        mm(A("pn", c(1536, 1664)), A("Ib"), hi, False, False)
+        mm(A("pn", c(1536, 1664)), A("Ib"), lo, False, True)
+        tt(A("oh"), key, A("ME"), O.is_equal)
+        if t:
+            act(A("no"), A("oh"), scale=-1.0, bias=1.0)
+        else:
+            tt(A("no"), key, A("ME"), O.not_equal)
+        act(A("y1"), A("pn", c(1536, 1664)), scale=0.5, bias=MAGIC)
+        act(A("yb"), A("y1"), bias=-MAGIC)
+        tt(A("go"), A("p5", c(128, 256)), A("thE"), O.is_ge)
+        mm(A("p7", c(0, 128)), A("Ib"), A("ofd"), True, False)
+        for k in range(8):
+            mm(A("p7", c(16 * k, 16 * k + 16)), blk("eq", k), A("go", c(16 * k, 16 * k + 16)), False, k == 7)
+        tt(A("PS"), A("oh"), A("p6", c(128, 256)), O.mult)
+        tt(A("Fd"), A("p5", c(0, 128)), A("th2"), O.is_ge)
+        scan(A("SE"), A("no"), A("PS"), O.mult, O.add, 0.0)
+        tt(A("l2"), A("go"), A("p7", c(0, 128)), O.is_gt)
+        ts(A("tg"), spread("SE"), -float(VB), O.add, A("cT", c(t, t + 1)), O.max)
+        tt(A("l2"), A("l2"), A("An"), O.mult)
+        tt(A("l1"), A("tg"), A("dl"), O.mult)
+        group(A("pn", c(1024, 1032)), [(A("I32"), A("Cd")), (A("l2"), A("dc"))])
+        act(A("rv", t, rank, c(128, 136)), A("pn", c(1024, 1032)))
+        group(A("pn", c(512, 520)), [(A("Fd"), A("rh2")), (A("l1"), A("dc"))])
+        cp(A("sl16"), A("pn", c(512, 520)))
+        E("v", "tensor_copy", out=ind(A("W", c(VB, WEND)), A("sl16")), in_=A("yb"))
+        tt(A("rv", t, rank, c(136, 144)), A("pn", c(1024, 1032)), A("rv", t, rank, c(128, 136)), O.subtract)
+        E("v", "tensor_copy", out=A("rv", t, rank, c(0, 128)), in_=ind(A("W", c(VB, VD)), A("vl")))
+        toks = []
+        need("g", A("rv", t, rank), False, toks)
+        settle("g", toks)
+        piece = T.rv[:, t, rank, :]
+        g.remote_dma_fused([RemoteDMATransfer(dst_ids=[dst(topo, k, core)], dma_engine_mask=bits(es), remote_sem=T.sem["rl%d" % t],
+                                              srcs=[piece], dsts=[piece]) for (k, _), es in zip(relay, (loc[:4], e8[:4], loc[4:], e8[4:]))],
+                           local_sem=T.sem.lsD)
+        g.remote_dma_fused([RemoteDMATransfer(dst_ids=[dst(topo, T.cores[q], core) for q in near], dma_engine_mask=bits(e8),
+                                              remote_sem=T.sem["dr%d" % t], srcs=[piece], dsts=[piece for q in near])],
+                           local_sem=T.sem.lsD)
+        for q in range(NR):
+            if q != rank:
+                note("rem", A("rv", t, q), True, ("dr%d" % t, len(e8) * (NR - 1), {}))
+
+    def update(t, h, hn):
+        group(A("pn", c(0, 128)), [(A("Ib"), A("yb")), (A("nI"), A(h))])
+        act(A(hn), A("pn", c(0, 128)), F.Abs)
+        group(A("pn", c(1536, 1544)), [(A("yb"), A("B8th")), (A("Ib"), A("c716"))])
+        act(A("r8", c(0, 8)), A("pn", c(1536, 1544)), bias=MAGIC)
+        act(A("r8", c(8, 16)), A("r8", c(0, 8)), scale=256.0, bias=-256.0 * MAGIC)
+        group(A("pn", c(1024, 1032)), [(A("yb"), A("Bm32")), (A("Ib"), A("c960", c(8 * t, 8 * t + 8))), (A("I32"), A("r8", c(8, 16)))])
+        if t < STEPS - 1:
+            ac = lambda k: A("Ac", c(k, k + 1))
+            mm(A("pn", c(512, 640)), A("on32"), A("Fd"), True, True)
+            act(A("f1"), A("pn", c(512, 640)), scale=1.0 / 64, bias=-63.0 / 16384, accum_out=ac(2))
+            act(ac(3), ac(2), bias=MAGIC)
+            act(ac(4), ac(2), scale=64.0, bias=31.5)
+            act(ac(5), ac(3), scale=-64.0, bias=64.0 * MAGIC)
+            act(ac(0), ac(5), bias=ac(4))
+            act(ac(1), ac(0), scale=K_("odd"), bias=K_("ev8"))
+        s = lambda k: A("sm", c(8 * k, 8 * k + 8))
+        col = lambda n, k: A(n, c(k, 128, 16))
+        tt(A("f2"), A("go"), A("e1k"), O.mult)
+        ts(s(0), col("SE", 15), float(VB), O.is_lt)
+        tt(s(1), col("p5", 15), col("thE", 15), O.is_lt)
+        tt(s(3), col("SE", 15), col("nm", t), O.subtract)
+        tt(s(2), s(0), s(1), O.mult)
+        tt(A("pri"), A("pri"), A("f2"), O.subtract)
+        tt(s(3), s(3), s(2), O.mult)
+        tt(s(4), A("pn", c(1024, 1032)), s(2), O.mult)
+        tt(col("nm", t), col("nm", t), s(3), O.add)
+        tt(col("pri", t), col("pri", t), s(4), O.add)
+
+    def drains(t):
+        tt(A("dcd"), A("rv", t, c(None), c(128, 136)), A("rv", t, c(None), c(136, 144)), O.add)
+        cp(A("dL"), A("dcd"))
+        for q in range(NR - 1, -1, -1):
+            E("v", "tensor_copy", out=ind(A("W", c(0, VB)), A("dL", c(8 * q, 8 * q + 8))), in_=A("rv", t, q, c(0, 128)))
+
+    fill(A("on32"), 1.0)
+    cp(K_("tf"), A("tI"))
+    ts(A("thd"), A("I32"), K_("tf"), O.mult)
+    mm(A("p5", c(256, 384)), A("on32"), A("thd"), True, True)
+    ts(A("xl"), A("mI", c(0, 8)), 16.0, O.mult, 15.0, O.add)
+    ts(A("mm"), A("mI"), 15, O.bitwise_and)
+    ts(A("dl"), A("mm"), K_("pmf"), O.is_equal)
+    ts(A("dc"), A("mI", c(0, 8)), K_("pdf"), O.is_equal)
+    ts(A("dc128"), A("dc"), 128.0, O.mult)
+    ts(A("Cl"), A("mI", c(0, 8)), 16.0, O.mult, K_("pmf"), O.add)
+    ts(K_("nbc"), K_("pf"), -1.0, O.mult, -16384.0 - DUMP, O.add)
+    ts(A("tri"), A("dI"), 0, O.is_ge, 16384.0, O.mult)
+    for k in range(3):
+        ts(A("cT", c(k, k + 1)), K_("pf"), 128.0 * POS[k], O.add)
+    ts(A("ofd"), A("mm"), K_("pmf"), O.not_equal, 4.0, O.mult)
+    ts(A("B8th"), A("dc"), 0.125, O.mult)
+    ts(A("Bm32"), A("dc"), -32.0, O.mult)
+    fill(A("c716"), -0.4375)
+    for k in range(STEPS):
+        fill(A("c960", c(8 * k, 8 * k + 8)), 960.0 - 32 * k)
+    ts(A("B16"), A("dc"), 16.0, O.mult)
+    ts(A("Cd"), A("Cl"), float(DUMP), O.add)
+    ts(A("rh2"), A("dc"), 2048.0, O.mult)
+    fill(A("W", c(DUMP, VB)), 0.0)
+    fill(A("mh"), -0.5)
+    ts(A("th2"), A("ofd"), 1024.0, O.mult)
+    act(A("thE"), A("p5", c(256, 384)))
+    act(A("nB"), A("B"), scale=-1.0)
+    act(A("I2"), A("Ib"), scale=2.0)
+    prepare(0, H[0])
+    tt(A("th2"), A("thE"), A("th2"), O.add)
+    for t in range(STEPS):
+        h, hn = H[t % 2], H[1 - t % 2]
+        reads(t, h)
+        if t == 0:
+            for s in (0, 1):
+                ts(blk("Sel", s), A("B"), A("oh16", c(s, s + 1)), O.mult)
+                act(blk("KZ", s), A("Ib"), scale=float(VB + 128 * (POS[s] + 1)))
+        update(t, h, hn)
+        if t < STEPS - 1:
+            prepare(t + 1, hn)
+        else:
+            E("y", "dma_start", out=ext("yh"), in_=A(hn))
+            for s in range(16):
+                act(A("vv", c(s, None, 16)), vslot(s))
+            tr(A("pn", c(0, 128)), A("nm"))
+            ts(A("sI"), A("pri"), -0.03125, O.mult, 32.0 - 31.0 / 64, O.add)
+            ts(A("off"), A("sI"), 31.0, O.min)
+            tr(A("pn", c(512, 640)), A("off"))
+            cp(A("f1"), A("pn", c(0, 128)))
+            cp(A("l1"), A("pn", c(512, 640)))
+            E("y", "dma_start", out=ext("ypnd"), in_=A("f1"))
+            E("y", "dma_start", out=ext("ydue"), in_=A("l1"))
+            E("y", "dma_start", out=ext("yval"), in_=A("vv"))
+        drains(t)
+    E("y", "dma_start", out=ext("ymem"), in_=A("W", c(rank * C, rank * C + C)))
+    g.wait_ge(T.sem.lsD, STEPS * (2 * len(e8) + len(loc)))
+    for k in range(ndma[0]):
+        if not any(seen[q].get("dm%d" % k, 0) for q in Q):
+            g.sync.wait_ge(T.sem["dm%d" % k], 16)
+    for q in "gvst":
+        if cnt.get("q" + q, 0) > max(seen[o].get("q" + q, 0) for o in Q):
+            g.sync.wait_ge(T.sem["q" + q], cnt["q" + q])

@@ -5,66 +5,62 @@ NR, C, TH, STEPS = 8, 1024, 128, 3
 DUMP = NR * C
 VB = DUMP + TH
 VD = VB + 16 * TH
-WEND = VD + 16 * TH
-PW = 144
+WEND = VD + TH
+PW = 136
+OFF = 160.0
 MAGIC = 12582912.0
 POS = [2, 1, 0] + list(range(3, 16))
-NB = 48
-TA = TH - NB
+NB, CUTS = 56, [0, 32, 56, 96, 128]
+HOP, FAR, NEAR = 0.12, 5.5, 4.0
+LAND, PACE = (8.0, 11.5, 12.0), 1.5
+ROUNDS, ROOM, DOUBT = 1, 0.16, 2.0
+NSC = 1024
 
 S, P = "sbuf", "psum"
+f32, bf, i32, u16, f16 = "float32", "bfloat16", "int32", "uint16", "float16"
 SCRATCH = {
-    "W": (S, [128, WEND], "bfloat16"), "vv": (S, [128, 16 * TH], "bfloat16"),
-    "hb": (S, [128, 256], "bfloat16"),
-    "pI": (S, [128, 1], "int32"), "mI": (S, [128, 128], "int32"), "dI": (S, [128, 128], "int32"),
-    "ci1": (S, [128, 4], "int32"), "cols": (S, [128, 16], "float32"), "cT": (S, [128, 3], "float32"),
-    "md": (S, [128, 128], "int32"), "mm": (S, [128, 128], "int32"),
-    "I32": (S, [128, 128], "float32"), "Ib": (S, [128, 128], "bfloat16"), "nI": (S, [128, 128], "bfloat16"),
-    "I2": (S, [128, 128], "bfloat16"), "oddI": (S, [128, 128], "bfloat16"), "I8k": (S, [128, 128], "bfloat16"),
-    "I16k": (S, [128, 128], "bfloat16"),
-    "B": (S, [128, 128], "bfloat16"), "nB": (S, [128, 128], "bfloat16"), "dl": (S, [128, 128], "bfloat16"),
-    "ofd": (S, [128, 128], "bfloat16"), "dc": (S, [128, 8], "float32"), "B8th": (S, [128, 8], "bfloat16"),
-    "Bm32": (S, [128, 8], "bfloat16"), "c716": (S, [128, 8], "bfloat16"), "c960": (S, [128, 24], "bfloat16"),
-    "B16": (S, [128, 8], "bfloat16"), "dc128": (S, [128, 8], "bfloat16"), "Cl": (S, [128, 8], "bfloat16"),
-    "Cd": (S, [128, 8], "float32"), "rh2": (S, [128, 8], "float32"), "oh16": (S, [128, 16], "float32"),
-    "Sel": (S, [128, 2048], "bfloat16"), "KZ": (S, [128, 2048], "bfloat16"),
-    "TK": (S, [128, 128], "bfloat16"), "RS": (S, [128, 128], "float32"),
-    "xl": (S, [128, 8], "uint16"), "hl": (S, [128, 128], "uint16"),
-    "r1": (S, [128, 2048], "bfloat16"), "r2": (S, [128, 2048], "bfloat16"),
-    "tri": (S, [128, 128], "bfloat16"), "on1": (S, [128, 1024], "bfloat16"), "Sel0": (S, [128, 1024], "bfloat16"),
-    "nn": (S, [128, 8], "float32"), "on32": (S, [128, 128], "float32"), "t8k": (S, [128, 128], "bfloat16"),
-    "mh": (S, [128, 128], "bfloat16"), "ib": (S, [128, 128], "bfloat16"),
-    "wI": (S, [128, 1], "int32"), "kI": (S, [128, 1], "int32"), "tI": (S, [128, 1], "int32"),
-    "Wb": (S, [128, 128], "bfloat16"), "thd": (S, [128, 128], "float32"), "thE": (S, [128, 128], "float32"),
-    "th2": (S, [128, 128], "float32"),
-    "L1": (S, [128, 128], "int32"), "L2": (S, [128, 128], "int32"), "f1": (S, [128, 128], "float32"),
-    "f2": (S, [128, 128], "float32"),
-    "h0": (S, [128, 128], "bfloat16"), "h1": (S, [128, 128], "bfloat16"),
-    "nm": (S, [128, 128], "float32"), "pri": (S, [128, 128], "float32"),
-    "fr": (S, [128, 128], "bfloat16"), "qh": (S, [128, 128], "bfloat16"), "ql": (S, [128, 128], "bfloat16"),
-    "i1": (S, [128, 128], "int32"), "i2": (S, [128, 128], "int32"), "i3": (S, [128, 128], "int32"),
-    "i4": (S, [128, 128], "int32"), "i5": (S, [128, 128], "int32"), "i6": (S, [128, 128], "int32"),
-    "aI": (S, [128, 128], "int32"), "hit": (S, [128, 2048], "bfloat16"), "off": (S, [128, 128], "float32"),
-    "lst": (S, [128, 128], "uint16"), "hr": (S, [128, 2048], "bfloat16"), "d": (S, [128, 2048], "bfloat16"),
-    "ad": (S, [128, 2048], "bfloat16"), "sh": (S, [128, 2048], "bfloat16"), "sl": (S, [128, 2048], "bfloat16"),
-    "M0": (S, [128, 128], "float32"), "eq0": (S, [128, 128], "bfloat16"), "e1k": (S, [128, 128], "bfloat16"),
-    "N0": (S, [128, 128], "float32"), "n0c": (S, [128, 128], "float32"),
-    "sI": (S, [128, 128], "int32"), "sd": (S, [128, 128], "bfloat16"), "vl": (S, [128, 8], "uint16"),
-    "x1": (S, [128, 128], "bfloat16"), "x2": (S, [128, 128], "bfloat16"), "An": (S, [128, 128], "float32"),
-    "nh": (S, [128, 128], "bfloat16"), "nl": (S, [128, 128], "bfloat16"), "dab": (S, [128, 1024], "bfloat16"),
-    "eq": (S, [128, 1024], "bfloat16"), "y1": (S, [128, 128], "float32"), "yb": (S, [128, 128], "bfloat16"),
-    "ME": (S, [128, 128], "float32"), "oh": (S, [128, 128], "float32"), "no": (S, [128, 128], "float32"),
-    "PS": (S, [128, 128], "float32"), "SE": (S, [128, 128], "float32"), "go": (S, [128, 128], "bfloat16"),
-    "Fd": (S, [128, 128], "float32"), "r8": (S, [128, 16], "float32"),
-    "tg": (S, [128, 128], "float32"), "l1": (S, [128, 128], "float32"), "l2": (S, [128, 128], "float32"),
-    "sl16": (S, [128, 8], "uint16"), "sm": (S, [128, 64], "float32"),
-    "Ac": (S, [128, 8], "float32"), "rv": (S, [128, STEPS, NR, PW], "bfloat16"), "dcd": (S, [128, 64], "float32"),
-    "dL": (S, [128, 64], "uint16"),
-    "pn": (P, [128, 2048], "float32"), "pk": (P, [128, 512], "float32"), "p5": (P, [128, 512], "float32"),
-    "p6": (P, [128, 512], "float32"), "p7": (P, [128, 512], "float32"),
+    "W": (S, [128, WEND], bf), "vv": (S, [128, 16 * TH], bf), "ms": (S, [128, C], bf),
+    "xo": (S, [128, 512], f16), "xi": (S, [128, NR, 512], f16), "hb": (S, [128, 256], f16),
+    "pI": (S, [128, 1], i32), "mI": (S, [128, 128], i32), "dI": (S, [128, 128], i32),
+    "ci1": (S, [128, 4], i32), "cols": (S, [128, 20], f32), "aq": (S, [128, 1], bf), "md": (S, [128, 128], i32), "mm": (S, [128, 128], i32),
+    "I32": (S, [128, 128], f32), "Ib": (S, [128, 128], bf), "nI": (S, [128, 128], bf), "Ih": (S, [128, 128], f16),
+    "I64": (S, [128, 128], bf), "nI64": (S, [128, 128], bf), "oddI": (S, [128, 128], bf), "I8k": (S, [128, 128], bf),
+    "nI8k": (S, [128, 128], bf), "I16k": (S, [128, 128], bf),
+    "B3": (S, [128, 264], bf), "nB3": (S, [128, 264], bf), "dl": (S, [128, 128], bf), "cq": (S, [128, 128], bf),
+    "dc": (S, [128, 8], f32), "ndc": (S, [128, 8], f32), "B8th": (S, [128, 8], bf), "Bm32": (S, [128, 8], bf),
+    "TP": (S, [128, 128], bf), "uq": (S, [128, 128], bf), "c32k": (S, [128, 8], bf), "B16": (S, [128, 16], bf),
+    "dc128": (S, [128, 8], bf), "Cl": (S, [128, 8], bf), "Cd": (S, [128, 8], f32), "Ck": (S, [128, 8], f32),
+    "rh2": (S, [128, 16], bf), "cT": (S, [128, 24], f32), "oh16": (S, [128, 16], f32), "m1": (S, [128, 16], bf),
+    "KZ": (S, [128, 2048], bf), "on": (S, [128, 1024], bf), "Sel": (S, [128, 16, 128], bf), "Sel0": (S, [128, 1024], bf),
+    "TK": (S, [128, 256], bf), "RS": (S, [128, 256], f32), "xl": (S, [128, 8], u16), "x8": (S, [128, 8], u16),
+    "r1": (S, [128, NSC], bf), "r2": (S, [128, NSC], bf), "thh": (S, [128, 264], bf), "thl": (S, [128, 264], bf),
+    "nn": (S, [128, 8], f32), "on32": (S, [128, 128], f32), "ib": (S, [128, 128], bf),
+    "wI": (S, [128, 1], i32), "kI": (S, [128, 1], i32), "tI": (S, [128, 1], i32),
+    "Wb": (S, [128, 128], bf), "thd": (S, [128, 128], f32), "thc": (S, [128, 264], f32),
+    "L1": (S, [128, 128], i32), "L2": (S, [128, 128], i32), "f1": (S, [128, 128], f32),
+    "h0": (S, [128, 128], bf), "h1": (S, [128, 128], bf), "hT": (S, [128, 128], bf),
+    "nm": (S, [128, 128], f32), "pri": (S, [128, 128], f32),
+    "fr": (S, [128, 128], bf), "qh": (S, [128, 128], bf), "ql": (S, [128, 128], bf),
+    "i1": (S, [128, 128], i32), "i2": (S, [128, 128], i32), "i3": (S, [128, 128], i32),
+    "i4": (S, [128, 128], i32), "v2": (S, [128, 128], f32),
+    "aI": (S, [128, 128], i32), "hit": (S, [128, 2048], bf), "off": (S, [128, 128], f32), "ML": (S, [128, 128], bf),
+    "lst": (S, [128, 128], u16), "x": (S, [128, 2048], bf),
+    "ad": (S, [128, 2048], bf), "sh": (S, [128, 2048], bf), "sl": (S, [128, 2048], bf),
+    "M0": (S, [128, 128], f32), "eq0": (S, [128, 128], bf), "N0": (S, [128, 256], f32), "n0c": (S, [128, 128], f32),
+    "sI": (S, [128, 128], i32), "sd": (S, [128, 128], bf), "vl": (S, [128, 8], u16), "vl2": (S, [128, 8], u16),
+    "x1": (S, [128, 128], bf), "x2": (S, [128, 128], bf), "An": (S, [128, 128], f32),
+    "nh": (S, [128, 128], bf), "nl": (S, [128, 128], bf), "dab": (S, [128, 1024], bf), "eq": (S, [128, 1024], bf),
+    "OV": (S, [128, 256], bf), "ME": (S, [128, 256], f32), "e8": (S, [128, 8], f32), "ov": (S, [128, 128], bf),
+    "ng": (S, [128, 128], bf), "Rb": (S, [128, 128], f32), "sg": (S, [128, 16], bf), "ks": (S, [128, 128], f32),
+    "oh": (S, [128, 128], bf), "SE": (S, [128, 128], f32), "NF": (S, [128, 128], bf), "r8": (S, [128, 8], bf),
+    "l1": (S, [128, 128], f32), "l2": (S, [128, 128], f32), "sl16": (S, [128, 8], u16), "sm": (S, [128, 16], f32),
+    "Ac": (S, [128, 8], f32), "rv": (S, [128, STEPS, NR, PW], u16),
+    "pn": (P, [128, 2048], f32), "pk": (P, [128, 512], f32), "p5": (P, [128, 512], f32),
+    "p6": (P, [128, 512], f32), "p7": (P, [128, 512], f32),
 }
-SEMAPHORES = ["qg", "qv", "qs", "qt", "ag", "lsA", "lsD", "hin", "hout"] + ["dr%d" % t for t in range(STEPS)] \
-    + ["rl%d" % t for t in range(STEPS)] + ["dm%d" % k for k in range(16)]
+SEMAPHORES = ["qg", "qv", "qs", "qt", "lsA", "lsD", "hin", "hout"] \
+    + ["ag%d_%d" % (q, j) for q in range(NR) for j in range(2)] + ["dr%d_%d" % (t, q) for t in range(STEPS) for q in range(NR)] \
+    + ["rl%d" % t for t in range(STEPS)] + ["dm%d" % k for k in range(20)]
 
 
 def dst(topo, d, src):
@@ -83,43 +79,36 @@ def roles(T, topo, r):
     me = T.cores[r]
     near = [q for q in range(NR) if q != r and topo.may_write(me, T.cores[q])]
     far = [q for q in range(NR) if q != r and q not in near]
-    chip = [c for c in topo.cores_of(me) if c != me]
-    car = [c for c in chip if topo.may_write(c, T.cores[far[0]])]
+    car = [c for c in topo.cores_of(me) if c != me and topo.may_write(c, T.cores[far[0]])]
     car = sorted(car, key=lambda c: (topo.die(c) != topo.die(me), c))
-    plain = [c for c in chip if c not in car]
     a = sum(q < r for q in near)
     relay = [(car[(a + b) % 2 * 2 + b // 2], q) for b, q in enumerate(far)]
-    return near, far, car, plain, relay
+    near, far = near[a:] + near[:a], far[a:] + far[:a]
+    spread = [(me, 0, near), (me, 1, near[:2])] + [(k, j // 2, far[j % 2::2] + near[2:] * (j == 3)) for j, k in enumerate(car)]
+    return near, car, spread, relay
 
 
 def helper_program(g, core, T, topo):
     for r in range(NR):
         me = T.cores[r]
-        if core not in topo.cores_of(me):
+        if core == me or core not in topo.cores_of(me):
             continue
-        near, far, car, plain, relay = roles(T, topo, r)
-        n = 0
-        if core in car or core in plain:
-            serve = far if core in car else near
-            lo = r * C + 256 * (car.index(core) if core in car else 1 + plain.index(core))
-            es = topo.engines(core, T.cores[serve[0]])
-            g.wait_ge(T.sem.hin, 2)
-            g.remote_dma_fused([RemoteDMATransfer(dst_ids=[dst(topo, T.cores[q], core) for q in serve], dma_engine_mask=bits(es),
-                                                  remote_sem=T.sem.ag, srcs=[T.hb[:]],
-                                                  dsts=[T.W[:, lo:lo + 256] for q in serve])], local_sem=T.sem.hout)
-            n += len(es)
-        for c, q in relay:
-            if c != core:
-                continue
-            es = topo.engines(core, T.cores[q])
-            for t in range(STEPS):
-                g.wait_ge(T.sem["rl%d" % t], 4)
-                g.remote_dma_fused([RemoteDMATransfer(dst_ids=[dst(topo, T.cores[q], core)], dma_engine_mask=bits(es),
-                                                      remote_sem=T.sem["dr%d" % t], srcs=[T.rv[:, t, r, :]],
-                                                      dsts=[T.rv[:, t, r, :]])], local_sem=T.sem.hout)
-                n += len(es)
-        if n:
-            g.wait_ge(T.sem.hout, n)
+        near, car, spread, relay = roles(T, topo, r)
+        if core not in car:
+            continue
+        half, serve = [(j, to) for k, j, to in spread if k == core][0]
+        es = topo.engines(core, T.cores[serve[0]])
+        g.wait_ge(T.sem.hin, len(es))
+        g.remote_dma_fused([RemoteDMATransfer(dst_ids=[dst(topo, T.cores[q], core) for q in serve], dma_engine_mask=bits(es),
+                                              remote_sem=T.sem["ag%d_%d" % (r, half)], srcs=[T.hb[:]],
+                                              dsts=[T.xi[:, r, 256 * half:256 * half + 256] for q in serve])], local_sem=T.sem.hout)
+        q = dict(relay)[core]
+        for t in range(STEPS):
+            g.wait_ge(T.sem["rl%d" % t], len(es) // 2)
+            g.remote_dma_fused([RemoteDMATransfer(dst_ids=[dst(topo, T.cores[q], core)], dma_engine_mask=bits(es),
+                                                  remote_sem=T.sem["dr%d_%d" % (t, r)], srcs=[T.rv[:, t, r, :]],
+                                                  dsts=[T.rv[:, t, r, :]])], local_sem=T.sem.hout)
+        g.wait_ge(T.sem.hout, len(es) * (1 + STEPS))
 
 
 def rank_program(g, core, T, topo):
@@ -127,7 +116,7 @@ def rank_program(g, core, T, topo):
     if rank is None:
         helper_program(g, core, T, topo)
         return
-    near, far, car, plain, relay = roles(T, topo, rank)
+    near, car, spread_plan, relay = roles(T, topo, rank)
 
     Q = {"g": g, "v": g.vector, "s": g.scalar, "t": g.tensor, "y": g.sync}
     cnt, seen, log, ndma = {}, {q: {} for q in Q}, {}, [0]
@@ -137,42 +126,47 @@ def rank_program(g, core, T, topo):
         shape = [int(x) for x in ap.shape][1:]
         idx = idx + (slice(None),) * (len(shape) - len(idx))
         lo = hi = 0
+        step = size = 1
         for n, i in zip(shape, idx):
             if isinstance(i, slice):
                 a, b, st = i.indices(n)
                 last = a + (b - 1 - a) // st * st
+                step = st if len(shape) == 1 else 1
+                size *= (b - 1 - a) // st + 1
             else:
                 a = last = i
             lo, hi = lo * n + a, hi * n + last
-        return {"ap": ap[(slice(None),) + idx], "n": name, "r": (lo, hi + 1), "ind": None}
+        return {"ap": ap[(slice(None),) + idx], "n": name, "r": (lo, hi + 1, step), "e": size, "ind": None}
 
     def ind(win, offs):
-        return {"ap": win["ap"].indirect(offs["ap"]), "n": win["n"], "r": win["r"], "ind": offs}
+        return {"ap": win["ap"].indirect(offs["ap"]), "n": win["n"], "r": win["r"], "e": win["e"], "ind": offs}
 
     def spans(v):
-        lo, hi = v["r"]
+        lo, hi, st = v["r"]
         if v["n"] in SCRATCH and SCRATCH[v["n"]][0] == P:
-            return True, lo // 512 * 512, (hi + 511) // 512 * 512
-        return False, lo, hi
+            return True, lo // 512 * 512, (hi + 511) // 512 * 512, 1
+        return False, lo, hi, st
 
     def need(q, v, write, acc):
-        ps, lo, hi = spans(v)
+        ps, lo, hi, st = spans(v)
         for e in log.get(v["n"], []):
             if e["lo"] < hi and lo < e["hi"]:
                 same = e["q"] == q
                 if same and (ps and q == "t" or not e["w"]):
                     continue
+                if st > 1 and e["st"] == st and (lo - e["lo"]) % st and "dma" not in (q, e["q"]):
+                    continue
                 if e["w"] or write or ps and not same:
                     acc.append(e["tok"])
 
     def note(q, v, write, tok):
-        ps, lo, hi = spans(v)
+        ps, lo, hi, st = spans(v)
         L = log.setdefault(v["n"], [])
-        if write:
+        if write and st == 1:
             L[:] = [e for e in L if not (lo <= e["lo"] and e["hi"] <= hi and not ps)]
         if ps:
             L[:] = [e for e in L if not (e["q"] == q and e["w"] == write and e["lo"] == lo and e["hi"] == hi)]
-        L.append({"lo": lo, "hi": hi, "w": write, "q": q, "tok": tok})
+        L.append({"lo": lo, "hi": hi, "st": st, "w": write, "q": q, "tok": tok})
 
     def settle(q, toks):
         best = {}
@@ -195,18 +189,13 @@ def rank_program(g, core, T, topo):
              "v": {"tensor_copy": g.vector.tensor_copy, "tensor_tensor": g.vector.tensor_tensor, "memset": g.vector.memset,
                    "tensor_scalar": g.vector.tensor_scalar, "tensor_tensor_scan": g.vector.tensor_tensor_scan}}
 
-    def E(q, meth, _pos=(), **kw):
-        wr, rd = [], []
-        for k, v in list(kw.items()) + [("ap", p) for p in _pos]:
-            if isinstance(v, dict):
-                (wr if k in ("out", "ap", "accum_out") else rd).append(v)
-                if v["ind"]:
-                    rd.append(v["ind"])
+    def emit(q, meth, _pos, kw, rd, wr):
         toks = []
+        dq = q if meth != "dma_start" else "dma"
         for v in rd:
-            need(q, v, False, toks)
+            need(dq, v, False, toks)
         for v in wr:
-            need(q, v, True, toks)
+            need(dq, v, True, toks)
         settle(q, toks)
         un = lambda v: v["ap"] if isinstance(v, dict) else v
         ins = calls[q][meth](*[un(p) for p in _pos], **{k: un(v) for k, v in kw.items()})
@@ -219,11 +208,95 @@ def rank_program(g, core, T, topo):
             cnt[s] = n = cnt.get(s, 0) + 1
             ins.then_inc(T.sem[s], 1)
         tok = (s, n, dict(seen[q]))
-        dq = q if meth != "dma_start" else "dma"
         for v in rd:
             note(dq, v, False, tok)
         for v in wr:
             note(dq, v, True, tok)
+
+    ops, past, loads, early = [], {}, [0.0], []
+
+    def op(q, rd, wr, busy, done, run):
+        pre = {}
+        for v, write in [(v, False) for v in rd] + [(v, True) for v in wr]:
+            ps, lo, hi, st = spans(v)
+            for e in past.get(v["n"], []):
+                o = ops[e[4]]
+                if e[0] < hi and lo < e[1] and (e[3] or write or ps and o["q"] != q) and not (st > 1 and e[2] == st and (lo - e[0]) % st):
+                    free = o["q"] == q and (ps and q == "t" or not e[3] or v["n"] == "turn" + q)
+                    pre[e[4]] = max(pre.get(e[4], 0), o["busy"] if free else o["done"] + (ROOM if o["q"] == q else HOP))
+        for v, write in [(v, False) for v in rd] + [(v, True) for v in wr]:
+            ps, lo, hi, st = spans(v)
+            L = past.setdefault(v["n"], [])
+            if write and st == 1:
+                L[:] = [e for e in L if not (lo <= e[0] and e[1] <= hi)]
+            L.append((lo, hi, st, write, len(ops)))
+        ops.append({"q": q, "pre": pre, "busy": busy, "done": done, "run": run})
+
+    def issue():
+        N = range(len(ops))
+        busy = [o["busy"] for o in ops]
+        fore = [o["pre"] for o in ops]
+        back = [{} for o in ops]
+        for k in N:
+            for p, d in fore[k].items():
+                back[p][k] = d + busy[k] - busy[p] + (DOUBT if ops[p]["q"] == "n" or p in early else 0.0)
+
+        def place(order, pre, least):
+            at, used = {}, {}
+            for k in order:
+                t = max([least[k]] + [at[p] + d for p, d in pre[k].items()])
+                L = used.setdefault(ops[k]["q"], [])
+                if busy[k]:
+                    j = 0
+                    while j < len(L) and L[j][0] < t + busy[k] - 1e-9:
+                        t = max(t, L[j][1])
+                        j += 1
+                    L.insert(j, (t, t + busy[k]))
+                at[k] = t
+            return at
+
+        est = {}
+        for k in N:
+            est[k] = max([0.0] + [est[p] + d for p, d in fore[k].items()])
+        for _ in range(ROUNDS):
+            late = place(sorted(N, key=lambda k: (-est[k], -k)), back, [ops[k]["done"] - busy[k] for k in N])
+            est = place(sorted(N, key=lambda k: (-late[k] - busy[k], k)), fore, [0.0] * len(ops))
+        for k in sorted(N, key=lambda k: (est[k], k)):
+            ops[k]["run"]()
+
+    def mark(name):
+        return {"n": name, "r": (0, 1, 1), "ind": None}
+
+    def E(q, meth, _pos=(), **kw):
+        wr, rd = [], []
+        for k, v in list(kw.items()) + [("ap", p) for p in _pos]:
+            if isinstance(v, dict):
+                (wr if k in ("out", "ap", "accum_out") else rd).append(v)
+                if v["ind"]:
+                    rd.append(v["ind"])
+        run = lambda: emit(q, meth, _pos, kw, rd, wr)
+        out = wr[0]
+        wide = lambda v: SCRATCH[v["n"]][2] in (f32, i32)
+        if meth == "dma_start":
+            load = out["n"] in SCRATCH
+            loads[0] = loads[0] * load + 0.3 + (out if load else rd[0])["e"] / 1500
+            return op(q, rd + [mark("out%d" % (STEPS - 1))] * (not load), wr + [mark("turn" + q)], 0.06, 1.5 + loads[0], run)
+        n = out["e"]
+        if q == "t":
+            t = max(64, n) * (2.0 if wide(rd[0]) else 0.5)
+        elif q == "g":
+            t = 150 + 2 * n
+        elif out["ind"]:
+            t = 60 + 3.5 * 16 * out["ind"]["e"]
+        elif any(v["ind"] for v in rd):
+            t = 60 + 1.5 * n
+        elif q == "v" and meth == "tensor_tensor":
+            t = 30 + max(64, n * (2 if all(SCRATCH[v["n"]][0] == S for v in rd) else 1))
+        elif q == "v" and not any(wide(v) and v["e"] > 1 for v in rd + wr):
+            t = 30 + max(64, n / 2)
+        else:
+            t = 30 + max(64, n)
+        op(q, rd, wr, t / 1000, t / 1000, run)
 
     def cp(out, in_):
         E("v", "tensor_copy", out=out, in_=in_)
@@ -256,66 +329,59 @@ def rank_program(g, core, T, topo):
     def fill(v, x):
         E("v", "memset", (v, x))
 
-    def ext(name):
-        return {"ap": T[name][:], "n": name, "r": (0, 1), "ind": None}
+    def ext(name, *idx):
+        return {"ap": T[name][(slice(None),) + idx], "n": name + str(idx), "r": (0, 1, 1), "ind": None}
+
+    def send(v, name, run):
+        def go():
+            toks = []
+            need("g", v, False, toks)
+            settle("g", toks)
+            run()
+        op("g", [v], [mark(name)], 2.0, 0.0, go)
+
+    def lands(v, name, sem, n, time):
+        op("n", [mark(name)], [v], 0.0, time, lambda: note("rem", v, True, (sem, n, {})))
 
     c = slice
-    COLS = ["pdf", "pmf", "pf", "odd", "ev8", "nbc", "key", "wf", "k16", "tf"]
+    COLS = ["pdf", "pmf", "pf", "odd", "ev8", "nbc", "key", "wf", "k8", "k4", "kq", "kq2", "nod", "n64", "o16", "tf"]
     K_ = lambda n: A("cols", c(COLS.index(n), COLS.index(n) + 1))
     blk = lambda n, k: A(n, c(128 * k, 128 * k + 128))
-    spread = lambda n: ind(A(n), A("xl"))
+    spread = lambda n: ind(A(n, c(0, 128)), A("xl"))
     vslot = lambda s: A("W", c(VB + 128 * POS[s], VB + 128 * POS[s] + 128))
+    col = lambda n, k: A(n, c(k, 128, 16))
+    sel = lambda s: A("Sel", s)
+    RS = A("RS", c(0, 128))
+    B, ones = A("B3", c(0, 128)), A("on", c(0, 128))
+    own = A("W", c(rank * C, rank * C + C))
     H = ["h0", "h1"]
+    small = {"channel_multiplier": 0, "allow_small_or_imprecise_dtypes": True}
 
     def slots(t):
         return [s for s in range(16) if s >= STEPS or s < t]
 
-    E("y", "dma_start", out=A("W", c(rank * C, rank * C + C)), in_=ext("mem"))
-    E("s", "dma_start", out=A("L1"), in_=ext("pnd"))
+    E("y", "dma_start", out=A("ms", c(0, 512)), in_=ext("mem", c(0, 512)))
+    E("s", "dma_start", out=A("ms", c(512, C)), in_=ext("mem", c(512, C)))
+    E("y", "dma_start", out=A("L1"), in_=ext("pnd"))
     E("s", "dma_start", out=A("L2"), in_=ext("due"))
     E("y", "dma_start", out=A("h0"), in_=ext("h"))
     E("s", "dma_start", out=A("wI"), in_=ext("w"))
     E("y", "dma_start", out=A("kI"), in_=ext("kap"))
     E("y", "dma_start", out=A("tI"), in_=ext("th"))
+    E("y", "dma_start", out=A("vv"), in_=ext("val"))
+    E("g", "iota", out=A("dI"), pattern=[[-1, 128]], base=0, channel_multiplier=1)
     E("g", "iota", out=A("pI"), pattern=[[0, 1]], base=0, channel_multiplier=1)
     E("g", "iota", out=A("mI"), pattern=[[1, 128]], base=0, channel_multiplier=0)
-    E("g", "iota", out=A("dI"), pattern=[[-1, 128]], base=0, channel_multiplier=1)
-
-    toks = []
-    own = A("W", c(rank * C, rank * C + C))
-    need("g", own, False, toks)
-    settle("g", toks)
-    sub = lambda a, b: T.W[:, rank * C + a:rank * C + b]
-    e8 = topo.engines(core, T.cores[near[0]])
-    loc = [e for e in topo.engines(core, car[0]) if e not in e8]
-    parts = [(k, j, loc[2 * j:2 * j + 2]) for j, k in enumerate(car)] + [(k, j + 1, e8[2 * j:2 * j + 2]) for j, k in enumerate(plain)]
-    g.remote_dma_fused([RemoteDMATransfer(dst_ids=[dst(topo, k, core)], dma_engine_mask=bits(es), remote_sem=T.sem.hin,
-                                          srcs=[sub(256 * j, 256 * j + 256)], dsts=[T.hb[:]]) for k, j, es in parts],
-                       local_sem=T.sem.lsA)
-    g.remote_dma_fused([RemoteDMATransfer(dst_ids=[dst(topo, T.cores[q], core) for q in near], dma_engine_mask=bits(e8),
-                                          remote_sem=T.sem.ag, srcs=[sub(0, 256)], dsts=[sub(0, 256) for q in near])],
-                       local_sem=T.sem.lsA)
-    nown = 2 * len(parts) + len(e8)
-    note("rem", own, False, ("lsA", nown, {}))
-    nag = len(e8) * 4 * (NR - 1)
-    for q in range(NR):
-        if q != rank:
-            note("rem", A("W", c(q * C, q * C + C)), True, ("ag", nag, {}))
-    small = {"channel_multiplier": 0, "allow_small_or_imprecise_dtypes": True}
-    E("g", "iota", out=A("RS"), pattern=[[0, 8], [32767, 16]], base=0, **small)
-    settle("y", [("qg", cnt["qg"], {})])
-    E("y", "dma_start", out=A("vv"), in_=ext("val"))
-    E("g", "iota", out=A("on1"), pattern=[[0, 1024]], base=1, **small)
-    E("g", "affine_select", out=A("Sel0"), in_=A("on1"), pattern=[[-16, 8], [0, 128]], compare_op=O.is_equal, fill=0.0, base=0,
-      channel_multiplier=1)
-    E("g", "iota", out=A("TK"), pattern=[[0, 8], [-1, 16]], base=15, **small)
-    E("g", "iota", out=A("r1"), pattern=[[0, 128], [256, 16]], base=-128, **small)
-    E("g", "iota", out=A("r2"), pattern=[[0, 128], [-256, 16]], base=128, **small)
+    E("g", "iota", out=A("RS"), pattern=[[0, 16], [32767, 16]], base=0, **small)
+    E("g", "iota", out=A("TK"), pattern=[[0, 16], [-1, 16]], base=15, **small)
+    E("g", "iota", out=A("TP"), pattern=[[0, 8], [128, 16]], base=0, **small)
 
     cI = lambda k: A("ci1", c(k, k + 1))
-    ts(A("I32"), A("dI"), 0, O.is_equal)
+    fill(A("on", c(0, 128)), 1.0)
+    fill(A("on", c(128, 1024)), 1.0)
     ts(A("Ib"), A("dI"), 0, O.is_equal)
-    cp(A("hl"), A("mI"))
+    ts(A("I64"), A("dI"), 0, O.is_equal, 64.0, O.mult)
+    ts(A("I32"), A("dI"), 0, O.is_equal)
     ts(cI(0), A("pI"), 4, O.arith_shift_right)
     ts(cI(1), A("pI"), 15, O.bitwise_and)
     ts(cI(2), A("pI"), 1, O.bitwise_and)
@@ -324,261 +390,323 @@ def rank_program(g, core, T, topo):
     cp(K_("pmf"), cI(1))
     cp(K_("odd"), cI(2))
     cp(K_("pf"), A("pI"))
-    ts(A("B"), A("md"), K_("pdf"), O.is_equal)
+    ts(B, A("md"), K_("pdf"), O.is_equal)
     ts(A("oh16"), A("mI", c(0, 16)), K_("pmf"), O.is_equal)
-    ts(K_("key"), A("oh16", c(0, 1)), 14.0, O.mult, 1008.0, O.add)
-    tt(K_("key"), K_("key"), K_("pmf"), O.subtract)
-    fill(A("t8k"), 8192.0)
-    cp(A("f1"), A("L1"))
-    ts(A("f2"), A("L2"), -32.0, O.mult, K_("key"), O.add)
-    tr(A("p5", c(0, 128)), A("f1"))
-    tr(A("p6", c(0, 128)), A("f2"))
     act(A("I8k"), A("Ib"), scale=8192.0)
     act(A("I16k"), A("Ib"), scale=16384.0)
     act(A("nI"), A("Ib"), scale=-1.0)
-    act(A("hr"), ind(A("h0"), A("hl")))
-    act(A("nm"), A("p5", c(0, 128)))
-    act(A("pri"), A("p6", c(0, 128)))
+    act(A("nI8k"), A("Ib"), scale=-8192.0)
+    act(A("nI64"), A("Ib"), scale=-64.0)
+
+    for j, bank in enumerate(("p5", "p6")):
+        group(A(bank, c(0, 256)), [(A("I64"), A("ms", c(512 * j, 512 * j + 256))), (A("Ib"), A("ms", c(512 * j + 256, 512 * j + 512)))])
+        ts(A("xo", c(256 * j, 256 * j + 256)), A(bank, c(0, 256)), -2048.0, O.add)
+    e8 = topo.engines(core, T.cores[near[0]])
+    loc = [e for e in topo.engines(core, car[0]) if e not in e8]
+
+    def hand_out():
+        g.remote_dma_fused([RemoteDMATransfer(dst_ids=[dst(topo, k, core) for k in car[2 * j:2 * j + 2]], dma_engine_mask=bits(es),
+                                              remote_sem=T.sem.hin, srcs=[T.xo[:, 256 * j:256 * j + 256]], dsts=[T.hb[:], T.hb[:]])
+                            for j, es in enumerate((e8, loc))], local_sem=T.sem.lsA)
+        for _, j, serve in spread_plan[:2]:
+            g.remote_dma_fused([RemoteDMATransfer(dst_ids=[dst(topo, T.cores[q], core) for q in serve], dma_engine_mask=bits(e8),
+                                                  remote_sem=T.sem["ag%d_%d" % (rank, j)], srcs=[T.xo[:, 256 * j:256 * j + 256]],
+                                                  dsts=[T.xi[:, rank, 256 * j:256 * j + 256] for q in serve])], local_sem=T.sem.lsA)
+
+    send(A("xo"), "out", hand_out)
+    units = []
+    for q in range(NR):
+        for n, (k, j, serve) in enumerate(roles(T, topo, q)[2]):
+            if rank in serve:
+                units.append((LAND[min(n, 2)] + PACE * serve.index(rank), j, q))
+                lands(A("xi", q, c(256 * j, 256 * j + 256)), "out", "ag%d_%d" % (q, j), len(e8), units[-1][0])
+    units.sort()
+    E("g", "iota", out=A("ib"), pattern=[[1, 128]], base=-128, **small)
+    E("g", "affine_select", out=A("Sel0"), in_=A("on"), pattern=[[-16, 8], [0, 128]], compare_op=O.is_ge, fill=0.0,
+      base=0, channel_multiplier=1)
+    E("g", "affine_select", out=A("Sel0"), in_=A("Sel0"), pattern=[[16, 8], [0, 128]], compare_op=O.is_ge, fill=0.0,
+      base=1, channel_multiplier=-1)
+    E("g", "iota", out=A("r1"), pattern=[[0, NSC // 16], [256, 16]], base=0, **small)
+    E("g", "iota", out=A("r2"), pattern=[[0, NSC // 16], [-256, 16]], base=256, **small)
+
+    def unpack(n, j, q):
+        xi, lo = A("xi", q, c(256 * j, 256 * j + 256)), q * C + 512 * j
+        hi, ps = A("W", c(lo, lo + 256)), A("pn", c(512 * (n % 4), 512 * (n % 4) + 256))
+        ts(hi, xi, 1.0 / 64, O.mult, OFF + 32 - 63.0 / 128, O.add)
+        group(ps, [(A("Ih"), xi), (A("nI64"), hi)])
+        if n % 3 == 1 and n > 1:
+            ts(A("W", c(lo + 256, lo + 512)), ps, 2048 + 65 * OFF, O.add)
+        else:
+            act(A("W", c(lo + 256, lo + 512)), ps, bias=2048 + 65 * OFF)
+
+    KEY = [1022, 1007, 1006]
+    ts(K_("key"), A("oh16", c(0, 1)), 14.0, O.mult, 1008.0, O.add)
     cp(K_("wf"), A("wI"))
-    ts(A("Wb"), A("B"), K_("wf"), O.mult)
-    for s in range(3, 9):
-        act(blk("Sel", s), A("B"), scale=A("oh16", c(s, s + 1)))
-    for s in range(9, 16):
-        ts(blk("Sel", s), A("B"), A("oh16", c(s, s + 1)), O.mult)
-    ts(K_("k16"), A("kI"), 16.0, O.mult)
-    ts(K_("ev8"), K_("odd"), -8.0, O.mult, 8.0, O.add)
+    tt(K_("key"), K_("key"), K_("pmf"), O.subtract)
+    cp(A("f1"), A("L1"))
+    ts(A("Wb"), B, K_("wf"), O.mult)
+    ts(A("l1"), A("L2"), -32.0, O.mult, K_("key"), O.add)
+    tr(A("p7", c(0, 128)), A("f1"))
+    tr(A("pk", c(0, 128)), A("l1"))
+    act(A("nm"), A("p7", c(0, 128)))
+    act(A("pri"), A("pk", c(0, 128)))
+    ts(A("xl"), A("mI", c(0, 8)), 16.0, O.mult, 15.0, O.add)
+    ts(K_("k8"), A("kI"), 8.0, O.mult, 4096 * OFF, O.add)
+    act(K_("k4"), K_("k8"), F.Square, scale=0.25, bias=-1024 * OFF)
+    act(K_("kq"), K_("k4"), scale=-1.0, bias=1024 + 64 * OFF - 0.25)
+    act(A("Ac", c(0, 1)), K_("k4"), scale=-1.0, bias=-0.25)
+    act(K_("o16"), K_("odd"), scale=1.0 / 16)
+    act(K_("ev8"), K_("odd"), scale=-8.0, bias=8.0)
+    act(A("Ac", c(1, 2)), A("Ac", c(0, 1)), scale=K_("odd"), bias=K_("ev8"))
+    act(K_("kq2"), K_("kq"), scale=K_("odd"), bias=K_("ev8"))
+    act(K_("nod"), K_("odd"), scale=-1.0)
+    act(K_("n64"), K_("odd"), scale=-64.0)
     ts(A("oddI"), A("Ib"), K_("odd"), O.mult)
-    ts(A("ib"), A("mI"), -128.0, O.add)
+    ts(A("mm"), A("mI"), 15, O.bitwise_and)
+    ts(A("dc"), A("mI", c(0, 8)), K_("pdf"), O.is_equal)
+    ts(A("dl"), A("mm"), K_("pmf"), O.is_equal)
+    ts(A("dc128"), A("dc"), 128.0, O.mult)
+    ts(A("Cl"), A("mI", c(0, 8)), 16.0, O.mult, K_("pmf"), O.add)
+    ts(K_("nbc"), K_("pf"), 16384.0 + DUMP, O.add)
+    for s in range(16):
+        if s < 5:
+            act(sel(s), B, scale=A("oh16", c(s, s + 1)))
+        else:
+            ts(sel(s), B, A("oh16", c(s, s + 1)), O.mult)
 
     def twin_sums(b):
-        for k in range(4 * b, 4 * b + 4):
-            mm(blk("pn", k), A("Ib"), A("tri"), k == 4 * b, False)
-            mm(blk("pn", k), blk("Sel0", k), A("nh"), False, False)
-            mm(blk("pn", k), blk("Sel0", k), A("nl"), False, k == 4 * b + 3)
-
-    def twin_flags(b):
-        for k in range(4 * b, 4 * b + 4):
-            act(blk("dab", k), blk("pn", k), F.Abs, bias=A("nn", c(k, k + 1)))
+        ps = lambda k: blk("pn", 12 + k) if b else blk("p7", k)
+        for k in range(4):
+            mm(ps(k), blk("Sel0", 4 * b + k), A("nl"), k == 0, k == 3)
+        for k in range(4):
+            act(blk("dab", 4 * b + k), ps(k), F.Abs, bias=A("nn", c(4 * b + k, 4 * b + k + 1)))
         half = c(512 * b, 512 * b + 512)
-        act(A("eq", half), A("dab", half), F.Relu, scale=-1.0, bias=1.0)
+        act(A("eq", half), A("dab", half), F.Relu, scale=-8192.0, bias=8192.0)
+        early.append(len(ops) - 1)
+        E("g", "affine_select", out=A("eq", half), in_=A("eq", half), pattern=[[0, 4], [1, 128]], compare_op=O.is_gt, fill=0.0,
+          base=0, channel_multiplier=-1)
 
     def prepare(t, h):
         L = slots(t)
         mm(A("p6", c(384, 512)), A("Wb"), A(h), True, True)
+        act(A("uq"), A("p6", c(384, 512)), scale=1.0 / 8192, bias=(OFF - 0.5 + 1.0 / 8192) / 2)
+        group(A("p6", c(256, 384)), [(A("Wb"), A(h)), (A("nI8k"), A("uq"))])
+        act(A("v2"), A("p6", c(256, 384)), F.Square, bias=K_("k8"))
+        ts(A("i1"), A("v2"), 1.0 / 16, O.mult, A("Ac", c(0, 1)), O.add)
+        ts(A("i2"), A("v2"), K_("o16"), O.mult, A("Ac", c(1, 2)), O.add)
+        ts(A("i3"), A("i2"), 3, O.arith_shift_right, 1, O.bitwise_and)
+        tt(A("i4"), A("i1"), A("i3"), O.mult)
         act(A("fr"), A("pri"), F.Sign, scale=-1.0, bias=32.5)
-        group(A("p7", c(0, 128)), [(A("nm"), A("I32")), (A("Ib"), A("t8k")), (A("fr"), A("I8k"))])
-        act(A("qh"), A("p7", c(0, 128)))
-        if t == 0:
-            for s in range(3, 16):
-                act(blk("KZ", s), A("Ib"), scale=float(VB + 128 * (POS[s] + 1)))
-        cp(A("i1"), A("p6", c(384, 512)))
-        scan(A("M0"), A("RS"), A("pri"), O.min, O.max, 0.0)
-        ts(A("i2"), A("i1"), 4095, O.bitwise_and)
-        tt(A("eq0"), spread("M0"), A("pri"), O.is_equal)
-        ts(A("i3"), A("i2"), K_("k16"), O.add)
-        group(A("pk", c(128, 256)), [(A("I32"), A("nm")), (A("I16k"), A("eq0"))])
-        tt(A("ql"), A("p7", c(0, 128)), A("qh"), O.subtract)
+        group(A("p5", c(0, 128)), [(A("nm"), A("I32")), (A("I8k"), ones), (A("fr"), A("I8k"))])
+        act(A("qh"), A("p5", c(0, 128)))
+        tt(A("ql"), A("p5", c(0, 128)), A("qh"), O.subtract)
         group(A("p6", c(0, 128)), [(A("oddI"), A("qh")), (A("oddI"), A("ql"))])
-        tt(A("i4"), A("i2"), A("i3"), O.mult)
-        scan(A("N0"), A("RS"), A("pk", c(128, 256)), O.min, O.max, 0.0)
+        tt(A("i2"), A("i4"), A("p6", c(0, 128)), O.add)
+        ts(A("aI"), A("i2"), 8191, O.bitwise_and)
+        scan(A("M0"), RS, A("pri"), O.min, O.max, 0.0)
+        tt(A("eq0"), spread("M0"), A("pri"), O.is_equal)
+        mm(A("pk", c(0, 128)), A("I32"), A("nm"), True, False)
+        mm(A("pk", c(128, 256)), A("Ib"), A("TP"), False, False)
+        mm(A("pk", c(0, 128)), A("I16k"), A("eq0"), False, False)
+        mm(A("pk", c(128, 256)), A("I8k"), A("eq0"), False, True)
+        scan(A("N0"), A("RS"), A("pk", c(0, 256)), O.min, O.max, 0.0)
         act(A("n0c"), spread("N0"), bias=-16384.0)
-        tr(A("p7", c(256, 384)), A("n0c"))
-        act(A("nh"), A("p7", c(256, 384)))
-        for j, s in enumerate(L):
-            group(blk("pn", j), [(blk("Sel", s), A("qh")), (blk("Sel", s), A("ql"))])
-        ts(A("i5"), A("i4"), 4, O.arith_shift_right)
-        act(A("An"), spread("N0"), bias=K_("nbc"))
-        act(A("nn"), A("N0", c(15, 128, 16)), scale=-1.0, bias=16384.0)
-        act(A("e1k"), A("eq0"), scale=1024.0)
+        tr(A("p5", c(256, 384)), A("n0c"))
+        act(A("nh"), A("p5", c(256, 384)), scale=K_("odd"))
+        tt(A("nl"), A("p5", c(256, 384)), A("nh"), O.subtract)
+        act(A("nn"), col("N0", 15), scale=-1.0, bias=16384.0)
+        act(A("An"), spread("N0"), scale=-1.0, bias=K_("nbc"))
         act(A("x1"), spread("M0"), F.Relu, scale=-2048.0, bias=2048.0 * 33)
         act(A("x2"), spread("M0"), F.Relu, scale=2048.0, bias=-2048.0 * (1024 - 32 * (t + 1)))
-        if t:
-            act(A("hr"), ind(A(h), A("hl")))
-        else:
-            for s in range(16):
-                act(vslot(s), A("vv", c(s, None, 16)))
-        ts(A("sI"), spread("M0"), -1.0, O.mult, 1024.0, O.add)
-        if t:
-            ts(A("i6"), A("i5"), K_("odd"), O.mult, A("Ac", c(1, 2)), O.add)
-            ts(A("i1"), A("i5"), A("Ac", c(0, 1)), O.add)
-            z = "i1"
-        else:
-            ts(A("i6"), A("i5"), K_("odd"), O.mult, K_("ev8"), O.add)
-            z = "i5"
-        ts(A("sI"), A("sI"), 15, O.bitwise_and)
-        ts(A("i3"), A("i6"), 3, O.arith_shift_right, 1, O.bitwise_and)
-        tt(A("sd"), A("sI"), A("dl"), O.mult)
-        group(A("pk", c(480, 488)), [(A("sd"), A("dc128")), (A("Ib"), A("Cl"))])
-        tt(A("i4"), A(z), A("i3"), O.mult)
-        tt(A("i6"), A("i4"), A("p6", c(0, 128)), O.add)
-        ts(A("aI"), A("i6"), 8191, O.bitwise_and)
-        for j in range(len(L)):
-            tt(blk("hit", j), A("aI"), blk("pn", j), O.is_equal)
-        tt(A("nl"), A("p7", c(256, 384)), A("nh"), O.subtract)
-        group(A("p5", c(0, 128)), [(A("Ib"), A("ib"))] + [(blk("KZ", s), blk("hit", j)) for j, s in enumerate(L)])
-        tt(A("off"), A("aI"), A("p5", c(0, 128)), O.max)
-        cp(A("lst"), A("off"))
-        tr(A("p6", c(128, 256)), A("off"))
+        tt(A("sd"), ind(A("N0", c(128, 256)), A("xl")), A("dl"), O.mult)
+        group(A("pk", c(480, 488)), [(A("nI8k"), A("on", c(0, 8))), (A("Ib"), A("Cl")), (A("sd"), A("B3", c(256, 264)))])
+        cp(A("vl"), A("pk", c(480, 488)))
+        act(A("OV", c(0, 128)), ind(A("W", c(VB, VD)), A("vl")))
+        tt(A("ML"), A("aI"), A("p5", c(256, 384)), O.is_equal)
         twin_sums(0)
-        if t:
-            twin_sums(1)
-            twin_flags(0)
-            twin_flags(1)
+        twin_sums(1)
+        mm(A("pk", c(0, 128)), A("Ib"), A("ib"), True, False)
+        for a in range(0, len(L), 4):
+            four = list(enumerate(L))[a:a + 4]
+            for j, s in four:
+                group(blk("pn", j % 12), [(sel(s), A("qh")), (sel(s), A("ql"))])
+            for j, s in four:
+                tt(blk("hit", j), A("aI"), blk("pn", j % 12), O.is_equal)
+                mm(A("pk", c(0, 128)), blk("KZ", s), blk("hit", j), False, j == len(L) - 1)
+        tt(A("off"), A("aI"), A("pk", c(0, 128)), O.max)
+        cp(A("lst"), A("off"))
+
+    def first_terms():
+        mm(A("p6", c(0, 264)), A("Ib"), A("thh"), True, False)
+        mm(A("p6", c(0, 264)), A("Ib"), A("thl"), False, False)
+        mm(A("p6", c(0, 128)), A("Ib"), A("x1"), False, False)
+        mm(A("p6", c(0, 128)), A("nI"), A("x2"), False, False)
+        mm(A("p5", c(0, 128)), A("I32"), A("An"), True, False)
+        mm(A("p5", c(0, 128)), A("Ib"), A("cq"), False, False)
+        for k in range(8):
+            mm(A("p5", c(16 * k, 16 * k + 16)), blk("eq", k), A("m1"), False, False)
+        mm(A("p7", c(0, 128)), A("off"), A("I32"), True, False)
+        mm(A("pk", c(0, 256)), A("Ib"), A("TK"), True, False)
+        mm(A("pk", c(128, 256)), A("ML"), A("I16k"), False, False)
 
     def reads(t, h):
         win = A("W", c(0, VD))
-        A2 = TA // 4 * 2
-        act(A("d", c(16 * TA, 2048)), ind(win, A("lst", c(TA, TH))))
-        for a, b in ((0, A2), (A2, TA)):
-            part = c(16 * a, 16 * b)
-            E("v", "tensor_tensor", out=A("d", part), in0=ind(win, A("lst", c(a, b))), in1=A("hr", part), op=O.subtract)
-        cp(A("vl"), A("pk", c(480, 488)))
-        for a in range(TA, TH, 32):
-            b = min(a + 32, TH)
-            out = A("pn", c(1024 + 16 * (a - TA), 1024 + 16 * (b - TA)))
-            mm(out, A("nI"), A("hr", c(16 * a, 16 * b)), True, False)
-            mm(out, A("Ib"), A("d", c(16 * a, 16 * b)), False, True)
-        if t == 0:
-            twin_sums(1)
-        for a, b in ((0, A2), (A2, TA)):
-            act(A("ad", c(16 * a, 16 * b)), A("d", c(16 * a, 16 * b)), F.Abs)
-        act(A("ad", c(16 * TA, 2048)), A("pn", c(1024, 1024 + 16 * NB)), F.Abs)
-        key = A("pk", c(0, 128))
-        mm(key, A("Ib"), A("TK"), True, False)
-        for k in range(16):
-            mm(A("pk", c(k, 128, 16)), A("ad", c(k, None, 16)), A("B16"), False, k == 15)
-        if t == 0:
-            twin_flags(0)
-            twin_flags(1)
-        scan(A("sh"), A("r1"), A("d"), O.min, O.max, -128.0)
-        scan(A("sl"), A("r2"), A("d"), O.max, O.min, 128.0)
-        hi, lo = A("sh", c(15, None, 16)), A("sl", c(15, None, 16))
-        scan(A("ME"), A("RS"), key, O.min, O.max, 0.0)
-        group(A("p5", c(128, 256)), [(A("nI"), A("x1")), (A("Ib"), A("x2")), (hi, A("B")), (lo, A("nB"))])
-        group(A("p5", c(0, 128)), [(hi, A("B")), (lo, A("nB"))])
-        mm(A("pn", c(1536, 1664)), A("Ib"), A("mh"), True, False)
-        mm(A("pn", c(1536, 1536 + TA)), A("I2"), A(h, c(0, TA)), False, False)
-        mm(A("pn", c(1536, 1664)), A("Ib"), hi, False, False)
-        mm(A("pn", c(1536, 1664)), A("Ib"), lo, False, True)
-        tt(A("oh"), key, A("ME"), O.is_equal)
-        if t:
-            act(A("no"), A("oh"), scale=-1.0, bias=1.0)
-        else:
-            tt(A("no"), key, A("ME"), O.not_equal)
-        act(A("y1"), A("pn", c(1536, 1664)), scale=0.5, bias=MAGIC)
-        act(A("yb"), A("y1"), bias=-MAGIC)
-        tt(A("go"), A("p5", c(128, 256)), A("thE"), O.is_ge)
-        mm(A("p7", c(0, 128)), A("Ib"), A("ofd"), True, False)
         for k in range(8):
-            mm(A("p7", c(16 * k, 16 * k + 16)), blk("eq", k), A("go", c(16 * k, 16 * k + 16)), False, k == 7)
-        tt(A("PS"), A("oh"), A("p6", c(128, 256)), O.mult)
-        tt(A("Fd"), A("p5", c(0, 128)), A("th2"), O.is_ge)
-        scan(A("SE"), A("no"), A("PS"), O.mult, O.add, 0.0)
-        tt(A("l2"), A("go"), A("p7", c(0, 128)), O.is_gt)
-        ts(A("tg"), spread("SE"), -float(VB), O.add, A("cT", c(t, t + 1)), O.max)
-        tt(A("l2"), A("l2"), A("An"), O.mult)
-        tt(A("l1"), A("tg"), A("dl"), O.mult)
-        group(A("pn", c(1024, 1032)), [(A("I32"), A("Cd")), (A("l2"), A("dc"))])
-        act(A("rv", t, rank, c(128, 136)), A("pn", c(1024, 1032)))
-        group(A("pn", c(512, 520)), [(A("Fd"), A("rh2")), (A("l1"), A("dc"))])
-        cp(A("sl16"), A("pn", c(512, 520)))
-        E("v", "tensor_copy", out=ind(A("W", c(VB, WEND)), A("sl16")), in_=A("yb"))
-        tt(A("rv", t, rank, c(136, 144)), A("pn", c(1024, 1032)), A("rv", t, rank, c(128, 136)), O.subtract)
-        E("v", "tensor_copy", out=A("rv", t, rank, c(0, 128)), in_=ind(A("W", c(VB, VD)), A("vl")))
-        toks = []
-        need("g", A("rv", t, rank), False, toks)
-        settle("g", toks)
+            mm(A("pn", c(256 * k, 256 * k + 256)), A("hT"), A("Sel", c(None), c(16 * k, 16 * k + 16)), k % 2 == 0, False)
+        for a, b in zip(CUTS, CUTS[1:]):
+            (act if a < NB else cp)(A("x", c(16 * a, 16 * b)), ind(win, A("lst", c(a, b))))
+            if a == 0:
+                ops[-1]["pre"].update({k: ops[k]["busy"] for k in early[-2:]})
+        fine = sorted(set(CUTS + [32, 64, 96]))
+        for a, b in zip(fine, fine[1:]):
+            mm(A("pn", c(16 * a, 16 * b)), A("Ib"), A("x", c(16 * a, 16 * b)), False, b % 32 == 0)
+        for a in range(0, 2048, 512):
+            act(A("ad", c(a, a + 512)), A("pn", c(a, a + 512)), F.Abs, bias=-OFF)
+        for a in range(0, 2048, NSC):
+            scan(A("sh", c(a, a + NSC)), A("r1"), A("x", c(a, a + NSC)), O.min, O.max, 0.0)
+        for a in range(0, 2048, NSC):
+            scan(A("sl", c(a, a + NSC)), A("r2"), A("x", c(a, a + NSC)), O.max, O.min, 256.0)
+        hi, lo = A("sh", c(15, None, 16)), A("sl", c(15, None, 16))
+        mm(A("p6", c(0, 264)), hi, A("nB3"), False, False)
+        for k in range(16):
+            mm(A("pk", c(k, 256, 16)), A("ad", c(k, None, 16)), A("B16"), False, k == 15)
+        mm(A("p6", c(0, 264)), lo, A("B3"), False, True)
+        group(blk("pn", 0), [(A("Ib"), hi), (A("Ib"), lo)])
+        scan(A("ME"), A("RS"), A("pk", c(0, 256)), O.min, O.max, 0.0)
+        act(A("ng"), A("p6", c(0, 128)), F.Sign)
+        act(A("Rb"), A("p6", c(128, 256)), scale=-1.0 / 1024, bias=16384.0)
+        act(A("OV", c(128, 256)), blk("pn", 0), scale=0.5, bias=-0.25)
+        mm(A("p5", c(0, 128)), A("nI8k"), A("ng"), False, False)
+        for k in range(8):
+            mm(A("p5", c(16 * k, 16 * k + 16)), blk("eq", k), A("ng", c(16 * k, 16 * k + 16)), False, k == 7)
+        tt(A("e8"), A("ME", c(143, 256, 16)), col("ME", 15), O.subtract)
+        act(A("l2"), A("p5", c(0, 128)), F.Relu)
+        tt(A("ov"), ind(A("e8"), A("x8")), A("Rb"), O.is_gt)
+        group(A("pn", c(512, 520)), [(A("Ib"), A("Cl")), (A("ov"), A("dc128"))])
+        group(A("pn", c(1024, 1032)), [(A("I32"), A("Cd")), (A("l2"), A("ndc"))])
+        act(A("sg", c(0, 8)), A("p6", c(256, 264)), F.Sign)
+        act(A("ks"), A("pk", c(0, 128)))
+        cp(A("vl2"), A("pn", c(512, 520)))
+        cp(A("rv", t, rank, c(128, 136)), A("pn", c(1024, 1032)))
+        if t < STEPS - 1:
+            cp(A("rv", t, rank, c(0, 128)), ind(A("OV"), A("vl2")))
+        else:
+            ts(A("rv", t, rank, c(0, 128)), ind(A("OV"), A("vl2")), -OFF, O.add)
         piece = T.rv[:, t, rank, :]
-        g.remote_dma_fused([RemoteDMATransfer(dst_ids=[dst(topo, k, core)], dma_engine_mask=bits(es), remote_sem=T.sem["rl%d" % t],
-                                              srcs=[piece], dsts=[piece]) for (k, _), es in zip(relay, (loc[:4], e8[:4], loc[4:], e8[4:]))],
-                           local_sem=T.sem.lsD)
-        g.remote_dma_fused([RemoteDMATransfer(dst_ids=[dst(topo, T.cores[q], core) for q in near], dma_engine_mask=bits(e8),
-                                              remote_sem=T.sem["dr%d" % t], srcs=[piece], dsts=[piece for q in near])],
-                           local_sem=T.sem.lsD)
+
+        def pass_on():
+            g.remote_dma_fused([RemoteDMATransfer(dst_ids=[dst(topo, k, core)], dma_engine_mask=bits(es), remote_sem=T.sem["rl%d" % t],
+                                                  srcs=[piece], dsts=[piece])
+                                for (k, _), es in zip(relay, (loc[:4], e8[:4], loc[4:], e8[4:]))], local_sem=T.sem.lsD)
+            g.remote_dma_fused([RemoteDMATransfer(dst_ids=[dst(topo, T.cores[q], core) for q in near], dma_engine_mask=bits(e8),
+                                                  remote_sem=T.sem["dr%d_%d" % (t, rank)], srcs=[piece], dsts=[piece for q in near])],
+                               local_sem=T.sem.lsD)
+
+        send(A("rv", t, rank), "out%d" % t, pass_on)
         for q in range(NR):
             if q != rank:
-                note("rem", A("rv", t, q), True, ("dr%d" % t, len(e8) * (NR - 1), {}))
+                lands(A("rv", t, q), "out%d" % t, "dr%d_%d" % (t, q), len(e8), NEAR if q in near else FAR)
 
     def update(t, h, hn):
-        group(A("pn", c(0, 128)), [(A("Ib"), A("yb")), (A("nI"), A(h))])
-        act(A(hn), A("pn", c(0, 128)), F.Abs)
-        group(A("pn", c(1536, 1544)), [(A("yb"), A("B8th")), (A("Ib"), A("c716"))])
-        act(A("r8", c(0, 8)), A("pn", c(1536, 1544)), bias=MAGIC)
-        act(A("r8", c(8, 16)), A("r8", c(0, 8)), scale=256.0, bias=-256.0 * MAGIC)
-        group(A("pn", c(1024, 1032)), [(A("yb"), A("Bm32")), (A("Ib"), A("c960", c(8 * t, 8 * t + 8))), (A("I32"), A("r8", c(8, 16)))])
+        yb = A("OV", c(128, 256))
+        group(blk("pn", 0), [(A("Ib"), yb), (A("nI"), A(h))])
+        act(A(hn), blk("pn", 0), F.Abs, bias=-OFF)
+        tt(A("oh"), spread("ME"), A("ks"), O.is_equal)
+        mm(A("p7", c(0, 128)), A("I16k"), A("oh"), False, True)
+        act(A("ov"), A("Rb"), F.Sign, scale=-1.0, bias=16384.0)
+        ac = lambda k: A("Ac", c(k, k + 1))
+        act(A("NF"), A("ov"), F.Relu, accum_out=ac(2))
         if t < STEPS - 1:
-            ac = lambda k: A("Ac", c(k, k + 1))
-            mm(A("pn", c(512, 640)), A("on32"), A("Fd"), True, True)
-            act(A("f1"), A("pn", c(512, 640)), scale=1.0 / 64, bias=-63.0 / 16384, accum_out=ac(2))
-            act(ac(3), ac(2), bias=MAGIC)
-            act(ac(4), ac(2), scale=64.0, bias=31.5)
-            act(ac(5), ac(3), scale=-64.0, bias=64.0 * MAGIC)
-            act(ac(0), ac(5), bias=ac(4))
-            act(ac(1), ac(0), scale=K_("odd"), bias=K_("ev8"))
-        s = lambda k: A("sm", c(8 * k, 8 * k + 8))
-        col = lambda n, k: A(n, c(k, 128, 16))
-        tt(A("f2"), A("go"), A("e1k"), O.mult)
-        ts(s(0), col("SE", 15), float(VB), O.is_lt)
-        tt(s(1), col("p5", 15), col("thE", 15), O.is_lt)
-        tt(s(3), col("SE", 15), col("nm", t), O.subtract)
-        tt(s(2), s(0), s(1), O.mult)
-        tt(A("pri"), A("pri"), A("f2"), O.subtract)
-        tt(s(3), s(3), s(2), O.mult)
-        tt(s(4), A("pn", c(1024, 1032)), s(2), O.mult)
-        tt(col("nm", t), col("nm", t), s(3), O.add)
-        tt(col("pri", t), col("pri", t), s(4), O.add)
+            tot = A("pn", c(512, 513))
+            mm(tot, A("on32"), ac(2), True, True)
+            act(A("aq"), tot, scale=-1.0 / 64, bias=16 + OFF - 63.0 / 128)
+            act(ac(3), tot, scale=-1.0, bias=K_("kq"))
+            act(ac(4), tot, scale=K_("nod"), bias=K_("kq2"))
+            act(ac(0), A("aq"), scale=-64.0, bias=ac(3))
+            act(ac(1), A("aq"), scale=K_("n64"), bias=ac(4))
+        group(A("pn", c(1536, 1664)), [(A("I16k"), ones), (A("nI8k"), A("eq0")), (A("I8k"), A("ng"))])
+        mm(A("pn", c(1024, 1032)), yb, A("B8th"), True, True)
+        act(A("r8"), A("pn", c(1024, 1032)), scale=1.0 / 32, bias=(129 - 2 * OFF - 0.4375) / 32)
+        scan(A("SE"), RS, A("p7", c(0, 128)), O.min, O.max, 0.0)
+        act(A("sg", c(8, 16)), col("SE", 15), F.Sign, scale=-1.0, bias=16384.0 + VB - 0.5)
+        tt(A("pri"), A("pri"), A("pn", c(1536, 1664)), O.min)
+        tt(A("l1"), spread("SE"), A("NF"), O.mult)
+        group(A("pn", c(512, 520)), [(A("I32"), A("Ck")), (A("NF"), A("rh2", c(0, 8))), (A("NF"), A("rh2", c(8, 16))), (A("l1"), A("dc"))])
+        sg = lambda k: A("sg", c(8 * k, 8 * k + 8))
+        new = lambda k: A("pn", c(1024 + 8 * k, 1032 + 8 * k))
+        terms = [(new(0), yb, A("Bm32")), (new(0), A("I8k"), A("r8")), (new(1), A("Ib"), A("c32k")), (new(0), A("I8k"), sg(0)),
+                 (new(1), A("I8k"), sg(0)), (new(2), A("nI8k"), sg(0)), (new(1), A("I32"), col("SE", 15)),
+                 (new(2), A("I32"), col("SE", 15)), (new(0), A("I8k"), sg(1)), (new(1), A("I8k"), sg(1)), (new(2), A("nI8k"), sg(1))]
+        for k, (o, a, b) in enumerate(terms):
+            mm(o, a, b, k == 0, k == len(terms) - 1)
+        tt(A("sm", c(0, 8)), A("pn", c(512, 520)), A("cT", c(8 * t, 8 * t + 8)), O.max)
+        act(col("pri", t), new(0), F.Relu, bias=KEY[t] - 32.0 * (t + 1) + 512 * OFF - 256 * 129 - 16384)
+        cp(A("sl16"), A("sm", c(0, 8)))
+        tt(A("sm", c(8, 16)), col("nm", t), new(1), O.max)
+        cp(ind(A("W", c(VB, WEND)), A("sl16")), yb)
+        tt(col("nm", t), A("sm", c(8, 16)), new(2), O.min)
+        if t < STEPS - 1:
+            mm(A("pn", c(1536, 1664)), A(hn), A("nI"), True, True)
+            act(A("hT"), A("pn", c(1536, 1664)))
 
     def drains(t):
-        tt(A("dcd"), A("rv", t, c(None), c(128, 136)), A("rv", t, c(None), c(136, 144)), O.add)
-        cp(A("dL"), A("dcd"))
         for q in range(NR - 1, -1, -1):
-            E("v", "tensor_copy", out=ind(A("W", c(0, VB)), A("dL", c(8 * q, 8 * q + 8))), in_=A("rv", t, q, c(0, 128)))
+            cp(ind(A("W", c(0, VB)), A("rv", t, q, c(128, 136))), A("rv", t, q, c(0, 128)))
 
+    for s in range(16):
+        act(blk("KZ", s), A("Ib"), scale=float(VB + 128 * (POS[s] + 1)))
+        if s % 2:
+            ts(vslot(s), A("vv", c(s, None, 16)), OFF, O.add)
+        else:
+            act(vslot(s), A("vv", c(s, None, 16)), bias=OFF)
+    fill(col("TP", 0), 128.0 * POS[0])
+    ts(A("Ih"), A("dI"), 0, O.is_equal)
+    ts(own, A("ms"), OFF, O.add)
     fill(A("on32"), 1.0)
     cp(K_("tf"), A("tI"))
     ts(A("thd"), A("I32"), K_("tf"), O.mult)
-    mm(A("p5", c(256, 384)), A("on32"), A("thd"), True, True)
-    ts(A("xl"), A("mI", c(0, 8)), 16.0, O.mult, 15.0, O.add)
-    ts(A("mm"), A("mI"), 15, O.bitwise_and)
-    ts(A("dl"), A("mm"), K_("pmf"), O.is_equal)
-    ts(A("dc"), A("mI", c(0, 8)), K_("pdf"), O.is_equal)
-    ts(A("dc128"), A("dc"), 128.0, O.mult)
-    ts(A("Cl"), A("mI", c(0, 8)), 16.0, O.mult, K_("pmf"), O.add)
-    ts(K_("nbc"), K_("pf"), -1.0, O.mult, -16384.0 - DUMP, O.add)
-    ts(A("tri"), A("dI"), 0, O.is_ge, 16384.0, O.mult)
-    for k in range(3):
-        ts(A("cT", c(k, k + 1)), K_("pf"), 128.0 * POS[k], O.add)
-    ts(A("ofd"), A("mm"), K_("pmf"), O.not_equal, 4.0, O.mult)
-    ts(A("B8th"), A("dc"), 0.125, O.mult)
-    ts(A("Bm32"), A("dc"), -32.0, O.mult)
-    fill(A("c716"), -0.4375)
-    for k in range(STEPS):
-        fill(A("c960", c(8 * k, 8 * k + 8)), 960.0 - 32 * k)
-    ts(A("B16"), A("dc"), 16.0, O.mult)
-    ts(A("Cd"), A("Cl"), float(DUMP), O.add)
-    ts(A("rh2"), A("dc"), 2048.0, O.mult)
+    mm(A("p6", c(0, 128)), A("on32"), A("thd"), True, True)
+    mm(A("p5", c(0, 128)), A(H[0]), A("nI"), True, True)
+    act(A("hT"), A("p5", c(0, 128)))
+    act(A("thc", c(0, 128)), A("p6", c(0, 128)), bias=-0.5)
+    act(A("thc", c(256, 264)), A("p6", c(15, 128, 16)), bias=-0.5)
+    tt(A("thc", c(128, 256)), A("p6", c(0, 128)), A("dl"), O.mult)
+    act(A("thh"), A("thc"))
+    tt(A("thl"), A("thc"), A("thh"), O.subtract)
+    act(A("B3", c(128, 256)), B)
+    act(A("B3", c(256, 264)), A("dc"))
+    act(A("nB3"), A("B3"), scale=-1.0)
+    ts(A("cq"), A("dl"), 16384.0, O.mult, -24576.0, O.add)
+    fill(A("m1"), -1.0)
     fill(A("W", c(DUMP, VB)), 0.0)
-    fill(A("mh"), -0.5)
-    ts(A("th2"), A("ofd"), 1024.0, O.mult)
-    act(A("thE"), A("p5", c(256, 384)))
-    act(A("nB"), A("B"), scale=-1.0)
-    act(A("I2"), A("Ib"), scale=2.0)
+    ts(A("B16", c(0, 8)), A("dc"), 16.0, O.mult)
+    ts(A("B16", c(8, 16)), A("dc"), 16.0, O.mult)
+    cp(A("x8"), A("mI", c(0, 8)))
+    ts(A("Cd"), A("Cl"), float(DUMP), O.add)
+    ts(A("ndc"), A("dc"), -1.0, O.mult)
+    act(A("B8th"), A("dc"), scale=0.125)
+    act(A("Bm32"), A("dc"), scale=-32.0)
+    fill(A("c32k"), -32768.0)
+    for k in range(STEPS):
+        act(A("cT", c(8 * k, 8 * k + 8)), A("Cl"), bias=128.0 * POS[k])
+    act(A("Ck"), A("Cl"), bias=float(VD - VB))
+    act(A("rh2", c(0, 8)), A("dc"), scale=-16384.0 - VD)
+    act(A("rh2", c(8, 16)), A("ndc"), scale=K_("pf"))
     prepare(0, H[0])
-    tt(A("th2"), A("thE"), A("th2"), O.add)
+    first_terms()
+    for n, (_, j, q) in enumerate(units):
+        unpack(n, j, q)
     for t in range(STEPS):
         h, hn = H[t % 2], H[1 - t % 2]
         reads(t, h)
-        if t == 0:
-            for s in (0, 1):
-                ts(blk("Sel", s), A("B"), A("oh16", c(s, s + 1)), O.mult)
-                act(blk("KZ", s), A("Ib"), scale=float(VB + 128 * (POS[s] + 1)))
         update(t, h, hn)
         if t < STEPS - 1:
             prepare(t + 1, hn)
+            first_terms()
         else:
-            E("y", "dma_start", out=ext("yh"), in_=A(hn))
+            act(own, own, bias=-OFF)
             for s in range(16):
-                act(A("vv", c(s, None, 16)), vslot(s))
+                act(A("vv", c(s, None, 16)), vslot(s), bias=-OFF)
             tr(A("pn", c(0, 128)), A("nm"))
             ts(A("sI"), A("pri"), -0.03125, O.mult, 32.0 - 31.0 / 64, O.add)
             ts(A("off"), A("sI"), 31.0, O.min)
@@ -586,10 +714,13 @@ def rank_program(g, core, T, topo):
             cp(A("f1"), A("pn", c(0, 128)))
             cp(A("l1"), A("pn", c(512, 640)))
             E("y", "dma_start", out=ext("ypnd"), in_=A("f1"))
+            E("y", "dma_start", out=ext("yh"), in_=A(hn))
             E("y", "dma_start", out=ext("ydue"), in_=A("l1"))
             E("y", "dma_start", out=ext("yval"), in_=A("vv"))
         drains(t)
-    E("y", "dma_start", out=ext("ymem"), in_=A("W", c(rank * C, rank * C + C)))
+    E("y", "dma_start", out=ext("ymem"), in_=own)
+    issue()
+    g.wait_ge(T.sem.lsA, 3 * len(e8) + len(loc))
     g.wait_ge(T.sem.lsD, STEPS * (2 * len(e8) + len(loc)))
     for k in range(ndma[0]):
         if not any(seen[q].get("dm%d" % k, 0) for q in Q):

@@ -11,9 +11,9 @@ OFF = 160.0
 MAGIC = 12582912.0
 POS = [2, 1, 0] + list(range(3, 16))
 NB, CUTS = 56, [0, 32, 56, 96, 128]
-HOP, FAR, NEAR = 0.12, 5.5, 4.0
-LAND, PACE = (8.0, 11.5, 12.0), 1.5
-ROUNDS, ROOM, DOUBT = 1, 0.16, 2.0
+HOP, FAR, NEAR, LAG = 0.12, 4.5, 3.5, 0.15
+LAND, PACE = (7.0, 9.8, 10.3, 10.9, 10.0, 10.6), 1.0
+ROUNDS, ROOM, DOUBT = 1, 0.05, 1.5
 NSC = 1024
 
 S, P = "sbuf", "psum"
@@ -30,13 +30,13 @@ SCRATCH = {
     "dc": (S, [128, 8], f32), "ndc": (S, [128, 8], f32), "B8th": (S, [128, 8], bf), "Bm32": (S, [128, 8], bf),
     "TP": (S, [128, 128], bf), "uq": (S, [128, 128], bf), "c32k": (S, [128, 8], bf), "B16": (S, [128, 16], bf),
     "dc128": (S, [128, 8], bf), "Cl": (S, [128, 8], bf), "Cd": (S, [128, 8], f32), "Ck": (S, [128, 8], f32),
-    "rh2": (S, [128, 16], bf), "cT": (S, [128, 24], f32), "oh16": (S, [128, 16], f32), "m1": (S, [128, 16], bf),
+    "rh2": (S, [128, 16], bf), "cT": (S, [128, 24], f32), "oh16": (S, [128, 16], f32), "m3": (S, [128, 128], bf),
     "KZ": (S, [128, 2048], bf), "on": (S, [128, 1024], bf), "Sel": (S, [128, 16, 128], bf), "Sel0": (S, [128, 1024], bf),
     "TK": (S, [128, 256], bf), "RS": (S, [128, 256], f32), "xl": (S, [128, 8], u16), "x8": (S, [128, 8], u16),
-    "r1": (S, [128, NSC], bf), "r2": (S, [128, NSC], bf), "thh": (S, [128, 264], bf), "thl": (S, [128, 264], bf),
+    "r1": (S, [128, NSC], bf), "r2": (S, [128, NSC], bf),
     "nn": (S, [128, 8], f32), "on32": (S, [128, 128], f32), "ib": (S, [128, 128], bf),
     "wI": (S, [128, 1], i32), "kI": (S, [128, 1], i32), "tI": (S, [128, 1], i32),
-    "Wb": (S, [128, 128], bf), "thd": (S, [128, 128], f32), "thc": (S, [128, 264], f32),
+    "Wb": (S, [128, 128], bf), "thd": (S, [128, 128], f32), "thc": (S, [128, 264], f16),
     "L1": (S, [128, 128], i32), "L2": (S, [128, 128], i32), "f1": (S, [128, 128], f32),
     "h0": (S, [128, 128], bf), "h1": (S, [128, 128], bf), "hT": (S, [128, 128], bf),
     "nm": (S, [128, 128], f32), "pri": (S, [128, 128], f32),
@@ -82,7 +82,7 @@ def roles(T, topo, r):
     car = [c for c in topo.cores_of(me) if c != me and topo.may_write(c, T.cores[far[0]])]
     car = sorted(car, key=lambda c: (topo.die(c) != topo.die(me), c))
     a = sum(q < r for q in near)
-    relay = [(car[(a + b) % 2 * 2 + b // 2], q) for b, q in enumerate(far)]
+    relay = [(car[(a + b) % 2 * 2 + b // 2], [q]) for b, q in enumerate(far)][::-1]
     near, far = near[a:] + near[:a], far[a:] + far[:a]
     spread = [(me, 0, near), (me, 1, near[:2])] + [(k, j // 2, far[j % 2::2] + near[2:] * (j == 3)) for j, k in enumerate(car)]
     return near, car, spread, relay
@@ -102,12 +102,12 @@ def helper_program(g, core, T, topo):
         g.remote_dma_fused([RemoteDMATransfer(dst_ids=[dst(topo, T.cores[q], core) for q in serve], dma_engine_mask=bits(es),
                                               remote_sem=T.sem["ag%d_%d" % (r, half)], srcs=[T.hb[:]],
                                               dsts=[T.xi[:, r, 256 * half:256 * half + 256] for q in serve])], local_sem=T.sem.hout)
-        q = dict(relay)[core]
+        serve = dict(relay)[core]
         for t in range(STEPS):
-            g.wait_ge(T.sem["rl%d" % t], len(es) // 2)
-            g.remote_dma_fused([RemoteDMATransfer(dst_ids=[dst(topo, T.cores[q], core)], dma_engine_mask=bits(es),
+            g.wait_ge(T.sem["rl%d" % t], len(topo.engines(me, core)))
+            g.remote_dma_fused([RemoteDMATransfer(dst_ids=[dst(topo, T.cores[q], core) for q in serve], dma_engine_mask=bits(es),
                                                   remote_sem=T.sem["dr%d_%d" % (t, r)], srcs=[T.rv[:, t, r, :]],
-                                                  dsts=[T.rv[:, t, r, :]])], local_sem=T.sem.hout)
+                                                  dsts=[T.rv[:, t, r, :] for q in serve])], local_sem=T.sem.hout)
         g.wait_ge(T.sem.hout, len(es) * (1 + STEPS))
 
 
@@ -117,6 +117,7 @@ def rank_program(g, core, T, topo):
         helper_program(g, core, T, topo)
         return
     near, car, spread_plan, relay = roles(T, topo, rank)
+    straight = sorted(near, reverse=rank >= NR // 2)
 
     Q = {"g": g, "v": g.vector, "s": g.scalar, "t": g.tensor, "y": g.sync}
     cnt, seen, log, ndma = {}, {q: {} for q in Q}, {}, [0]
@@ -136,7 +137,10 @@ def rank_program(g, core, T, topo):
             else:
                 a = last = i
             lo, hi = lo * n + a, hi * n + last
-        return {"ap": ap[(slice(None),) + idx], "n": name, "r": (lo, hi + 1, step), "e": size, "ind": None}
+        return {"ap": ap[(slice(None),) + idx], "n": name, "r": (lo, hi + 1, (step, 1)), "e": size, "ind": None}
+
+    def apart(lo, st, lo2, st2):
+        return st[0] == st2[0] > 1 and st2[1] <= (lo - lo2) % st[0] <= st[0] - st[1]
 
     def ind(win, offs):
         return {"ap": win["ap"].indirect(offs["ap"]), "n": win["n"], "r": win["r"], "e": win["e"], "ind": offs}
@@ -144,7 +148,7 @@ def rank_program(g, core, T, topo):
     def spans(v):
         lo, hi, st = v["r"]
         if v["n"] in SCRATCH and SCRATCH[v["n"]][0] == P:
-            return True, lo // 512 * 512, (hi + 511) // 512 * 512, 1
+            return True, lo // 512 * 512, (hi + 511) // 512 * 512, (1, 1)
         return False, lo, hi, st
 
     def need(q, v, write, acc):
@@ -154,7 +158,7 @@ def rank_program(g, core, T, topo):
                 same = e["q"] == q
                 if same and (ps and q == "t" or not e["w"]):
                     continue
-                if st > 1 and e["st"] == st and (lo - e["lo"]) % st and "dma" not in (q, e["q"]):
+                if apart(lo, st, e["lo"], e["st"]):
                     continue
                 if e["w"] or write or ps and not same:
                     acc.append(e["tok"])
@@ -162,7 +166,7 @@ def rank_program(g, core, T, topo):
     def note(q, v, write, tok):
         ps, lo, hi, st = spans(v)
         L = log.setdefault(v["n"], [])
-        if write and st == 1:
+        if write and st[0] == 1:
             L[:] = [e for e in L if not (lo <= e["lo"] and e["hi"] <= hi and not ps)]
         if ps:
             L[:] = [e for e in L if not (e["q"] == q and e["w"] == write and e["lo"] == lo and e["hi"] == hi)]
@@ -213,7 +217,7 @@ def rank_program(g, core, T, topo):
         for v in wr:
             note(dq, v, True, tok)
 
-    ops, past, loads, early = [], {}, [0.0], []
+    ops, past, loads, early, last_hit = [], {}, [0.0], [], [0]
 
     def op(q, rd, wr, busy, done, run):
         pre = {}
@@ -221,13 +225,13 @@ def rank_program(g, core, T, topo):
             ps, lo, hi, st = spans(v)
             for e in past.get(v["n"], []):
                 o = ops[e[4]]
-                if e[0] < hi and lo < e[1] and (e[3] or write or ps and o["q"] != q) and not (st > 1 and e[2] == st and (lo - e[0]) % st):
+                if e[0] < hi and lo < e[1] and (e[3] or write or ps and o["q"] != q) and not apart(lo, st, e[0], e[2]):
                     free = o["q"] == q and (ps and q == "t" or not e[3] or v["n"] == "turn" + q)
-                    pre[e[4]] = max(pre.get(e[4], 0), o["busy"] if free else o["done"] + (ROOM if o["q"] == q else HOP))
+                    pre[e[4]] = max(pre.get(e[4], 0), o["busy"] if free else o["done"] + HOP)
         for v, write in [(v, False) for v in rd] + [(v, True) for v in wr]:
             ps, lo, hi, st = spans(v)
             L = past.setdefault(v["n"], [])
-            if write and st == 1:
+            if write and st[0] == 1:
                 L[:] = [e for e in L if not (lo <= e[0] and e[1] <= hi)]
             L.append((lo, hi, st, write, len(ops)))
         ops.append({"q": q, "pre": pre, "busy": busy, "done": done, "run": run})
@@ -248,7 +252,7 @@ def rank_program(g, core, T, topo):
                 L = used.setdefault(ops[k]["q"], [])
                 if busy[k]:
                     j = 0
-                    while j < len(L) and L[j][0] < t + busy[k] - 1e-9:
+                    while j < len(L) and L[j][0] < t + busy[k] - ROOM:
                         t = max(t, L[j][1])
                         j += 1
                     L.insert(j, (t, t + busy[k]))
@@ -264,8 +268,12 @@ def rank_program(g, core, T, topo):
         for k in sorted(N, key=lambda k: (est[k], k)):
             ops[k]["run"]()
 
+    def behind(*ks):
+        for k in ks:
+            ops[-1]["pre"][k] = max(ops[-1]["pre"].get(k, 0.0), ops[k]["busy"])
+
     def mark(name):
-        return {"n": name, "r": (0, 1, 1), "ind": None}
+        return {"n": name, "r": (0, 1, (1, 1)), "ind": None}
 
     def E(q, meth, _pos=(), **kw):
         wr, rd = [], []
@@ -330,7 +338,7 @@ def rank_program(g, core, T, topo):
         E("v", "memset", (v, x))
 
     def ext(name, *idx):
-        return {"ap": T[name][(slice(None),) + idx], "n": name + str(idx), "r": (0, 1, 1), "ind": None}
+        return {"ap": T[name][(slice(None),) + idx], "n": name + str(idx), "r": (0, 1, (1, 1)), "ind": None}
 
     def send(v, name, run):
         def go():
@@ -418,7 +426,7 @@ def rank_program(g, core, T, topo):
     for q in range(NR):
         for n, (k, j, serve) in enumerate(roles(T, topo, q)[2]):
             if rank in serve:
-                units.append((LAND[min(n, 2)] + PACE * serve.index(rank), j, q))
+                units.append((LAND[n] + PACE * serve.index(rank), j, q))
                 lands(A("xi", q, c(256 * j, 256 * j + 256)), "out", "ag%d_%d" % (q, j), len(e8), units[-1][0])
     units.sort()
     E("g", "iota", out=A("ib"), pattern=[[1, 128]], base=-128, **small)
@@ -518,10 +526,6 @@ def rank_program(g, core, T, topo):
         act(A("An"), spread("N0"), scale=-1.0, bias=K_("nbc"))
         act(A("x1"), spread("M0"), F.Relu, scale=-2048.0, bias=2048.0 * 33)
         act(A("x2"), spread("M0"), F.Relu, scale=2048.0, bias=-2048.0 * (1024 - 32 * (t + 1)))
-        tt(A("sd"), ind(A("N0", c(128, 256)), A("xl")), A("dl"), O.mult)
-        group(A("pk", c(480, 488)), [(A("nI8k"), A("on", c(0, 8))), (A("Ib"), A("Cl")), (A("sd"), A("B3", c(256, 264)))])
-        cp(A("vl"), A("pk", c(480, 488)))
-        act(A("OV", c(0, 128)), ind(A("W", c(VB, VD)), A("vl")))
         tt(A("ML"), A("aI"), A("p5", c(256, 384)), O.is_equal)
         twin_sums(0)
         twin_sums(1)
@@ -533,19 +537,16 @@ def rank_program(g, core, T, topo):
             for j, s in four:
                 tt(blk("hit", j), A("aI"), blk("pn", j % 12), O.is_equal)
                 mm(A("pk", c(0, 128)), blk("KZ", s), blk("hit", j), False, j == len(L) - 1)
+        last_hit[0] = len(ops) - 1
         tt(A("off"), A("aI"), A("pk", c(0, 128)), O.max)
         cp(A("lst"), A("off"))
 
     def first_terms():
-        mm(A("p6", c(0, 264)), A("Ib"), A("thh"), True, False)
-        mm(A("p6", c(0, 264)), A("Ib"), A("thl"), False, False)
+        mm(A("p6", c(0, 264)), A("Ih"), A("thc"), True, False)
         mm(A("p6", c(0, 128)), A("Ib"), A("x1"), False, False)
         mm(A("p6", c(0, 128)), A("nI"), A("x2"), False, False)
         mm(A("p5", c(0, 128)), A("I32"), A("An"), True, False)
         mm(A("p5", c(0, 128)), A("Ib"), A("cq"), False, False)
-        for k in range(8):
-            mm(A("p5", c(16 * k, 16 * k + 16)), blk("eq", k), A("m1"), False, False)
-        mm(A("p7", c(0, 128)), A("off"), A("I32"), True, False)
         mm(A("pk", c(0, 256)), A("Ib"), A("TK"), True, False)
         mm(A("pk", c(128, 256)), A("ML"), A("I16k"), False, False)
 
@@ -553,27 +554,35 @@ def rank_program(g, core, T, topo):
         win = A("W", c(0, VD))
         for k in range(8):
             mm(A("pn", c(256 * k, 256 * k + 256)), A("hT"), A("Sel", c(None), c(16 * k, 16 * k + 16)), k % 2 == 0, False)
+            behind(last_hit[0])
         for a, b in zip(CUTS, CUTS[1:]):
             (act if a < NB else cp)(A("x", c(16 * a, 16 * b)), ind(win, A("lst", c(a, b))))
             if a == 0:
-                ops[-1]["pre"].update({k: ops[k]["busy"] for k in early[-2:]})
+                behind(*early[-2:])
         fine = sorted(set(CUTS + [32, 64, 96]))
         for a, b in zip(fine, fine[1:]):
             mm(A("pn", c(16 * a, 16 * b)), A("Ib"), A("x", c(16 * a, 16 * b)), False, b % 32 == 0)
+        mm(A("p7", c(0, 128)), A("off"), A("I32"), True, False)
+        behind(len(ops) - 2)
         for a in range(0, 2048, 512):
             act(A("ad", c(a, a + 512)), A("pn", c(a, a + 512)), F.Abs, bias=-OFF)
         for a in range(0, 2048, NSC):
             scan(A("sh", c(a, a + NSC)), A("r1"), A("x", c(a, a + NSC)), O.min, O.max, 0.0)
         for a in range(0, 2048, NSC):
             scan(A("sl", c(a, a + NSC)), A("r2"), A("x", c(a, a + NSC)), O.max, O.min, 256.0)
+        tt(A("sd"), ind(A("N0", c(128, 256)), A("xl")), A("dl"), O.mult)
+        behind(len(ops) - 2)
+        group(A("pn", c(528, 536)), [(A("Ib"), A("Cl")), (A("sd"), A("B3", c(256, 264)))])
+        ts(A("vl"), A("pn", c(528, 536)), -8192.0, O.add)
+        act(A("OV", c(0, 128)), ind(A("W", c(VB, VD)), A("vl")))
         hi, lo = A("sh", c(15, None, 16)), A("sl", c(15, None, 16))
         mm(A("p6", c(0, 264)), hi, A("nB3"), False, False)
+        mm(A("p6", c(0, 264)), lo, A("B3"), False, True)
         for k in range(16):
             mm(A("pk", c(k, 256, 16)), A("ad", c(k, None, 16)), A("B16"), False, k == 15)
-        mm(A("p6", c(0, 264)), lo, A("B3"), False, True)
         group(blk("pn", 0), [(A("Ib"), hi), (A("Ib"), lo)])
         scan(A("ME"), A("RS"), A("pk", c(0, 256)), O.min, O.max, 0.0)
-        act(A("ng"), A("p6", c(0, 128)), F.Sign)
+        ts(A("ng"), A("p6", c(0, 128)), 0.0, O.is_lt, -2.0, O.mult)
         act(A("Rb"), A("p6", c(128, 256)), scale=-1.0 / 1024, bias=16384.0)
         act(A("OV", c(128, 256)), blk("pn", 0), scale=0.5, bias=-0.25)
         mm(A("p5", c(0, 128)), A("nI8k"), A("ng"), False, False)
@@ -595,17 +604,17 @@ def rank_program(g, core, T, topo):
         piece = T.rv[:, t, rank, :]
 
         def pass_on():
-            g.remote_dma_fused([RemoteDMATransfer(dst_ids=[dst(topo, k, core)], dma_engine_mask=bits(es), remote_sem=T.sem["rl%d" % t],
-                                                  srcs=[piece], dsts=[piece])
-                                for (k, _), es in zip(relay, (loc[:4], e8[:4], loc[4:], e8[4:]))], local_sem=T.sem.lsD)
-            g.remote_dma_fused([RemoteDMATransfer(dst_ids=[dst(topo, T.cores[q], core) for q in near], dma_engine_mask=bits(e8),
-                                                  remote_sem=T.sem["dr%d_%d" % (t, rank)], srcs=[piece], dsts=[piece for q in near])],
+            g.remote_dma_fused([RemoteDMATransfer(dst_ids=[dst(topo, k, core) for k, _ in relay], dma_engine_mask=bits(e8 + loc),
+                                                  remote_sem=T.sem["rl%d" % t], srcs=[piece], dsts=[piece for k in relay])],
+                               local_sem=T.sem.lsD)
+            g.remote_dma_fused([RemoteDMATransfer(dst_ids=[dst(topo, T.cores[q], core) for q in straight], dma_engine_mask=bits(e8),
+                                                  remote_sem=T.sem["dr%d_%d" % (t, rank)], srcs=[piece], dsts=[piece for q in straight])],
                                local_sem=T.sem.lsD)
 
         send(A("rv", t, rank), "out%d" % t, pass_on)
         for q in range(NR):
             if q != rank:
-                lands(A("rv", t, q), "out%d" % t, "dr%d_%d" % (t, q), len(e8), NEAR if q in near else FAR)
+                lands(A("rv", t, q), "out%d" % t, "dr%d_%d" % (t, q), len(e8), (NEAR if q in near else FAR) + LAG * (NR - 1 - q))
 
     def update(t, h, hn):
         yb = A("OV", c(128, 256))
@@ -624,7 +633,7 @@ def rank_program(g, core, T, topo):
             act(ac(4), tot, scale=K_("nod"), bias=K_("kq2"))
             act(ac(0), A("aq"), scale=-64.0, bias=ac(3))
             act(ac(1), A("aq"), scale=K_("n64"), bias=ac(4))
-        group(A("pn", c(1536, 1664)), [(A("I16k"), ones), (A("nI8k"), A("eq0")), (A("I8k"), A("ng"))])
+        group(A("pn", c(1536, 1664)), [(A("I8k"), A("m3")), (A("nI8k"), A("eq0")), (A("I8k"), A("ng"))])
         mm(A("pn", c(1024, 1032)), yb, A("B8th"), True, True)
         act(A("r8"), A("pn", c(1024, 1032)), scale=1.0 / 32, bias=(129 - 2 * OFF - 0.4375) / 32)
         scan(A("SE"), RS, A("p7", c(0, 128)), O.min, O.max, 0.0)
@@ -668,25 +677,23 @@ def rank_program(g, core, T, topo):
     mm(A("p6", c(0, 128)), A("on32"), A("thd"), True, True)
     mm(A("p5", c(0, 128)), A(H[0]), A("nI"), True, True)
     act(A("hT"), A("p5", c(0, 128)))
-    act(A("thc", c(0, 128)), A("p6", c(0, 128)), bias=-0.5)
-    act(A("thc", c(256, 264)), A("p6", c(15, 128, 16)), bias=-0.5)
+    ts(A("thc", c(0, 128)), A("p6", c(0, 128)), -0.5, O.add)
+    ts(A("thc", c(256, 264)), A("p6", c(15, 128, 16)), -0.5, O.add)
     tt(A("thc", c(128, 256)), A("p6", c(0, 128)), A("dl"), O.mult)
-    act(A("thh"), A("thc"))
-    tt(A("thl"), A("thc"), A("thh"), O.subtract)
     act(A("B3", c(128, 256)), B)
     act(A("B3", c(256, 264)), A("dc"))
     act(A("nB3"), A("B3"), scale=-1.0)
-    ts(A("cq"), A("dl"), 16384.0, O.mult, -24576.0, O.add)
-    fill(A("m1"), -1.0)
-    fill(A("W", c(DUMP, VB)), 0.0)
-    ts(A("B16", c(0, 8)), A("dc"), 16.0, O.mult)
-    ts(A("B16", c(8, 16)), A("dc"), 16.0, O.mult)
+    act(A("cq"), A("dl"), scale=16384.0, bias=-32768.0)
+    E("g", "iota", out=A("m3"), pattern=[[0, 128]], base=3, **small)
+    E("g", "iota", out=A("W", c(DUMP, VB)), pattern=[[0, 128]], base=0, **small)
+    act(A("B16", c(0, 8)), A("dc"), scale=16.0)
+    act(A("B16", c(8, 16)), A("dc"), scale=16.0)
     cp(A("x8"), A("mI", c(0, 8)))
-    ts(A("Cd"), A("Cl"), float(DUMP), O.add)
-    ts(A("ndc"), A("dc"), -1.0, O.mult)
+    act(A("Cd"), A("Cl"), bias=float(DUMP))
+    act(A("ndc"), A("dc"), scale=-1.0)
     act(A("B8th"), A("dc"), scale=0.125)
     act(A("Bm32"), A("dc"), scale=-32.0)
-    fill(A("c32k"), -32768.0)
+    E("g", "iota", out=A("c32k"), pattern=[[0, 8]], base=-32768, **small)
     for k in range(STEPS):
         act(A("cT", c(8 * k, 8 * k + 8)), A("Cl"), bias=128.0 * POS[k])
     act(A("Ck"), A("Cl"), bias=float(VD - VB))

@@ -5,15 +5,25 @@ NR, C, TH, STEPS = 8, 1024, 128, 3
 DUMP = NR * C
 VB = DUMP + TH
 VD = VB + 16 * TH
-WEND = VD + TH
+WEND = VD + 16 * TH
 PW = 136
 OFF = 160.0
-MAGIC = 12582912.0
+HI = OFF - 63.5 / 128
+SLOT = OFF + VB // 128
+NOFF = 128 * OFF + 24576.0
 POS = [2, 1, 0] + list(range(3, 16))
 NB, CUTS = 56, [0, 32, 56, 96, 128]
-HOP, FAR, NEAR, LAG = 0.12, 4.5, 3.5, 0.15
+ABS = [((0, 32), (0, 16)), ((32, 64), (0, 16)), ((64, 128), (0, 8)), ((64, 128), (8, 12)), ((64, 128), (12, 16))]
+HOP, FAR, NEAR, LAG = 0.25, 4.8, 4.0, 0.15
 LAND, PACE = (7.0, 9.8, 10.3, 10.9, 10.0, 10.6), 1.0
 ROUNDS, ROOM, DOUBT = 1, 0.05, 1.5
+SCA, GAT = 2.5, 1.5
+TFIX, TCYC = 20, 0.55
+VFIX, SFIX = 40, 30
+NV, LOV, NW = (8, 3, 16), (9, 11, 13), 0
+LAST = 4
+TRI, TWV, HITS, PL, OFFQ, YF, RK = 0, 0, 3, 0, 2, 1, -1
+UV, SAME = 0, 0.25
 NSC = 1024
 
 S, P = "sbuf", "psum"
@@ -22,43 +32,45 @@ SCRATCH = {
     "W": (S, [128, WEND], bf), "vv": (S, [128, 16 * TH], bf), "ms": (S, [128, C], bf),
     "xo": (S, [128, 512], f16), "xi": (S, [128, NR, 512], f16), "hb": (S, [128, 256], f16),
     "pI": (S, [128, 1], i32), "mI": (S, [128, 128], i32), "dI": (S, [128, 128], i32),
-    "ci1": (S, [128, 4], i32), "cols": (S, [128, 20], f32), "aq": (S, [128, 1], bf), "md": (S, [128, 128], i32), "mm": (S, [128, 128], i32),
+    "ci1": (S, [128, 8], i32), "cols": (S, [128, 24], f32), "aq": (S, [128, 1], bf), "md": (S, [128, 128], i32), "mm": (S, [128, 128], i32),
     "I32": (S, [128, 128], f32), "Ib": (S, [128, 128], bf), "nI": (S, [128, 128], bf), "Ih": (S, [128, 128], f16),
-    "I64": (S, [128, 128], bf), "nI64": (S, [128, 128], bf), "oddI": (S, [128, 128], bf), "I8k": (S, [128, 128], bf),
-    "nI8k": (S, [128, 128], bf), "I16k": (S, [128, 128], bf),
+    "I64": (S, [128, 128], bf), "nI64": (S, [128, 128], bf), "oddI": (S, [128, 128], f32), "I8k": (S, [128, 128], bf),
+    "nI8k": (S, [128, 128], bf), "I16k": (S, [128, 128], bf), "I32k": (S, [128, 128], bf),
+    "I129": (S, [128, 128], bf), "nI129": (S, [128, 128], bf), "nI128": (S, [128, 128], bf),
     "B3": (S, [128, 264], bf), "nB3": (S, [128, 264], bf), "dl": (S, [128, 128], bf), "cq": (S, [128, 128], bf),
-    "dc": (S, [128, 8], f32), "ndc": (S, [128, 8], f32), "B8th": (S, [128, 8], bf), "Bm32": (S, [128, 8], bf),
-    "TP": (S, [128, 128], bf), "uq": (S, [128, 128], bf), "c32k": (S, [128, 8], bf), "B16": (S, [128, 16], bf),
-    "dc128": (S, [128, 8], bf), "Cl": (S, [128, 8], bf), "Cd": (S, [128, 8], f32), "Ck": (S, [128, 8], f32),
-    "rh2": (S, [128, 16], bf), "cT": (S, [128, 24], f32), "oh16": (S, [128, 16], f32), "m3": (S, [128, 128], bf),
-    "KZ": (S, [128, 2048], bf), "on": (S, [128, 1024], bf), "Sel": (S, [128, 16, 128], bf), "Sel0": (S, [128, 1024], bf),
-    "TK": (S, [128, 256], bf), "RS": (S, [128, 256], f32), "xl": (S, [128, 8], u16), "x8": (S, [128, 8], u16),
+    "dc": (S, [128, 8], f32), "ndc": (S, [128, 8], f32), "B8th": (S, [128, 8], bf), "Bm32": (S, [128, 8], bf), "r8": (S, [128, 8], bf),
+    "TP": (S, [128, 256], bf), "uq": (S, [128, 128], bf), "B16": (S, [128, 24], bf),
+    "dc128": (S, [128, 16], bf), "Cl": (S, [128, 16], bf), "dc64": (S, [128, 8], bf),
+    "dcm": (S, [128, 8], bf), "oh16": (S, [128, 16], f32), "B2": (S, [128, 128], bf),
+    "oh2": (S, [128, 8], f32), "Sel2": (S, [128, 1024], bf), "nt": (S, [128, 48], bf),
+    "KZ": (S, [128, 2048], bf), "on": (S, [128, 512], bf), "Sel": (S, [128, 8, 16, 16], bf), "Sel0": (S, [128, 1024], bf),
+    "TK": (S, [128, 384], bf), "RS": (S, [128, 384], f32), "xl": (S, [128, 8], u16), "x8": (S, [128, 8], u16),
     "r1": (S, [128, NSC], bf), "r2": (S, [128, NSC], bf),
     "nn": (S, [128, 8], f32), "on32": (S, [128, 128], f32), "ib": (S, [128, 128], bf),
     "wI": (S, [128, 1], i32), "kI": (S, [128, 1], i32), "tI": (S, [128, 1], i32),
-    "Wb": (S, [128, 128], bf), "thd": (S, [128, 128], f32), "thc": (S, [128, 264], f16),
+    "Wb": (S, [128, 128], bf), "thc": (S, [128, 264], bf),
     "L1": (S, [128, 128], i32), "L2": (S, [128, 128], i32), "f1": (S, [128, 128], f32),
     "h0": (S, [128, 128], bf), "h1": (S, [128, 128], bf), "hT": (S, [128, 128], bf),
-    "nm": (S, [128, 128], f32), "pri": (S, [128, 128], f32),
-    "fr": (S, [128, 128], bf), "qh": (S, [128, 128], bf), "ql": (S, [128, 128], bf),
+    "nq": (S, [128, 256], bf), "pri": (S, [128, 128], f32),
+    "fr": (S, [128, 256], bf), "qq": (S, [128, 384], bf), "hiL": (S, [128, 128], bf),
     "i1": (S, [128, 128], i32), "i2": (S, [128, 128], i32), "i3": (S, [128, 128], i32),
     "i4": (S, [128, 128], i32), "v2": (S, [128, 128], f32),
-    "aI": (S, [128, 128], i32), "hit": (S, [128, 2048], bf), "off": (S, [128, 128], f32), "ML": (S, [128, 128], bf),
+    "aI": (S, [128, 128], i32), "hit": (S, [128, 2048], bf), "off": (S, [128, 128], f32),
     "lst": (S, [128, 128], u16), "x": (S, [128, 2048], bf),
-    "ad": (S, [128, 2048], bf), "sh": (S, [128, 2048], bf), "sl": (S, [128, 2048], bf),
-    "M0": (S, [128, 128], f32), "eq0": (S, [128, 128], bf), "N0": (S, [128, 256], f32), "n0c": (S, [128, 128], f32),
-    "sI": (S, [128, 128], i32), "sd": (S, [128, 128], bf), "vl": (S, [128, 8], u16), "vl2": (S, [128, 8], u16),
-    "x1": (S, [128, 128], bf), "x2": (S, [128, 128], bf), "An": (S, [128, 128], f32),
-    "nh": (S, [128, 128], bf), "nl": (S, [128, 128], bf), "dab": (S, [128, 1024], bf), "eq": (S, [128, 1024], bf),
-    "OV": (S, [128, 256], bf), "ME": (S, [128, 256], f32), "e8": (S, [128, 8], f32), "ov": (S, [128, 128], bf),
-    "ng": (S, [128, 128], bf), "Rb": (S, [128, 128], f32), "sg": (S, [128, 16], bf), "ks": (S, [128, 128], f32),
-    "oh": (S, [128, 128], bf), "SE": (S, [128, 128], f32), "NF": (S, [128, 128], bf), "r8": (S, [128, 8], bf),
-    "l1": (S, [128, 128], f32), "l2": (S, [128, 128], f32), "sl16": (S, [128, 8], u16), "sm": (S, [128, 16], f32),
+    "ad": (S, [128, 128, 16], bf), "sh": (S, [128, 2048], bf), "sl": (S, [128, 2048], bf),
+    "M0": (S, [128, 128], f32), "eq0": (S, [128, 128], bf), "N0": (S, [128, 256], f32),
+    "sI": (S, [128, 128], i32), "sd": (S, [128, 128], bf), "vl": (S, [128, 16], u16), "vl2": (S, [128, 8], u16),
+    "x2": (S, [128, 128], bf), "tri": (S, [128, 512], bf),
+    "tw": (S, [128, 128], bf), "nl": (S, [128, 128], bf), "dab": (S, [128, 1024], bf), "eq": (S, [128, 1024], bf),
+    "OV": (S, [128, 384], bf), "ME": (S, [128, 384], f32), "e8": (S, [128, 16], bf), "ov": (S, [128, 128], bf),
+    "ng": (S, [128, 128], bf), "sgn": (S, [128, 432], bf), "R8": (S, [128, 48], bf), "m1": (S, [128, 16], bf),
+    "lm": (S, [128, 128], bf), "Ur": (S, [128, 512], bf),
+    "l1": (S, [128, 128], f32), "l2": (S, [128, 128], f32), "sl16": (S, [128, 8], u16),
     "Ac": (S, [128, 8], f32), "rv": (S, [128, STEPS, NR, PW], u16),
-    "pn": (P, [128, 2048], f32), "pk": (P, [128, 512], f32), "p5": (P, [128, 512], f32),
+    "pn": (P, [128, 128, 16], f32), "pk": (P, [128, 512], f32), "p5": (P, [128, 512], f32),
     "p6": (P, [128, 512], f32), "p7": (P, [128, 512], f32),
 }
-SEMAPHORES = ["qg", "qv", "qs", "qt", "lsA", "lsD", "hin", "hout"] \
+SEMAPHORES = ["qg", "qv", "qs", "qt", "lsA", "lsH", "lsD", "hin", "hout"] \
     + ["ag%d_%d" % (q, j) for q in range(NR) for j in range(2)] + ["dr%d_%d" % (t, q) for t in range(STEPS) for q in range(NR)] \
     + ["rl%d" % t for t in range(STEPS)] + ["dm%d" % k for k in range(20)]
 
@@ -124,6 +136,9 @@ def rank_program(g, core, T, topo):
 
     def A(name, *idx):
         ap = T[name]
+        if name == "pn" and len(idx) == 1:
+            a, b = idx[0].start, idx[0].stop
+            idx = (slice(a // 16, b // 16),) if a % 16 == b % 16 == 0 else (a // 16, slice(a % 16, (b - 1) % 16 + 1))
         shape = [int(x) for x in ap.shape][1:]
         idx = idx + (slice(None),) * (len(shape) - len(idx))
         lo = hi = 0
@@ -156,7 +171,7 @@ def rank_program(g, core, T, topo):
         for e in log.get(v["n"], []):
             if e["lo"] < hi and lo < e["hi"]:
                 same = e["q"] == q
-                if same and (ps and q == "t" or not e["w"]):
+                if same and ps and q == "t":
                     continue
                 if apart(lo, st, e["lo"], e["st"]):
                     continue
@@ -217,7 +232,7 @@ def rank_program(g, core, T, topo):
         for v in wr:
             note(dq, v, True, tok)
 
-    ops, past, loads, early, last_hit = [], {}, [0.0], [], [0]
+    ops, past, loads, early, made, vl_at = [], {}, [0.0], [], [], []
 
     def op(q, rd, wr, busy, done, run):
         pre = {}
@@ -226,8 +241,8 @@ def rank_program(g, core, T, topo):
             for e in past.get(v["n"], []):
                 o = ops[e[4]]
                 if e[0] < hi and lo < e[1] and (e[3] or write or ps and o["q"] != q) and not apart(lo, st, e[0], e[2]):
-                    free = o["q"] == q and (ps and q == "t" or not e[3] or v["n"] == "turn" + q)
-                    pre[e[4]] = max(pre.get(e[4], 0), o["busy"] if free else o["done"] + HOP)
+                    free = o["q"] == q and (ps and q == "t" or v["n"] == "turn" + q)
+                    pre[e[4]] = max(pre.get(e[4], 0), o["busy"] if free else o["done"] + (SAME if o["q"] == q else HOP))
         for v, write in [(v, False) for v in rd] + [(v, True) for v in wr]:
             ps, lo, hi, st = spans(v)
             L = past.setdefault(v["n"], [])
@@ -275,8 +290,8 @@ def rank_program(g, core, T, topo):
     def mark(name):
         return {"n": name, "r": (0, 1, (1, 1)), "ind": None}
 
-    def E(q, meth, _pos=(), **kw):
-        wr, rd = [], []
+    def E(q, meth, _pos=(), after=(), **kw):
+        wr, rd = [], list(after)
         for k, v in list(kw.items()) + [("ap", p) for p in _pos]:
             if isinstance(v, dict):
                 (wr if k in ("out", "ap", "accum_out") else rd).append(v)
@@ -288,23 +303,26 @@ def rank_program(g, core, T, topo):
         if meth == "dma_start":
             load = out["n"] in SCRATCH
             loads[0] = loads[0] * load + 0.3 + (out if load else rd[0])["e"] / 1500
-            return op(q, rd + [mark("out%d" % (STEPS - 1))] * (not load), wr + [mark("turn" + q)], 0.06, 1.5 + loads[0], run)
+            return op(q, rd + [mark("out%d" % (STEPS - 1))] * (not load), wr + [mark("turn" + q)], 0.06,
+                      1.7 if out["n"] == "ms" else 1.5 + loads[0], run)
         n = out["e"]
         if q == "t":
-            t = max(64, n) * (2.0 if wide(rd[0]) else 0.5)
+            t = TFIX + max(min(64, rd[0]["e"]), n) * TCYC * (4 if wide(rd[0]) else 1)
         elif q == "g":
             t = 150 + 2 * n
         elif out["ind"]:
-            t = 60 + 3.5 * 16 * out["ind"]["e"]
+            t = 60 + SCA * 16 * out["ind"]["e"]
         elif any(v["ind"] for v in rd):
-            t = 60 + 1.5 * n
+            t = 60 + GAT * n
         elif q == "v" and meth == "tensor_tensor":
-            t = 30 + max(64, n * (2 if all(SCRATCH[v["n"]][0] == S for v in rd) else 1))
-        elif q == "v" and not any(wide(v) and v["e"] > 1 for v in rd + wr):
-            t = 30 + max(64, n / 2)
+            t = VFIX + max(64, n * (2 if all(SCRATCH[v["n"]][0] == S for v in rd) else 1))
+        elif q == "v" and not any(wide(v) for v in rd + wr):
+            t = VFIX + max(64, n / 2)
         else:
-            t = 30 + max(64, n)
+            t = (VFIX if q == "v" else SFIX) + max(64, n)
         op(q, rd, wr, t / 1000, t / 1000, run)
+        if q == "g":
+            behind(*vl_at)
 
     def cp(out, in_):
         E("v", "tensor_copy", out=out, in_=in_)
@@ -320,6 +338,12 @@ def rank_program(g, core, T, topo):
 
     def act(out, in_, func=F.Identity, **kw):
         E("s", "activation", out=out, in_=in_, func=func, **kw)
+
+    def times(on_v, out, in_, x):
+        if on_v:
+            ts(out, in_, x, O.mult)
+        else:
+            act(out, in_, scale=x)
 
     def mm(out, lhsT, rhs, start, stop):
         E("t", "matmul", out=out, lhsT=lhsT, rhs=rhs, start=start, stop=stop)
@@ -352,21 +376,27 @@ def rank_program(g, core, T, topo):
         op("n", [mark(name)], [v], 0.0, time, lambda: note("rem", v, True, (sem, n, {})))
 
     c = slice
-    COLS = ["pdf", "pmf", "pf", "odd", "ev8", "nbc", "key", "wf", "k8", "k4", "kq", "kq2", "nod", "n64", "o16", "tf"]
+    COLS = ["pdf", "pmf", "odd", "gq", "p8", "pf", "w0", "wq", "qb", "ev", "nbc", "key", "wf", "k8", "k4", "kq", "tf",
+            "k0", "t1", "t2", "t3", "kp"]
     K_ = lambda n: A("cols", c(COLS.index(n), COLS.index(n) + 1))
     blk = lambda n, k: A(n, c(128 * k, 128 * k + 128))
     spread = lambda n: ind(A(n, c(0, 128)), A("xl"))
     vslot = lambda s: A("W", c(VB + 128 * POS[s], VB + 128 * POS[s] + 128))
     col = lambda n, k: A(n, c(k, 128, 16))
-    sel = lambda s: A("Sel", s)
     RS = A("RS", c(0, 128))
     B, ones = A("B3", c(0, 128)), A("on", c(0, 128))
     own = A("W", c(rank * C, rank * C + C))
     H = ["h0", "h1"]
     small = {"channel_multiplier": 0, "allow_small_or_imprecise_dtypes": True}
 
+    def ad(threads, a, b=None):
+        v = A("ad", c(*threads), a if b is None else c(a, b))
+        if b is None or b - a < 16:
+            v["r"] = v["r"][:2] + ((16, 1 if b is None else b - a),)
+        return v
+
     def slots(t):
-        return [s for s in range(16) if s >= STEPS or s < t]
+        return list(range(STEPS, 16)) + list(range(t))
 
     E("y", "dma_start", out=A("ms", c(0, 512)), in_=ext("mem", c(0, 512)))
     E("s", "dma_start", out=A("ms", c(512, C)), in_=ext("mem", c(512, C)))
@@ -376,17 +406,15 @@ def rank_program(g, core, T, topo):
     E("s", "dma_start", out=A("wI"), in_=ext("w"))
     E("y", "dma_start", out=A("kI"), in_=ext("kap"))
     E("y", "dma_start", out=A("tI"), in_=ext("th"))
-    E("y", "dma_start", out=A("vv"), in_=ext("val"))
     E("g", "iota", out=A("dI"), pattern=[[-1, 128]], base=0, channel_multiplier=1)
     E("g", "iota", out=A("pI"), pattern=[[0, 1]], base=0, channel_multiplier=1)
     E("g", "iota", out=A("mI"), pattern=[[1, 128]], base=0, channel_multiplier=0)
-    E("g", "iota", out=A("RS"), pattern=[[0, 16], [32767, 16]], base=0, **small)
-    E("g", "iota", out=A("TK"), pattern=[[0, 16], [-1, 16]], base=15, **small)
-    E("g", "iota", out=A("TP"), pattern=[[0, 8], [128, 16]], base=0, **small)
+    E("g", "iota", out=A("RS"), pattern=[[0, 24], [32767, 16]], base=0, **small)
+    E("g", "iota", out=blk("TP", 1), pattern=[[0, 8], [1, 16]], base=int(SLOT) - 129, **small)
 
     cI = lambda k: A("ci1", c(k, k + 1))
-    fill(A("on", c(0, 128)), 1.0)
-    fill(A("on", c(128, 1024)), 1.0)
+    fill(A("on"), 1.0)
+    act(A("RS"), A("RS"), scale=256.0)
     ts(A("Ib"), A("dI"), 0, O.is_equal)
     ts(A("I64"), A("dI"), 0, O.is_equal, 64.0, O.mult)
     ts(A("I32"), A("dI"), 0, O.is_equal)
@@ -394,20 +422,18 @@ def rank_program(g, core, T, topo):
     ts(cI(1), A("pI"), 15, O.bitwise_and)
     ts(cI(2), A("pI"), 1, O.bitwise_and)
     ts(A("md"), A("mI"), 4, O.arith_shift_right)
-    cp(K_("pdf"), cI(0))
-    cp(K_("pmf"), cI(1))
-    cp(K_("odd"), cI(2))
+    ts(cI(3), A("pI"), 63, O.bitwise_and, 3, O.arith_shift_right)
+    ts(cI(4), A("pI"), 7, O.bitwise_and)
+    cp(A("cols", c(0, 5)), A("ci1", c(0, 5)))
     cp(K_("pf"), A("pI"))
     ts(B, A("md"), K_("pdf"), O.is_equal)
     ts(A("oh16"), A("mI", c(0, 16)), K_("pmf"), O.is_equal)
-    act(A("I8k"), A("Ib"), scale=8192.0)
-    act(A("I16k"), A("Ib"), scale=16384.0)
-    act(A("nI"), A("Ib"), scale=-1.0)
-    act(A("nI8k"), A("Ib"), scale=-8192.0)
-    act(A("nI64"), A("Ib"), scale=-64.0)
+    for n, x in (("I8k", 8192), ("I16k", 16384), ("nI", -1), ("nI8k", -8192), ("nI64", -64), ("I129", 129), ("nI129", -129),
+                 ("nI128", -128)):
+        act(A(n), A("Ib"), scale=float(x))
 
     for j, bank in enumerate(("p5", "p6")):
-        group(A(bank, c(0, 256)), [(A("I64"), A("ms", c(512 * j, 512 * j + 256))), (A("Ib"), A("ms", c(512 * j + 256, 512 * j + 512)))])
+        group(A(bank, c(0, 256)), [(A("I64"), A("ms", c(256 * j, 256 * j + 256))), (A("Ib"), A("ms", c(256 * j + 512, 256 * j + 768)))])
         ts(A("xo", c(256 * j, 256 * j + 256)), A(bank, c(0, 256)), -2048.0, O.add)
     e8 = topo.engines(core, T.cores[near[0]])
     loc = [e for e in topo.engines(core, car[0]) if e not in e8]
@@ -415,13 +441,15 @@ def rank_program(g, core, T, topo):
     def hand_out():
         g.remote_dma_fused([RemoteDMATransfer(dst_ids=[dst(topo, k, core) for k in car[2 * j:2 * j + 2]], dma_engine_mask=bits(es),
                                               remote_sem=T.sem.hin, srcs=[T.xo[:, 256 * j:256 * j + 256]], dsts=[T.hb[:], T.hb[:]])
-                            for j, es in enumerate((e8, loc))], local_sem=T.sem.lsA)
+                            for j, es in enumerate((e8, loc))], local_sem=T.sem.lsH)
         for _, j, serve in spread_plan[:2]:
             g.remote_dma_fused([RemoteDMATransfer(dst_ids=[dst(topo, T.cores[q], core) for q in serve], dma_engine_mask=bits(e8),
                                                   remote_sem=T.sem["ag%d_%d" % (rank, j)], srcs=[T.xo[:, 256 * j:256 * j + 256]],
                                                   dsts=[T.xi[:, rank, 256 * j:256 * j + 256] for q in serve])], local_sem=T.sem.lsA)
 
     send(A("xo"), "out", hand_out)
+    vl_at.append(len(ops) - 1)
+    E("y", "dma_start", out=A("vv"), in_=ext("val"))
     units = []
     for q in range(NR):
         for n, (k, j, serve) in enumerate(roles(T, topo, q)[2]):
@@ -429,178 +457,251 @@ def rank_program(g, core, T, topo):
                 units.append((LAND[n] + PACE * serve.index(rank), j, q))
                 lands(A("xi", q, c(256 * j, 256 * j + 256)), "out", "ag%d_%d" % (q, j), len(e8), units[-1][0])
     units.sort()
+    done = sorted((max(u[0] for u in units if u[2] == q), None, q) for q in range(NR) if q != rank)[:NW]
+    units = done + [u for u in units if u[2] not in [d[2] for d in done]]
     E("g", "iota", out=A("ib"), pattern=[[1, 128]], base=-128, **small)
-    E("g", "affine_select", out=A("Sel0"), in_=A("on"), pattern=[[-16, 8], [0, 128]], compare_op=O.is_ge, fill=0.0,
-      base=0, channel_multiplier=1)
-    E("g", "affine_select", out=A("Sel0"), in_=A("Sel0"), pattern=[[16, 8], [0, 128]], compare_op=O.is_ge, fill=0.0,
-      base=1, channel_multiplier=-1)
+    E("g", "iota", out=A("TK", c(0, 256)), pattern=[[0, 16], [-256, 16]], base=256 * 15, **small)
+    E("g", "iota", out=A("TK", c(256, 384)), pattern=[[0, 8], [-256, 16]], base=256 * 15 + int(128 * OFF), **small)
+    if TRI:
+        E("g", "affine_select", out=A("tri"), in_=A("on"), pattern=[[0, 4], [-1, 128]], compare_op=O.is_ge, fill=0.0,
+          base=0, channel_multiplier=1)
     E("g", "iota", out=A("r1"), pattern=[[0, NSC // 16], [256, 16]], base=0, **small)
     E("g", "iota", out=A("r2"), pattern=[[0, NSC // 16], [-256, 16]], base=256, **small)
 
     def unpack(n, j, q):
-        xi, lo = A("xi", q, c(256 * j, 256 * j + 256)), q * C + 512 * j
-        hi, ps = A("W", c(lo, lo + 256)), A("pn", c(512 * (n % 4), 512 * (n % 4) + 256))
+        a, b = (0, 512) if j is None else (256 * j, 256 * j + 256)
+        xi, hi, lo = A("xi", q, c(a, b)), A("W", c(q * C + a, q * C + b)), A("W", c(q * C + 512 + a, q * C + 512 + b))
+        ps = A(("p5", "p6", "p7", "pk")[n % 4], c(0, b - a))
         ts(hi, xi, 1.0 / 64, O.mult, OFF + 32 - 63.0 / 128, O.add)
         group(ps, [(A("Ih"), xi), (A("nI64"), hi)])
-        if n % 3 == 1 and n > 1:
-            ts(A("W", c(lo + 256, lo + 512)), ps, 2048 + 65 * OFF, O.add)
+        if n in LOV:
+            ts(lo, ps, 2048 + 65 * OFF, O.add)
         else:
-            act(A("W", c(lo + 256, lo + 512)), ps, bias=2048 + 65 * OFF)
+            act(lo, ps, bias=2048 + 65 * OFF)
 
     KEY = [1022, 1007, 1006]
-    ts(K_("key"), A("oh16", c(0, 1)), 14.0, O.mult, 1008.0, O.add)
+    act(K_("k0"), A("oh16", c(0, 1)), scale=14.0, bias=1008.0)
     cp(K_("wf"), A("wI"))
-    tt(K_("key"), K_("key"), K_("pmf"), O.subtract)
+    act(K_("key"), K_("pmf"), scale=-1.0, bias=K_("k0"))
     cp(A("f1"), A("L1"))
-    ts(A("Wb"), B, K_("wf"), O.mult)
+    act(A("Wb"), B, scale=K_("wf"))
     ts(A("l1"), A("L2"), -32.0, O.mult, K_("key"), O.add)
     tr(A("p7", c(0, 128)), A("f1"))
     tr(A("pk", c(0, 128)), A("l1"))
-    act(A("nm"), A("p7", c(0, 128)))
+    nh, nlo = blk("nq", 0), blk("nq", 1)
+    nslot = lambda s: A("nq", c(s, 256, 16))
+    first = lambda s: A("nt", c(16 * s, 16 * s + 16))
+    act(nh, A("p7", c(0, 128)), scale=1.0 / 128, bias=HI)
+    group(A("p7", c(128, 256)), [(A("f1"), A("I32")), (A("nI129"), nh)])
+    act(nlo, A("p7", c(128, 256)), bias=128 * OFF)
+    for s in range(STEPS):
+        act(first(s), nslot(s))
     act(A("pri"), A("pk", c(0, 128)))
     ts(A("xl"), A("mI", c(0, 8)), 16.0, O.mult, 15.0, O.add)
     ts(K_("k8"), A("kI"), 8.0, O.mult, 4096 * OFF, O.add)
     act(K_("k4"), K_("k8"), F.Square, scale=0.25, bias=-1024 * OFF)
-    act(K_("kq"), K_("k4"), scale=-1.0, bias=1024 + 64 * OFF - 0.25)
+    act(K_("kq"), K_("k4"), scale=-1.0, bias=-3328 + 64 * OFF - 0.25)
     act(A("Ac", c(0, 1)), K_("k4"), scale=-1.0, bias=-0.25)
-    act(K_("o16"), K_("odd"), scale=1.0 / 16)
-    act(K_("ev8"), K_("odd"), scale=-8.0, bias=8.0)
-    act(A("Ac", c(1, 2)), A("Ac", c(0, 1)), scale=K_("odd"), bias=K_("ev8"))
-    act(K_("kq2"), K_("kq"), scale=K_("odd"), bias=K_("ev8"))
-    act(K_("nod"), K_("odd"), scale=-1.0)
-    act(K_("n64"), K_("odd"), scale=-64.0)
-    ts(A("oddI"), A("Ib"), K_("odd"), O.mult)
+    act(K_("ev"), K_("odd"), scale=-1.0, bias=1.0)
+    act(A("oddI"), A("I32"), scale=K_("odd"))
     ts(A("mm"), A("mI"), 15, O.bitwise_and)
     ts(A("dc"), A("mI", c(0, 8)), K_("pdf"), O.is_equal)
     ts(A("dl"), A("mm"), K_("pmf"), O.is_equal)
-    ts(A("dc128"), A("dc"), 128.0, O.mult)
-    ts(A("Cl"), A("mI", c(0, 8)), 16.0, O.mult, K_("pmf"), O.add)
-    ts(K_("nbc"), K_("pf"), 16384.0 + DUMP, O.add)
+    for k in range(2):
+        act(A("dc128", c(8 * k, 8 * k + 8)), A("dc"), scale=128.0)
+        ts(A("Cl", c(8 * k, 8 * k + 8)), A("mI", c(0, 8)), 16.0, O.mult, K_("pmf"), O.add)
+    act(K_("nbc"), K_("pf"), bias=DUMP - 8192.0)
+    E("g", "iota", out=A("m1"), pattern=[[0, 16]], base=-1, **small)
+    for k in range(8):
+        times(k % 2, blk("Sel0", k), ones, A("dc", c(k, k + 1)))
     for s in range(16):
-        if s < 5:
-            act(sel(s), B, scale=A("oh16", c(s, s + 1)))
-        else:
-            ts(sel(s), B, A("oh16", c(s, s + 1)), O.mult)
+        times(s >= 16 - NV[0], A("Sel", c(None), s), B, A("oh16", c(s, s + 1)))
+    ts(K_("w0"), K_("pf"), 64.0, O.is_lt, 128.0, O.mult)
+    act(K_("wq"), K_("w0"), bias=1.0)
+    act(K_("qb"), K_("w0"), scale=-2.0, bias=OFF)
+    ts(A("B2"), A("md"), K_("gq"), O.is_equal)
+    ts(A("oh2"), A("mI", c(0, 8)), K_("p8"), O.is_equal, K_("wq"), O.mult)
+    for r in range(8):
+        times(r < NV[1], blk("Sel2", r), A("B2"), A("oh2", c(r, r + 1)))
 
     def twin_sums(b):
-        ps = lambda k: blk("pn", 12 + k) if b else blk("p7", k)
+        ps = lambda k: blk("p5" if b else "p7", k)
+        if TRI:
+            mm(A("p5" if b else "p7"), A("I32k"), A("tri"), True, False)
         for k in range(4):
-            mm(ps(k), blk("Sel0", 4 * b + k), A("nl"), k == 0, k == 3)
-        for k in range(4):
-            act(blk("dab", 4 * b + k), ps(k), F.Abs, bias=A("nn", c(4 * b + k, 4 * b + k + 1)))
+            mm(ps(k), blk("Sel0", 4 * b + k), A("nl"), k == 0 and not TRI, k == 3)
         half = c(512 * b, 512 * b + 512)
-        act(A("eq", half), A("dab", half), F.Relu, scale=-8192.0, bias=8192.0)
-        early.append(len(ops) - 1)
-        E("g", "affine_select", out=A("eq", half), in_=A("eq", half), pattern=[[0, 4], [1, 128]], compare_op=O.is_gt, fill=0.0,
-          base=0, channel_multiplier=-1)
+        if b < TWV:
+            for k in range(4):
+                ts(blk("eq", 4 * b + k), ps(k), A("N0", c(64 * b + 16 * k + 15, 64 * b + 16 * k + 16)), O.is_equal, 8192.0, O.mult)
+        else:
+            for k in range(4):
+                act(blk("dab", 4 * b + k), ps(k), F.Abs, bias=A("nn", c(4 * b + k, 4 * b + k + 1)))
+            act(A("eq", half), A("dab", half), F.Relu, scale=-8192.0, bias=8192.0)
+            early.append(len(ops) - 1)
+        if not TRI:
+            E("g", "affine_select", out=A("eq", half), in_=A("eq", half), pattern=[[0, 4], [1, 128]], compare_op=O.is_gt, fill=0.0,
+              base=0, channel_multiplier=-1)
+
+    hits, turns = [], []
+
+    def names(b, s=None):
+        if b:
+            act(col("fr", s), col("pri", s), F.Sign, scale=-1.0, bias=32.5)
+        else:
+            act(blk("fr", 0), A("pri"), F.Sign, scale=-1.0, bias=32.5)
+        for n, m in (("nq", "Ib"), ("fr", "I64")):
+            for k in range(2 - b):
+                mm(blk("p5", k), A(n, c(s % 2 if b else k, 256, 2)), A(m), (n, k) == ("nq", 0), (n, k) == ("fr", 1 - b))
+                behind(*made[1:])
+        act(A("qq", c(256 * b, 256 + 128 * b)), A("p5", c(0, 256 - 128 * b)), bias=K_("qb"))
 
     def prepare(t, h):
         L = slots(t)
         mm(A("p6", c(384, 512)), A("Wb"), A(h), True, True)
-        act(A("uq"), A("p6", c(384, 512)), scale=1.0 / 8192, bias=(OFF - 0.5 + 1.0 / 8192) / 2)
-        group(A("p6", c(256, 384)), [(A("Wb"), A(h)), (A("nI8k"), A("uq"))])
-        act(A("v2"), A("p6", c(256, 384)), F.Square, bias=K_("k8"))
+        if UV and t:
+            cp(A("i2"), A("p6", c(384, 512)))
+            ts(A("i3"), A("i2"), 4095, O.bitwise_and)
+            ts(A("l1"), A("i3"), K_("kp"), O.add)
+            tt(A("v2"), A("l1"), A("l1"), O.mult)
+        else:
+            act(A("uq"), A("p6", c(384, 512)), scale=1.0 / 8192, bias=(OFF - 0.5 + 1.0 / 8192) / 2)
+            group(A("p6", c(256, 384)), [(A("Wb"), A(h)), (A("nI8k"), A("uq"))])
+            act(A("v2"), A("p6", c(256, 384)), F.Square, bias=K_("k8"))
         ts(A("i1"), A("v2"), 1.0 / 16, O.mult, A("Ac", c(0, 1)), O.add)
-        ts(A("i2"), A("v2"), K_("o16"), O.mult, A("Ac", c(1, 2)), O.add)
-        ts(A("i3"), A("i2"), 3, O.arith_shift_right, 1, O.bitwise_and)
-        tt(A("i4"), A("i1"), A("i3"), O.mult)
-        act(A("fr"), A("pri"), F.Sign, scale=-1.0, bias=32.5)
-        group(A("p5", c(0, 128)), [(A("nm"), A("I32")), (A("I8k"), ones), (A("fr"), A("I8k"))])
-        act(A("qh"), A("p5", c(0, 128)))
-        tt(A("ql"), A("p5", c(0, 128)), A("qh"), O.subtract)
-        group(A("p6", c(0, 128)), [(A("oddI"), A("qh")), (A("oddI"), A("ql"))])
-        tt(A("i2"), A("i4"), A("p6", c(0, 128)), O.add)
+        ts(A("i3"), A("i1"), 3, O.arith_shift_right, 1, O.bitwise_and)
+        ts(A("p6", c(128, 256)), A("i3"), K_("ev"), O.max)
+        tt(A("i4"), A("i1"), A("p6", c(128, 256)), O.mult)
+        if t == 0:
+            names(0)
+        if t != 1:
+            mm(blk("pk", 3), A("oddI"), A("f1"), True, t == 0)
+            behind(*made[1:])
+        if t == 2:
+            for k, n in enumerate(("I129", "Ib", "nI129", "nI")):
+                mm(blk("pk", 3), blk("Ur", k), A(n), False, k == 3)
+        tt(A("i2"), A("i4"), blk("pk", 3), O.add)
         ts(A("aI"), A("i2"), 8191, O.bitwise_and)
+        if t:
+            names(1, t - 1)
         scan(A("M0"), RS, A("pri"), O.min, O.max, 0.0)
         tt(A("eq0"), spread("M0"), A("pri"), O.is_equal)
-        mm(A("pk", c(0, 128)), A("I32"), A("nm"), True, False)
-        mm(A("pk", c(128, 256)), A("Ib"), A("TP"), False, False)
-        mm(A("pk", c(0, 128)), A("I16k"), A("eq0"), False, False)
-        mm(A("pk", c(128, 256)), A("I8k"), A("eq0"), False, True)
-        scan(A("N0"), A("RS"), A("pk", c(0, 256)), O.min, O.max, 0.0)
-        act(A("n0c"), spread("N0"), bias=-16384.0)
-        tr(A("p5", c(256, 384)), A("n0c"))
-        act(A("nh"), A("p5", c(256, 384)), scale=K_("odd"))
-        tt(A("nl"), A("p5", c(256, 384)), A("nh"), O.subtract)
-        act(A("nn"), col("N0", 15), scale=-1.0, bias=16384.0)
-        act(A("An"), spread("N0"), scale=-1.0, bias=K_("nbc"))
-        act(A("x1"), spread("M0"), F.Relu, scale=-2048.0, bias=2048.0 * 33)
+        mm(A("p7", c(0, 256)), A("Ib"), A("TP"), True, False)
+        mm(A("p7", c(0, 128)), A("I129"), nh, False, False)
+        mm(A("p7", c(0, 128)), A("Ib"), nlo, False, False)
+        mm(A("p7", c(0, 128)), A("I8k"), blk("fr", 0), False, False)
+        mm(A("p7", c(0, 128)), A("I32k"), A("eq0"), False, False)
+        mm(A("p7", c(128, 256)), A("I129"), A("eq0"), False, True)
+        scan(A("N0"), A("RS", c(0, 256)), A("p7", c(0, 256)), O.min, O.max, 0.0)
+        cp(col("tw", 0), col("N0", 15))
+        tt(col("tw", 1), col("N0", 15), col("tw", 0), O.subtract)
+        act(A("nn"), col("N0", 15), scale=-1.0)
+        mm(A("p5", c(256, 384)), A("tw"), A("Ib"), True, True)
+        act(A("nl"), A("p5", c(256, 384)))
         act(A("x2"), spread("M0"), F.Relu, scale=2048.0, bias=-2048.0 * (1024 - 32 * (t + 1)))
-        tt(A("ML"), A("aI"), A("p5", c(256, 384)), O.is_equal)
         twin_sums(0)
         twin_sums(1)
         mm(A("pk", c(0, 128)), A("Ib"), A("ib"), True, False)
         for a in range(0, len(L), 4):
             four = list(enumerate(L))[a:a + 4]
             for j, s in four:
-                group(blk("pn", j % 12), [(sel(s), A("qh")), (sel(s), A("ql"))])
+                mm(blk("pn", j), blk("Sel2", s // 2), blk("qq", 2 if s == t - 1 else s % 2), True, True)
             for j, s in four:
-                tt(blk("hit", j), A("aI"), blk("pn", j % 12), O.is_equal)
+                tt(blk("hit", j), A("aI"), blk("pn", j), O.is_equal)
+                hits.append(len(ops) - 1)
                 mm(A("pk", c(0, 128)), blk("KZ", s), blk("hit", j), False, j == len(L) - 1)
-        last_hit[0] = len(ops) - 1
+
+    def lists():
         tt(A("off"), A("aI"), A("pk", c(0, 128)), O.max)
+        behind(*turns[:NR - OFFQ])
         cp(A("lst"), A("off"))
+        for k in range(4):
+            mm(A("pn", c(512 * k, 512 * k + 512)), A("hT"), A("Sel", c(2 * k, 2 * k + 2)), True, False)
+
+    diag = lambda t: A("sgn", c(144 * t, 144 * t + 128))
+    plain = lambda t: A("sgn", c(144 * t + 128, 144 * t + 136))
+    over = lambda t: A("R8", c(16 * t, 16 * t + 8))
 
     def first_terms():
-        mm(A("p6", c(0, 264)), A("Ih"), A("thc"), True, False)
-        mm(A("p6", c(0, 128)), A("Ib"), A("x1"), False, False)
+        mm(A("p6", c(0, 264)), ones, A("thc"), True, False)
+        mm(A("p6", c(128, 256)), A("Ib"), A("cq"), False, False)
         mm(A("p6", c(0, 128)), A("nI"), A("x2"), False, False)
-        mm(A("p5", c(0, 128)), A("I32"), A("An"), True, False)
+        mm(A("p5", c(0, 128)), A("nl"), A("nB3", c(0, 128)), True, False)
         mm(A("p5", c(0, 128)), A("Ib"), A("cq"), False, False)
-        mm(A("pk", c(0, 256)), A("Ib"), A("TK"), True, False)
-        mm(A("pk", c(128, 256)), A("ML"), A("I16k"), False, False)
+        act(A("hiL"), A("off"), scale=1.0 / 128, bias=HI)
+        mm(A("pk", c(0, 384)), A("Ib"), A("TK"), True, False)
+        mm(A("pk", c(256, 384)), A("off"), A("I32"), False, False)
+        mm(A("pk", c(128, 256)), A("hiL"), A("Ib"), False, False)
+        mm(A("pk", c(256, 384)), A("hiL"), A("nI128"), False, False)
 
     def reads(t, h):
         win = A("W", c(0, VD))
-        for k in range(8):
-            mm(A("pn", c(256 * k, 256 * k + 256)), A("hT"), A("Sel", c(None), c(16 * k, 16 * k + 16)), k % 2 == 0, False)
-            behind(last_hit[0])
         for a, b in zip(CUTS, CUTS[1:]):
             (act if a < NB else cp)(A("x", c(16 * a, 16 * b)), ind(win, A("lst", c(a, b))))
             if a == 0:
-                behind(*early[-2:])
+                behind(*early[len(early) - 2 + TWV:])
         fine = sorted(set(CUTS + [32, 64, 96]))
         for a, b in zip(fine, fine[1:]):
             mm(A("pn", c(16 * a, 16 * b)), A("Ib"), A("x", c(16 * a, 16 * b)), False, b % 32 == 0)
-        mm(A("p7", c(0, 128)), A("off"), A("I32"), True, False)
-        behind(len(ops) - 2)
-        for a in range(0, 2048, 512):
-            act(A("ad", c(a, a + 512)), A("pn", c(a, a + 512)), F.Abs, bias=-OFF)
-        for a in range(0, 2048, NSC):
+        for k in range(8):
+            mm(A("p5", c(16 * k, 16 * k + 16)), blk("eq", k), A("m1"), False, False)
+            behind(len(ops) - 2)
+        for threads, ks in ABS:
+            act(ad(threads, *ks), A("pn", c(*threads), c(*ks)), F.Abs, bias=-OFF)
+        for a in range(2048 - NSC, -1, -NSC):
             scan(A("sh", c(a, a + NSC)), A("r1"), A("x", c(a, a + NSC)), O.min, O.max, 0.0)
+            if a == 0:
+                behind(len(ops) - 2)
         for a in range(0, 2048, NSC):
             scan(A("sl", c(a, a + NSC)), A("r2"), A("x", c(a, a + NSC)), O.max, O.min, 256.0)
+            behind(len(ops) - 2)
         tt(A("sd"), ind(A("N0", c(128, 256)), A("xl")), A("dl"), O.mult)
         behind(len(ops) - 2)
-        group(A("pn", c(528, 536)), [(A("Ib"), A("Cl")), (A("sd"), A("B3", c(256, 264)))])
-        ts(A("vl"), A("pn", c(528, 536)), -8192.0, O.add)
-        act(A("OV", c(0, 128)), ind(A("W", c(VB, VD)), A("vl")))
+        group(A("pn", c(528, 544)), [(A("Ib"), A("Cl")), (A("sd"), A("dc128"))])
         hi, lo = A("sh", c(15, None, 16)), A("sl", c(15, None, 16))
         mm(A("p6", c(0, 264)), hi, A("nB3"), False, False)
         mm(A("p6", c(0, 264)), lo, A("B3"), False, True)
+        ranges = len(ops) - 1
         for k in range(16):
-            mm(A("pk", c(k, 256, 16)), A("ad", c(k, None, 16)), A("B16"), False, k == 15)
-        group(blk("pn", 0), [(A("Ib"), hi), (A("Ib"), lo)])
-        scan(A("ME"), A("RS"), A("pk", c(0, 256)), O.min, O.max, 0.0)
-        ts(A("ng"), A("p6", c(0, 128)), 0.0, O.is_lt, -2.0, O.mult)
-        act(A("Rb"), A("p6", c(128, 256)), scale=-1.0 / 1024, bias=16384.0)
-        act(A("OV", c(128, 256)), blk("pn", 0), scale=0.5, bias=-0.25)
+            mm(A("pk", c(k, 384, 16)), ad((0, 128), k), A("B16"), False, k == 15)
+            if k == RK:
+                behind(ranges)
+        group(blk("p7", 0), [(A("Ib"), hi), (A("Ib"), lo)])
+        scan(A("ME"), A("RS"), A("pk", c(0, 384)), O.min, O.max, 0.0)
+        ts(A("vl"), A("pn", c(528, 544)), -128 * SLOT, O.add)
+        behind(len(ops) - 2)
+        turn = {"vl": len(ops) - 1}
+        act(A("ng"), A("p6", c(0, 128)), F.Sign, bias=-0.5)
+        act(A("OV", c(256, 384)), blk("p7", 0), scale=0.5, bias=-0.25)
+        act(A("sgn", c(144 * t, 144 * t + 136)), A("p6", c(128, 264)), F.Sign, bias=-0.5, accum_out=A("Ac", c(2, 3)))
+        if YF: behind(len(ops) - 2)
         mm(A("p5", c(0, 128)), A("nI8k"), A("ng"), False, False)
         for k in range(8):
             mm(A("p5", c(16 * k, 16 * k + 16)), blk("eq", k), A("ng", c(16 * k, 16 * k + 16)), False, k == 7)
-        tt(A("e8"), A("ME", c(143, 256, 16)), col("ME", 15), O.subtract)
-        act(A("l2"), A("p5", c(0, 128)), F.Relu)
-        tt(A("ov"), ind(A("e8"), A("x8")), A("Rb"), O.is_gt)
-        group(A("pn", c(512, 520)), [(A("Ib"), A("Cl")), (A("ov"), A("dc128"))])
-        group(A("pn", c(1024, 1032)), [(A("I32"), A("Cd")), (A("l2"), A("ndc"))])
-        act(A("sg", c(0, 8)), A("p6", c(256, 264)), F.Sign)
-        act(A("ks"), A("pk", c(0, 128)))
-        cp(A("vl2"), A("pn", c(512, 520)))
-        cp(A("rv", t, rank, c(128, 136)), A("pn", c(1024, 1032)))
+        tt(A("e8"), A("ME", c(143, 384, 16)), A("ME", c(15, 256, 16)), O.subtract)
+        behind(turn["vl"])
+        turn["e8"] = len(ops) - 1
+        act(A("l2"), A("p5", c(0, 128)), F.Relu, bias=K_("nbc"))
+        act(over(t), A("e8", c(0, 8)), F.Relu, bias=-SLOT - POS[t])
+        group(blk("pn", 13), [(A("I16k"), ones), (A("nI8k"), A("eq0")), (A("I8k"), A("ng"))])
+        tt(A("ov"), ind(A("e8"), A("x8")), A("sd"), O.is_equal)
+        cp(A("OV", c(0, 256)), ind(A("W", c(VB, VD)), A("vl")))
+        behind(len(ops) - 2)
+        turn["lm"] = len(ops) - 1
+        group(A("pn", c(512, 520)), [(A("Ib"), A("Cl", c(0, 8))), (diag(t), A("dc64")), (A("ov"), A("dc128", c(0, 8)))])
+        group(A("pn", c(0, 8)), [(A("Ib"), A("Cl", c(0, 8))), (A("l2"), A("ndc"))])
+        ts(A("vl2"), A("pn", c(512, 520)), 1024.0, O.add)
+        behind(turn["lm"])
         if t < STEPS - 1:
             cp(A("rv", t, rank, c(0, 128)), ind(A("OV"), A("vl2")))
         else:
             ts(A("rv", t, rank, c(0, 128)), ind(A("OV"), A("vl2")), -OFF, O.add)
+        ts(A("rv", t, rank, c(128, 136)), A("pn", c(0, 8)), float(DUMP), O.add)
+        behind(len(ops) - 2)
+        made[:] = [len(ops) - 1, len(ops) - 4, len(ops) - 6]
+        tt(A("pri"), A("pri"), blk("pn", 13), O.min)
+        tt(A("lm"), ind(over(t), A("x8")), A("dl"), O.mult)
+        behind(made[0])
         piece = T.rv[:, t, rank, :]
 
         def pass_on():
@@ -616,118 +717,140 @@ def rank_program(g, core, T, topo):
             if q != rank:
                 lands(A("rv", t, q), "out%d" % t, "dr%d_%d" % (t, q), len(e8), (NEAR if q in near else FAR) + LAG * (NR - 1 - q))
 
-    def update(t, h, hn):
-        yb = A("OV", c(128, 256))
-        group(blk("pn", 0), [(A("Ib"), yb), (A("nI"), A(h))])
-        act(A(hn), blk("pn", 0), F.Abs, bias=-OFF)
-        tt(A("oh"), spread("ME"), A("ks"), O.is_equal)
-        mm(A("p7", c(0, 128)), A("I16k"), A("oh"), False, True)
-        act(A("ov"), A("Rb"), F.Sign, scale=-1.0, bias=16384.0)
-        ac = lambda k: A("Ac", c(k, k + 1))
-        act(A("NF"), A("ov"), F.Relu, accum_out=ac(2))
-        if t < STEPS - 1:
-            tot = A("pn", c(512, 513))
-            mm(tot, A("on32"), ac(2), True, True)
-            act(A("aq"), tot, scale=-1.0 / 64, bias=16 + OFF - 63.0 / 128)
-            act(ac(3), tot, scale=-1.0, bias=K_("kq"))
-            act(ac(4), tot, scale=K_("nod"), bias=K_("kq2"))
-            act(ac(0), A("aq"), scale=-64.0, bias=ac(3))
-            act(ac(1), A("aq"), scale=K_("n64"), bias=ac(4))
-        group(A("pn", c(1536, 1664)), [(A("I8k"), A("m3")), (A("nI8k"), A("eq0")), (A("I8k"), A("ng"))])
-        mm(A("pn", c(1024, 1032)), yb, A("B8th"), True, True)
-        act(A("r8"), A("pn", c(1024, 1032)), scale=1.0 / 32, bias=(129 - 2 * OFF - 0.4375) / 32)
-        scan(A("SE"), RS, A("p7", c(0, 128)), O.min, O.max, 0.0)
-        act(A("sg", c(8, 16)), col("SE", 15), F.Sign, scale=-1.0, bias=16384.0 + VB - 0.5)
-        tt(A("pri"), A("pri"), A("pn", c(1536, 1664)), O.min)
-        tt(A("l1"), spread("SE"), A("NF"), O.mult)
-        group(A("pn", c(512, 520)), [(A("I32"), A("Ck")), (A("NF"), A("rh2", c(0, 8))), (A("NF"), A("rh2", c(8, 16))), (A("l1"), A("dc"))])
-        sg = lambda k: A("sg", c(8 * k, 8 * k + 8))
-        new = lambda k: A("pn", c(1024 + 8 * k, 1032 + 8 * k))
-        terms = [(new(0), yb, A("Bm32")), (new(0), A("I8k"), A("r8")), (new(1), A("Ib"), A("c32k")), (new(0), A("I8k"), sg(0)),
-                 (new(1), A("I8k"), sg(0)), (new(2), A("nI8k"), sg(0)), (new(1), A("I32"), col("SE", 15)),
-                 (new(2), A("I32"), col("SE", 15)), (new(0), A("I8k"), sg(1)), (new(1), A("I8k"), sg(1)), (new(2), A("nI8k"), sg(1))]
+    def change(t, more=[]):
+        old, new = first(t), lambda k, n=1: A("pn", c(1040 + 8 * k, 1040 + 8 * (k + n)))
+        now = A("e8") if t == 1 else nslot(t)
+        terms = [(new(0, 2), A("nI"), old), (new(2, 2), A("Ib"), old), (new(0, 2), A("Ib"), now), (new(2, 2), A("nI"), now)] \
+            + [(new(k), A("I8k"), plain(t)) for k in range(4)] + [(new(k), A("nI8k"), over(t)) for k in range(4)] + more
         for k, (o, a, b) in enumerate(terms):
             mm(o, a, b, k == 0, k == len(terms) - 1)
-        tt(A("sm", c(0, 8)), A("pn", c(512, 520)), A("cT", c(8 * t, 8 * t + 8)), O.max)
-        act(col("pri", t), new(0), F.Relu, bias=KEY[t] - 32.0 * (t + 1) + 512 * OFF - 256 * 129 - 16384)
-        cp(A("sl16"), A("sm", c(0, 8)))
-        tt(A("sm", c(8, 16)), col("nm", t), new(1), O.max)
+        act(A("Ur", c(1, 512, 16)), new(0, 4), F.Relu, bias=-8192.0)
+
+    def update(t, h, hn):
+        yb = A("OV", c(256, 384))
+        group(blk("p7", 0), [(A("Ib"), yb), (A("nI"), A(h))])
+        act(A(hn), blk("p7", 0), F.Abs, bias=-OFF)
+        ac = lambda k: A("Ac", c(k, k + 1))
+        if t < STEPS - 1:
+            tot = A("pn", c(1792, 1793))
+            mm(tot, A("on32"), ac(2), True, True)
+            behind(*made[1:])
+            act(A("aq"), tot, scale=-1.0 / 256, bias=OFF - 52 - 63.0 / 128)
+            act(ac(3), tot, scale=-0.25, bias=K_("kq"))
+            act(ac(0), A("aq"), scale=-64.0, bias=ac(3))
+        mm(A("pn", c(1024, 1032)), yb, A("B8th"), True, True)
+        act(A("r8"), A("pn", c(1024, 1032)), scale=1.0 / 32, bias=(129 - 2 * OFF - 0.4375) / 32)
+        if t < STEPS - 1:
+            names(0)
+        group(A("pn", c(512, 520)), [(A("Ib"), A("Cl", c(0, 8))), (diag(t), A("dcm")), (A("lm"), A("dc128", c(0, 8)))])
+        ts(A("sl16"), A("pn", c(512, 520)), 128.0 * POS[t] - 14336, O.add)
         cp(ind(A("W", c(VB, WEND)), A("sl16")), yb)
-        tt(col("nm", t), A("sm", c(8, 16)), new(2), O.min)
+        act(nslot(t), A("e8"))
+        due = [(A("pn", c(1024, 1032)), a, b) for a, b in ((yb, A("Bm32")), (A("I8k"), plain(t)), (A("I8k"), A("r8")), (A("nI8k"), over(t)))]
+        if t == 1:
+            change(t, due)
+        else:
+            group(due[0][0], [d[1:] for d in due])
+        act(col("pri", t), A("pn", c(1024, 1032)), F.Relu, bias=KEY[t] - 32.0 * (t + 1) + 512 * OFF - 256 * 129 - 8192)
         if t < STEPS - 1:
             mm(A("pn", c(1536, 1664)), A(hn), A("nI"), True, True)
             act(A("hT"), A("pn", c(1536, 1664)))
 
     def drains(t):
+        turns[:] = range(len(ops), len(ops) + NR)
         for q in range(NR - 1, -1, -1):
             cp(ind(A("W", c(0, VB)), A("rv", t, q, c(128, 136))), A("rv", t, q, c(0, 128)))
+            if q == HITS and t < STEPS - 1:
+                behind(*hits)
 
     for s in range(16):
         act(blk("KZ", s), A("Ib"), scale=float(VB + 128 * (POS[s] + 1)))
-        if s % 2:
+        if s >= 16 - NV[2]:
             ts(vslot(s), A("vv", c(s, None, 16)), OFF, O.add)
         else:
             act(vslot(s), A("vv", c(s, None, 16)), bias=OFF)
-    fill(col("TP", 0), 128.0 * POS[0])
+    fill(A("TP", c(128, 256, 16)), SLOT - 129 + POS[0])
+    fill(blk("TP", 0), -NOFF)
+    fill(A("tw"), 0.0)
+    fill(blk("fr", 1), 0.0)
+    E("g", "iota", out=A("Ur"), pattern=[[0, 512]], base=0, **small)
+    act(A("I32k"), A("Ib"), scale=32768.0)
     ts(A("Ih"), A("dI"), 0, O.is_equal)
     ts(own, A("ms"), OFF, O.add)
     fill(A("on32"), 1.0)
     cp(K_("tf"), A("tI"))
-    ts(A("thd"), A("I32"), K_("tf"), O.mult)
-    mm(A("p6", c(0, 128)), A("on32"), A("thd"), True, True)
+    act(A("aq"), K_("tf"))
+    act(K_("t1"), A("aq"), scale=-1.0, bias=K_("tf"))
+    act(K_("t2"), A("aq"), scale=A("oh16", c(0, 1)))
+    act(K_("t3"), K_("t1"), scale=A("oh16", c(1, 2)), bias=K_("t2"))
     mm(A("p5", c(0, 128)), A(H[0]), A("nI"), True, True)
     act(A("hT"), A("p5", c(0, 128)))
-    ts(A("thc", c(0, 128)), A("p6", c(0, 128)), -0.5, O.add)
-    ts(A("thc", c(256, 264)), A("p6", c(15, 128, 16)), -0.5, O.add)
-    tt(A("thc", c(128, 256)), A("p6", c(0, 128)), A("dl"), O.mult)
     act(A("B3", c(128, 256)), B)
     act(A("B3", c(256, 264)), A("dc"))
     act(A("nB3"), A("B3"), scale=-1.0)
-    act(A("cq"), A("dl"), scale=16384.0, bias=-32768.0)
-    E("g", "iota", out=A("m3"), pattern=[[0, 128]], base=3, **small)
+    act(A("thc"), A("B3"), scale=K_("t3"))
+    act(A("cq"), A("dl"), scale=16384.0, bias=-16384.0)
     E("g", "iota", out=A("W", c(DUMP, VB)), pattern=[[0, 128]], base=0, **small)
-    act(A("B16", c(0, 8)), A("dc"), scale=16.0)
-    act(A("B16", c(8, 16)), A("dc"), scale=16.0)
+    for k in range(3):
+        act(A("B16", c(8 * k, 8 * k + 8)), A("dc"), scale=4096.0)
     cp(A("x8"), A("mI", c(0, 8)))
-    act(A("Cd"), A("Cl"), bias=float(DUMP))
-    act(A("ndc"), A("dc"), scale=-1.0)
-    act(A("B8th"), A("dc"), scale=0.125)
-    act(A("Bm32"), A("dc"), scale=-32.0)
-    E("g", "iota", out=A("c32k"), pattern=[[0, 8]], base=-32768, **small)
-    for k in range(STEPS):
-        act(A("cT", c(8 * k, 8 * k + 8)), A("Cl"), bias=128.0 * POS[k])
-    act(A("Ck"), A("Cl"), bias=float(VD - VB))
-    act(A("rh2", c(0, 8)), A("dc"), scale=-16384.0 - VD)
-    act(A("rh2", c(8, 16)), A("ndc"), scale=K_("pf"))
+    for n, x in (("ndc", -1), ("B8th", 0.125), ("Bm32", -32), ("dc64", 64), ("dcm", -1024)):
+        act(A(n), A("dc"), scale=float(x))
     prepare(0, H[0])
-    first_terms()
+    lists()
+    before = len(ops)
     for n, (_, j, q) in enumerate(units):
+        if n == LAST:
+            late_units = len(ops)
         unpack(n, j, q)
+    late_units = range(late_units, len(ops))
+    first_terms()
     for t in range(STEPS):
         h, hn = H[t % 2], H[1 - t % 2]
         reads(t, h)
+        if t == 0:
+            used = {made[0]}
+            for k in range(made[0], -1, -1):
+                if k in used:
+                    used.update(ops[k]["pre"])
+            for u in late_units:
+                for k in used:
+                    if k < before and ops[k]["q"] == ops[u]["q"]:
+                        ops[u]["pre"].setdefault(k, ops[k]["busy"])
         update(t, h, hn)
         if t < STEPS - 1:
             prepare(t + 1, hn)
-            first_terms()
         else:
             act(own, own, bias=-OFF)
             for s in range(16):
-                act(A("vv", c(s, None, 16)), vslot(s), bias=-OFF)
-            tr(A("pn", c(0, 128)), A("nm"))
+                if s % 8 < 5:
+                    ts(A("vv", c(s, None, 16)), vslot(s), -OFF, O.add)
+                else:
+                    act(A("vv", c(s, None, 16)), vslot(s), bias=-OFF)
+            E("y", "dma_start", out=ext("yh"), in_=A(hn))
+            E("y", "dma_start", out=ext("yval"), in_=A("vv"))
+            for s in (1, 0, 2):
+                if s != 1:
+                    change(s)
+                group(A("pn", c(1072, 1088)), [(A("Ib"), first(s)), (A("Ib"), A("Ur", c(1, 256, 16))),
+                                               (A("nI"), A("Ur", c(257, 512, 16)))])
+                act(nslot(s), A("pn", c(1072, 1088)))
+            group(A("pn", c(0, 128)), [(nlo, A("Ib")), (nh, A("I129"))])
             ts(A("sI"), A("pri"), -0.03125, O.mult, 32.0 - 31.0 / 64, O.add)
             ts(A("off"), A("sI"), 31.0, O.min)
             tr(A("pn", c(512, 640)), A("off"))
-            cp(A("f1"), A("pn", c(0, 128)))
+            act(A("f1"), A("pn", c(0, 128)), bias=-128 * OFF)
             cp(A("l1"), A("pn", c(512, 640)))
-            E("y", "dma_start", out=ext("ypnd"), in_=A("f1"))
-            E("y", "dma_start", out=ext("yh"), in_=A(hn))
             E("y", "dma_start", out=ext("ydue"), in_=A("l1"))
-            E("y", "dma_start", out=ext("yval"), in_=A("vv"))
+            E("y", "dma_start", out=ext("ypnd"), in_=A("f1"))
         drains(t)
+        if t < STEPS - 1:
+            lists()
+            first_terms()
     E("y", "dma_start", out=ext("ymem"), in_=own)
     issue()
-    g.wait_ge(T.sem.lsA, 3 * len(e8) + len(loc))
+    g.wait_ge(T.sem.lsA, 2 * len(e8))
+    g.wait_ge(T.sem.lsH, len(e8 + loc))
     g.wait_ge(T.sem.lsD, STEPS * (2 * len(e8) + len(loc)))
     for k in range(ndma[0]):
         if not any(seen[q].get("dm%d" % k, 0) for q in Q):

from concourse.mybir import dt, AluOpType as O, AxisListType, ActivationFunctionType as F
from concourse.bass import DstId, RemoteDMATransfer

NR, C, TH, STEPS = 8, 1024, 128, 3
DUMP = NR * C
VB = DUMP + TH
VD = VB + 16 * TH
WEND = VD + 16 * TH
PW = 136
OFF = 160.0
HI = OFF - 63.5 / 128
SLOT = OFF + VB // 128
NOFF = 128 * OFF + 24576.0
POS = [2, 1, 0] + list(range(3, 16))
NB, CUTS = 56, [0, 32, 56, 96, 128]
ABS = [((0, 32), (0, 16)), ((32, 64), (0, 16)), ((64, 128), (0, 8)), ((64, 128), (8, 12)), ((64, 128), (12, 16))]
HOP, FAR, NEAR, LAG = 0.25, 4.8, 4.0, 0.15
LAND, PACE = (7.0, 9.8, 10.3, 10.9, 10.0, 10.6), 1.0
ROUNDS, ROOM, DOUBT = 1, 0.05, 1.5
SCA, GAT = 2.5, 1.5
TFIX, TCYC = 20, 0.55
VFIX, SFIX = 40, 30
NV, LOV, NW = (8, 3, 16), (9, 11, 13), 0
LAST = 4
TRI, TWV, HITS, PL, OFFQ, YF, RK = 0, 0, 3, 0, 2, 1, -1
UV, SAME = 0, 0.25
NSC = 1024

S, P = "sbuf", "psum"
f32, bf, i32, u16, f16 = "float32", "bfloat16", "int32", "uint16", "float16"
SCRATCH = {
    "W": (S, [128, WEND], bf), "vv": (S, [128, 16 * TH], bf), "ms": (S, [128, C], bf),
    "xo": (S, [128, 512], f16), "xi": (S, [128, NR, 512], f16), "hb": (S, [128, 256], f16),
    "pI": (S, [128, 1], i32), "mI": (S, [128, 128], i32), "dI": (S, [128, 128], i32),
    "ci1": (S, [128, 8], i32), "cols": (S, [128, 24], f32), "aq": (S, [128, 1], bf), "md": (S, [128, 128], i32), "mm": (S, [128, 128], i32),
    "I32": (S, [128, 128], f32), "Ib": (S, [128, 128], bf), "nI": (S, [128, 128], bf), "Ih": (S, [128, 128], f16),
    "I64": (S, [128, 128], bf), "nI64": (S, [128, 128], bf), "oddI": (S, [128, 128], f32), "I8k": (S, [128, 128], bf),
    "nI8k": (S, [128, 128], bf), "I16k": (S, [128, 128], bf), "I32k": (S, [128, 128], bf),
    "I129": (S, [128, 128], bf), "nI129": (S, [128, 128], bf), "nI128": (S, [128, 128], bf),
    "B3": (S, [128, 264], bf), "nB3": (S, [128, 264], bf), "dl": (S, [128, 128], bf), "cq": (S, [128, 128], bf),
    "dc": (S, [128, 8], f32), "ndc": (S, [128, 8], f32), "B8th": (S, [128, 8], bf), "Bm32": (S, [128, 8], bf), "r8": (S, [128, 8], bf),
    "TP": (S, [128, 256], bf), "uq": (S, [128, 128], bf), "B16": (S, [128, 24], bf),
    "dc128": (S, [128, 16], bf), "Cl": (S, [128, 16], bf), "dc64": (S, [128, 8], bf),
    "dcm": (S, [128, 8], bf), "oh16": (S, [128, 16], f32), "B2": (S, [128, 128], bf),
    "oh2": (S, [128, 8], f32), "Sel2": (S, [128, 1024], bf), "nt": (S, [128, 48], bf),
    "KZ": (S, [128, 2048], bf), "on": (S, [128, 512], bf), "Sel": (S, [128, 8, 16, 16], bf), "Sel0": (S, [128, 1024], bf),
    "TK": (S, [128, 384], bf), "RS": (S, [128, 384], f32), "xl": (S, [128, 8], u16), "x8": (S, [128, 8], u16),
    "r1": (S, [128, NSC], bf), "r2": (S, [128, NSC], bf),
    "nn": (S, [128, 8], f32), "on32": (S, [128, 128], f32), "ib": (S, [128, 128], bf),
    "wI": (S, [128, 1], i32), "kI": (S, [128, 1], i32), "tI": (S, [128, 1], i32),
    "Wb": (S, [128, 128], bf), "thc": (S, [128, 264], bf),
    "L1": (S, [128, 128], i32), "L2": (S, [128, 128], i32), "f1": (S, [128, 128], f32),
    "h0": (S, [128, 128], bf), "h1": (S, [128, 128], bf), "hT": (S, [128, 128], bf),
    "nq": (S, [128, 256], bf), "pri": (S, [128, 128], f32),
    "fr": (S, [128, 256], bf), "qq": (S, [128, 384], bf), "hiL": (S, [128, 128], bf),
    "i1": (S, [128, 128], i32), "i2": (S, [128, 128], i32), "i3": (S, [128, 128], i32),
    "i4": (S, [128, 128], i32), "v2": (S, [128, 128], f32),
    "aI": (S, [128, 128], i32), "hit": (S, [128, 2048], bf), "off": (S, [128, 128], f32),
    "lst": (S, [128, 128], u16), "x": (S, [128, 2048], bf),
    "ad": (S, [128, 128, 16], bf), "sh": (S, [128, 2048], bf), "sl": (S, [128, 2048], bf),
    "M0": (S, [128, 128], f32), "eq0": (S, [128, 128], bf), "N0": (S, [128, 256], f32),
    "sI": (S, [128, 128], i32), "sd": (S, [128, 128], bf), "vl": (S, [128, 16], u16), "vl2": (S, [128, 8], u16),
    "x2": (S, [128, 128], bf), "tri": (S, [128, 512], bf),
    "tw": (S, [128, 128], bf), "nl": (S, [128, 128], bf), "dab": (S, [128, 1024], bf), "eq": (S, [128, 1024], bf),
    "OV": (S, [128, 384], bf), "ME": (S, [128, 384], f32), "e8": (S, [128, 16], bf), "ov": (S, [128, 128], bf),
    "ng": (S, [128, 128], bf), "sgn": (S, [128, 432], bf), "R8": (S, [128, 48], bf), "m1": (S, [128, 16], bf),
    "lm": (S, [128, 128], bf), "Ur": (S, [128, 512], bf),
    "l1": (S, [128, 128], f32), "l2": (S, [128, 128], f32), "sl16": (S, [128, 8], u16),
    "Ac": (S, [128, 8], f32), "rv": (S, [128, STEPS, NR, PW], u16),
    "pn": (P, [128, 128, 16], f32), "pk": (P, [128, 512], f32), "p5": (P, [128, 512], f32),
    "p6": (P, [128, 512], f32), "p7": (P, [128, 512], f32),
}
SEMAPHORES = ["qg", "qv", "qs", "qt", "lsA", "lsH", "lsD", "hin", "hout"] \
    + ["ag%d_%d" % (q, j) for q in range(NR) for j in range(2)] + ["dr%d_%d" % (t, q) for t in range(STEPS) for q in range(NR)] \
    + ["rl%d" % t for t in range(STEPS)] + ["dm%d" % k for k in range(20)]


def dst(topo, d, src):
    rid, pid = topo.addr(d, src)
    return DstId(rid=rid, pnc=pid)


def bits(es):
    m = 0
    for e in es:
        m |= 1 << e
    return m


def roles(T, topo, r):
    me = T.cores[r]
    near = [q for q in range(NR) if q != r and topo.may_write(me, T.cores[q])]
    far = [q for q in range(NR) if q != r and q not in near]
    car = [c for c in topo.cores_of(me) if c != me and topo.may_write(c, T.cores[far[0]])]
    car = sorted(car, key=lambda c: (topo.die(c) != topo.die(me), c))
    a = sum(q < r for q in near)
    relay = [(car[(a + b) % 2 * 2 + b // 2], [q]) for b, q in enumerate(far)][::-1]
    near, far = near[a:] + near[:a], far[a:] + far[:a]
    spread = [(me, 0, near), (me, 1, near[:2])] + [(k, j // 2, far[j % 2::2] + near[2:] * (j == 3)) for j, k in enumerate(car)]
    return near, car, spread, relay


def helper_program(g, core, T, topo):
    for r in range(NR):
        me = T.cores[r]
        if core == me or core not in topo.cores_of(me):
            continue
        near, car, spread, relay = roles(T, topo, r)
        if core not in car:
            continue
        half, serve = [(j, to) for k, j, to in spread if k == core][0]
        es = topo.engines(core, T.cores[serve[0]])
        g.wait_ge(T.sem.hin, len(es))
        g.remote_dma_fused([RemoteDMATransfer(dst_ids=[dst(topo, T.cores[q], core) for q in serve], dma_engine_mask=bits(es),
                                              remote_sem=T.sem["ag%d_%d" % (r, half)], srcs=[T.hb[:]],
                                              dsts=[T.xi[:, r, 256 * half:256 * half + 256] for q in serve])], local_sem=T.sem.hout)
        serve = dict(relay)[core]
        for t in range(STEPS):
            g.wait_ge(T.sem["rl%d" % t], len(topo.engines(me, core)))
            g.remote_dma_fused([RemoteDMATransfer(dst_ids=[dst(topo, T.cores[q], core) for q in serve], dma_engine_mask=bits(es),
                                                  remote_sem=T.sem["dr%d_%d" % (t, r)], srcs=[T.rv[:, t, r, :]],
                                                  dsts=[T.rv[:, t, r, :] for q in serve])], local_sem=T.sem.hout)
        g.wait_ge(T.sem.hout, len(es) * (1 + STEPS))


def rank_program(g, core, T, topo):
    rank = T.rank_of(core)
    if rank is None:
        helper_program(g, core, T, topo)
        return
    near, car, spread_plan, relay = roles(T, topo, rank)
    straight = sorted(near, reverse=rank >= NR // 2)

    Q = {"g": g, "v": g.vector, "s": g.scalar, "t": g.tensor, "y": g.sync}
    cnt, seen, log, ndma = {}, {q: {} for q in Q}, {}, [0]

    def A(name, *idx):
        ap = T[name]
        if name == "pn" and len(idx) == 1:
            a, b = idx[0].start, idx[0].stop
            idx = (slice(a // 16, b // 16),) if a % 16 == b % 16 == 0 else (a // 16, slice(a % 16, (b - 1) % 16 + 1))
        shape = [int(x) for x in ap.shape][1:]
        idx = idx + (slice(None),) * (len(shape) - len(idx))
        lo = hi = 0
        step = size = 1
        for n, i in zip(shape, idx):
            if isinstance(i, slice):
                a, b, st = i.indices(n)
                last = a + (b - 1 - a) // st * st
                step = st if len(shape) == 1 else 1
                size *= (b - 1 - a) // st + 1
            else:
                a = last = i
            lo, hi = lo * n + a, hi * n + last
        return {"ap": ap[(slice(None),) + idx], "n": name, "r": (lo, hi + 1, (step, 1)), "e": size, "ind": None}

    def apart(lo, st, lo2, st2):
        return st[0] == st2[0] > 1 and st2[1] <= (lo - lo2) % st[0] <= st[0] - st[1]

    def ind(win, offs):
        return {"ap": win["ap"].indirect(offs["ap"]), "n": win["n"], "r": win["r"], "e": win["e"], "ind": offs}

    def spans(v):
        lo, hi, st = v["r"]
        if v["n"] in SCRATCH and SCRATCH[v["n"]][0] == P:
            return True, lo // 512 * 512, (hi + 511) // 512 * 512, (1, 1)
        return False, lo, hi, st

    def need(q, v, write, acc):
        ps, lo, hi, st = spans(v)
        for e in log.get(v["n"], []):
            if e["lo"] < hi and lo < e["hi"]:
                same = e["q"] == q
                if same and ps and q == "t":
                    continue
                if apart(lo, st, e["lo"], e["st"]):
                    continue
                if e["w"] or write or ps and not same:
                    acc.append(e["tok"])

    def note(q, v, write, tok):
        ps, lo, hi, st = spans(v)
        L = log.setdefault(v["n"], [])
        if write and st[0] == 1:
            L[:] = [e for e in L if not (lo <= e["lo"] and e["hi"] <= hi and not ps)]
        if ps:
            L[:] = [e for e in L if not (e["q"] == q and e["w"] == write and e["lo"] == lo and e["hi"] == hi)]
        L.append({"lo": lo, "hi": hi, "st": st, "w": write, "q": q, "tok": tok})

    def settle(q, toks):
        best = {}
        for s, n, snap in toks:
            if seen[q].get(s, 0) < n and best.get(s, (0, 0))[0] < n:
                best[s] = (n, snap)
        for s in list(best):
            if any(o != s and best[o][1].get(s, 0) >= best[s][0] for o in best):
                del best[s]
        for s in best:
            n, snap = best[s]
            Q[q].wait_ge(T.sem[s], n)
            for k in snap:
                seen[q][k] = max(seen[q].get(k, 0), snap[k])
            seen[q][s] = n

    calls = {"t": {"matmul": g.tensor.matmul, "transpose": g.tensor.transpose},
             "s": {"activation": g.scalar.activation, "dma_start": g.scalar.dma_start},
             "y": {"dma_start": g.sync.dma_start}, "g": {"iota": g.iota, "affine_select": g.affine_select},
             "v": {"tensor_copy": g.vector.tensor_copy, "tensor_tensor": g.vector.tensor_tensor, "memset": g.vector.memset,
                   "tensor_scalar": g.vector.tensor_scalar, "tensor_tensor_scan": g.vector.tensor_tensor_scan}}

    def emit(q, meth, _pos, kw, rd, wr):
        toks = []
        dq = q if meth != "dma_start" else "dma"
        for v in rd:
            need(dq, v, False, toks)
        for v in wr:
            need(dq, v, True, toks)
        settle(q, toks)
        un = lambda v: v["ap"] if isinstance(v, dict) else v
        ins = calls[q][meth](*[un(p) for p in _pos], **{k: un(v) for k, v in kw.items()})
        if meth == "dma_start":
            s, n = "dm%d" % ndma[0], 16
            ndma[0] += 1
            ins.then_inc(T.sem[s], 16)
        else:
            s = "q" + q
            cnt[s] = n = cnt.get(s, 0) + 1
            ins.then_inc(T.sem[s], 1)
        tok = (s, n, dict(seen[q]))
        for v in rd:
            note(dq, v, False, tok)
        for v in wr:
            note(dq, v, True, tok)

    ops, past, loads, early, made, vl_at = [], {}, [0.0], [], [], []

    def op(q, rd, wr, busy, done, run):
        pre = {}
        for v, write in [(v, False) for v in rd] + [(v, True) for v in wr]:
            ps, lo, hi, st = spans(v)
            for e in past.get(v["n"], []):
                o = ops[e[4]]
                if e[0] < hi and lo < e[1] and (e[3] or write or ps and o["q"] != q) and not apart(lo, st, e[0], e[2]):
                    free = o["q"] == q and (ps and q == "t" or v["n"] == "turn" + q)
                    pre[e[4]] = max(pre.get(e[4], 0), o["busy"] if free else o["done"] + (SAME if o["q"] == q else HOP))
        for v, write in [(v, False) for v in rd] + [(v, True) for v in wr]:
            ps, lo, hi, st = spans(v)
            L = past.setdefault(v["n"], [])
            if write and st[0] == 1:
                L[:] = [e for e in L if not (lo <= e[0] and e[1] <= hi)]
            L.append((lo, hi, st, write, len(ops)))
        ops.append({"q": q, "pre": pre, "busy": busy, "done": done, "run": run})

    def issue():
        N = range(len(ops))
        busy = [o["busy"] for o in ops]
        fore = [o["pre"] for o in ops]
        back = [{} for o in ops]
        for k in N:
            for p, d in fore[k].items():
                back[p][k] = d + busy[k] - busy[p] + (DOUBT if ops[p]["q"] == "n" or p in early else 0.0)

        def place(order, pre, least):
            at, used = {}, {}
            for k in order:
                t = max([least[k]] + [at[p] + d for p, d in pre[k].items()])
                L = used.setdefault(ops[k]["q"], [])
                if busy[k]:
                    j = 0
                    while j < len(L) and L[j][0] < t + busy[k] - ROOM:
                        t = max(t, L[j][1])
                        j += 1
                    L.insert(j, (t, t + busy[k]))
                at[k] = t
            return at

        est = {}
        for k in N:
            est[k] = max([0.0] + [est[p] + d for p, d in fore[k].items()])
        for _ in range(ROUNDS):
            late = place(sorted(N, key=lambda k: (-est[k], -k)), back, [ops[k]["done"] - busy[k] for k in N])
            est = place(sorted(N, key=lambda k: (-late[k] - busy[k], k)), fore, [0.0] * len(ops))
        for k in sorted(N, key=lambda k: (est[k], k)):
            ops[k]["run"]()

    def behind(*ks):
        for k in ks:
            ops[-1]["pre"][k] = max(ops[-1]["pre"].get(k, 0.0), ops[k]["busy"])

    def mark(name):
        return {"n": name, "r": (0, 1, (1, 1)), "ind": None}

    def E(q, meth, _pos=(), after=(), **kw):
        wr, rd = [], list(after)
        for k, v in list(kw.items()) + [("ap", p) for p in _pos]:
            if isinstance(v, dict):
                (wr if k in ("out", "ap", "accum_out") else rd).append(v)
                if v["ind"]:
                    rd.append(v["ind"])
        run = lambda: emit(q, meth, _pos, kw, rd, wr)
        out = wr[0]
        wide = lambda v: SCRATCH[v["n"]][2] in (f32, i32)
        if meth == "dma_start":
            load = out["n"] in SCRATCH
            loads[0] = loads[0] * load + 0.3 + (out if load else rd[0])["e"] / 1500
            return op(q, rd + [mark("out%d" % (STEPS - 1))] * (not load), wr + [mark("turn" + q)], 0.06,
                      1.7 if out["n"] == "ms" else 1.5 + loads[0], run)
        n = out["e"]
        if q == "t":
            t = TFIX + max(min(64, rd[0]["e"]), n) * TCYC * (4 if wide(rd[0]) else 1)
        elif q == "g":
            t = 150 + 2 * n
        elif out["ind"]:
            t = 60 + SCA * 16 * out["ind"]["e"]
        elif any(v["ind"] for v in rd):
            t = 60 + GAT * n
        elif q == "v" and meth == "tensor_tensor":
            t = VFIX + max(64, n * (2 if all(SCRATCH[v["n"]][0] == S for v in rd) else 1))
        elif q == "v" and not any(wide(v) for v in rd + wr):
            t = VFIX + max(64, n / 2)
        else:
            t = (VFIX if q == "v" else SFIX) + max(64, n)
        op(q, rd, wr, t / 1000, t / 1000, run)
        if q == "g":
            behind(*vl_at)

    def cp(out, in_):
        E("v", "tensor_copy", out=out, in_=in_)

    def tt(out, a, b, op):
        E("v", "tensor_tensor", out=out, in0=a, in1=b, op=op)

    def ts(out, a, s1, op0, s2=None, op1=None):
        if op1 is None:
            E("v", "tensor_scalar", out=out, in0=a, scalar1=s1, scalar2=None, op0=op0)
        else:
            E("v", "tensor_scalar", out=out, in0=a, scalar1=s1, scalar2=s2, op0=op0, op1=op1)

    def act(out, in_, func=F.Identity, **kw):
        E("s", "activation", out=out, in_=in_, func=func, **kw)

    def times(on_v, out, in_, x):
        if on_v:
            ts(out, in_, x, O.mult)
        else:
            act(out, in_, scale=x)

    def mm(out, lhsT, rhs, start, stop):
        E("t", "matmul", out=out, lhsT=lhsT, rhs=rhs, start=start, stop=stop)

    def tr(out, in_):
        E("t", "transpose", out=out, in_=in_, identity=A("I32"))

    def group(out, pairs):
        for k, (a, b) in enumerate(pairs):
            mm(out, a, b, k == 0, k == len(pairs) - 1)

    def scan(out, d0, d1, op0, op1, init):
        E("v", "tensor_tensor_scan", out=out, data0=d0, data1=d1, initial=init, op0=op0, op1=op1)

    def fill(v, x):
        E("v", "memset", (v, x))

    def ext(name, *idx):
        return {"ap": T[name][(slice(None),) + idx], "n": name + str(idx), "r": (0, 1, (1, 1)), "ind": None}

    def send(v, name, run):
        def go():
            toks = []
            need("g", v, False, toks)
            settle("g", toks)
            run()
        op("g", [v], [mark(name)], 2.0, 0.0, go)

    def lands(v, name, sem, n, time):
        op("n", [mark(name)], [v], 0.0, time, lambda: note("rem", v, True, (sem, n, {})))

    c = slice
    COLS = ["pdf", "pmf", "odd", "gq", "p8", "pf", "w0", "wq", "qb", "ev", "nbc", "key", "wf", "k8", "k4", "kq", "tf",
            "k0", "t1", "t2", "t3", "kp"]
    K_ = lambda n: A("cols", c(COLS.index(n), COLS.index(n) + 1))
    blk = lambda n, k: A(n, c(128 * k, 128 * k + 128))
    spread = lambda n: ind(A(n, c(0, 128)), A("xl"))
    vslot = lambda s: A("W", c(VB + 128 * POS[s], VB + 128 * POS[s] + 128))
    col = lambda n, k: A(n, c(k, 128, 16))
    RS = A("RS", c(0, 128))
    B, ones = A("B3", c(0, 128)), A("on", c(0, 128))
    own = A("W", c(rank * C, rank * C + C))
    H = ["h0", "h1"]
    small = {"channel_multiplier": 0, "allow_small_or_imprecise_dtypes": True}

    def ad(threads, a, b=None):
        v = A("ad", c(*threads), a if b is None else c(a, b))
        if b is None or b - a < 16:
            v["r"] = v["r"][:2] + ((16, 1 if b is None else b - a),)
        return v

    def slots(t):
        return list(range(STEPS, 16)) + list(range(t))

    E("y", "dma_start", out=A("ms", c(0, 512)), in_=ext("mem", c(0, 512)))
    E("s", "dma_start", out=A("ms", c(512, C)), in_=ext("mem", c(512, C)))
    E("y", "dma_start", out=A("L1"), in_=ext("pnd"))
    E("s", "dma_start", out=A("L2"), in_=ext("due"))
    E("y", "dma_start", out=A("h0"), in_=ext("h"))
    E("s", "dma_start", out=A("wI"), in_=ext("w"))
    E("y", "dma_start", out=A("kI"), in_=ext("kap"))
    E("y", "dma_start", out=A("tI"), in_=ext("th"))
    E("g", "iota", out=A("dI"), pattern=[[-1, 128]], base=0, channel_multiplier=1)
    E("g", "iota", out=A("pI"), pattern=[[0, 1]], base=0, channel_multiplier=1)
    E("g", "iota", out=A("mI"), pattern=[[1, 128]], base=0, channel_multiplier=0)
    E("g", "iota", out=A("RS"), pattern=[[0, 24], [32767, 16]], base=0, **small)
    E("g", "iota", out=blk("TP", 1), pattern=[[0, 8], [1, 16]], base=int(SLOT) - 129, **small)

    cI = lambda k: A("ci1", c(k, k + 1))
    fill(A("on"), 1.0)
    act(A("RS"), A("RS"), scale=256.0)
    ts(A("Ib"), A("dI"), 0, O.is_equal)
    ts(A("I64"), A("dI"), 0, O.is_equal, 64.0, O.mult)
    ts(A("I32"), A("dI"), 0, O.is_equal)
    ts(cI(0), A("pI"), 4, O.arith_shift_right)
    ts(cI(1), A("pI"), 15, O.bitwise_and)
    ts(cI(2), A("pI"), 1, O.bitwise_and)
    ts(A("md"), A("mI"), 4, O.arith_shift_right)
    ts(cI(3), A("pI"), 63, O.bitwise_and, 3, O.arith_shift_right)
    ts(cI(4), A("pI"), 7, O.bitwise_and)
    cp(A("cols", c(0, 5)), A("ci1", c(0, 5)))
    cp(K_("pf"), A("pI"))
    ts(B, A("md"), K_("pdf"), O.is_equal)
    ts(A("oh16"), A("mI", c(0, 16)), K_("pmf"), O.is_equal)
    for n, x in (("I8k", 8192), ("I16k", 16384), ("nI", -1), ("nI8k", -8192), ("nI64", -64), ("I129", 129), ("nI129", -129),
                 ("nI128", -128)):
        act(A(n), A("Ib"), scale=float(x))

    for j, bank in enumerate(("p5", "p6")):
        group(A(bank, c(0, 256)), [(A("I64"), A("ms", c(256 * j, 256 * j + 256))), (A("Ib"), A("ms", c(256 * j + 512, 256 * j + 768)))])
        ts(A("xo", c(256 * j, 256 * j + 256)), A(bank, c(0, 256)), -2048.0, O.add)
    e8 = topo.engines(core, T.cores[near[0]])
    loc = [e for e in topo.engines(core, car[0]) if e not in e8]

    def hand_out():
        g.remote_dma_fused([RemoteDMATransfer(dst_ids=[dst(topo, k, core) for k in car[2 * j:2 * j + 2]], dma_engine_mask=bits(es),
                                              remote_sem=T.sem.hin, srcs=[T.xo[:, 256 * j:256 * j + 256]], dsts=[T.hb[:], T.hb[:]])
                            for j, es in enumerate((e8, loc))], local_sem=T.sem.lsH)
        for _, j, serve in spread_plan[:2]:
            g.remote_dma_fused([RemoteDMATransfer(dst_ids=[dst(topo, T.cores[q], core) for q in serve], dma_engine_mask=bits(e8),
                                                  remote_sem=T.sem["ag%d_%d" % (rank, j)], srcs=[T.xo[:, 256 * j:256 * j + 256]],
                                                  dsts=[T.xi[:, rank, 256 * j:256 * j + 256] for q in serve])], local_sem=T.sem.lsA)

    send(A("xo"), "out", hand_out)
    vl_at.append(len(ops) - 1)
    E("y", "dma_start", out=A("vv"), in_=ext("val"))
    units = []
    for q in range(NR):
        for n, (k, j, serve) in enumerate(roles(T, topo, q)[2]):
            if rank in serve:
                units.append((LAND[n] + PACE * serve.index(rank), j, q))
                lands(A("xi", q, c(256 * j, 256 * j + 256)), "out", "ag%d_%d" % (q, j), len(e8), units[-1][0])
    units.sort()
    done = sorted((max(u[0] for u in units if u[2] == q), None, q) for q in range(NR) if q != rank)[:NW]
    units = done + [u for u in units if u[2] not in [d[2] for d in done]]
    E("g", "iota", out=A("ib"), pattern=[[1, 128]], base=-128, **small)
    E("g", "iota", out=A("TK", c(0, 256)), pattern=[[0, 16], [-256, 16]], base=256 * 15, **small)
    E("g", "iota", out=A("TK", c(256, 384)), pattern=[[0, 8], [-256, 16]], base=256 * 15 + int(128 * OFF), **small)
    if TRI:
        E("g", "affine_select", out=A("tri"), in_=A("on"), pattern=[[0, 4], [-1, 128]], compare_op=O.is_ge, fill=0.0,
          base=0, channel_multiplier=1)
    E("g", "iota", out=A("r1"), pattern=[[0, NSC // 16], [256, 16]], base=0, **small)
    E("g", "iota", out=A("r2"), pattern=[[0, NSC // 16], [-256, 16]], base=256, **small)

    def unpack(n, j, q):
        a, b = (0, 512) if j is None else (256 * j, 256 * j + 256)
        xi, hi, lo = A("xi", q, c(a, b)), A("W", c(q * C + a, q * C + b)), A("W", c(q * C + 512 + a, q * C + 512 + b))
        ps = A(("p5", "p6", "p7", "pk")[n % 4], c(0, b - a))
        ts(hi, xi, 1.0 / 64, O.mult, OFF + 32 - 63.0 / 128, O.add)
        group(ps, [(A("Ih"), xi), (A("nI64"), hi)])
        if n in LOV:
            ts(lo, ps, 2048 + 65 * OFF, O.add)
        else:
            act(lo, ps, bias=2048 + 65 * OFF)

    KEY = [1022, 1007, 1006]
    act(K_("k0"), A("oh16", c(0, 1)), scale=14.0, bias=1008.0)
    cp(K_("wf"), A("wI"))
    act(K_("key"), K_("pmf"), scale=-1.0, bias=K_("k0"))
    cp(A("f1"), A("L1"))
    act(A("Wb"), B, scale=K_("wf"))
    ts(A("l1"), A("L2"), -32.0, O.mult, K_("key"), O.add)
    tr(A("p7", c(0, 128)), A("f1"))
    tr(A("pk", c(0, 128)), A("l1"))
    nh, nlo = blk("nq", 0), blk("nq", 1)
    nslot = lambda s: A("nq", c(s, 256, 16))
    first = lambda s: A("nt", c(16 * s, 16 * s + 16))
    act(nh, A("p7", c(0, 128)), scale=1.0 / 128, bias=HI)
    group(A("p7", c(128, 256)), [(A("f1"), A("I32")), (A("nI129"), nh)])
    act(nlo, A("p7", c(128, 256)), bias=128 * OFF)
    for s in range(STEPS):
        act(first(s), nslot(s))
    act(A("pri"), A("pk", c(0, 128)))
    ts(A("xl"), A("mI", c(0, 8)), 16.0, O.mult, 15.0, O.add)
    ts(K_("k8"), A("kI"), 8.0, O.mult, 4096 * OFF, O.add)
    act(K_("k4"), K_("k8"), F.Square, scale=0.25, bias=-1024 * OFF)
    act(K_("kq"), K_("k4"), scale=-1.0, bias=-3328 + 64 * OFF - 0.25)
    act(A("Ac", c(0, 1)), K_("k4"), scale=-1.0, bias=-0.25)
    act(K_("ev"), K_("odd"), scale=-1.0, bias=1.0)
    act(A("oddI"), A("I32"), scale=K_("odd"))
    ts(A("mm"), A("mI"), 15, O.bitwise_and)
    ts(A("dc"), A("mI", c(0, 8)), K_("pdf"), O.is_equal)
    ts(A("dl"), A("mm"), K_("pmf"), O.is_equal)
    for k in range(2):
        act(A("dc128", c(8 * k, 8 * k + 8)), A("dc"), scale=128.0)
        ts(A("Cl", c(8 * k, 8 * k + 8)), A("mI", c(0, 8)), 16.0, O.mult, K_("pmf"), O.add)
    act(K_("nbc"), K_("pf"), bias=DUMP - 8192.0)
    E("g", "iota", out=A("m1"), pattern=[[0, 16]], base=-1, **small)
    for k in range(8):
        times(k % 2, blk("Sel0", k), ones, A("dc", c(k, k + 1)))
    for s in range(16):
        times(s >= 16 - NV[0], A("Sel", c(None), s), B, A("oh16", c(s, s + 1)))
    ts(K_("w0"), K_("pf"), 64.0, O.is_lt, 128.0, O.mult)
    act(K_("wq"), K_("w0"), bias=1.0)
    act(K_("qb"), K_("w0"), scale=-2.0, bias=OFF)
    ts(A("B2"), A("md"), K_("gq"), O.is_equal)
    ts(A("oh2"), A("mI", c(0, 8)), K_("p8"), O.is_equal, K_("wq"), O.mult)
    for r in range(8):
        times(r < NV[1], blk("Sel2", r), A("B2"), A("oh2", c(r, r + 1)))

    def twin_sums(b):
        ps = lambda k: blk("p5" if b else "p7", k)
        if TRI:
            mm(A("p5" if b else "p7"), A("I32k"), A("tri"), True, False)
        for k in range(4):
            mm(ps(k), blk("Sel0", 4 * b + k), A("nl"), k == 0 and not TRI, k == 3)
        half = c(512 * b, 512 * b + 512)
        if b < TWV:
            for k in range(4):
                ts(blk("eq", 4 * b + k), ps(k), A("N0", c(64 * b + 16 * k + 15, 64 * b + 16 * k + 16)), O.is_equal, 8192.0, O.mult)
        else:
            for k in range(4):
                act(blk("dab", 4 * b + k), ps(k), F.Abs, bias=A("nn", c(4 * b + k, 4 * b + k + 1)))
            act(A("eq", half), A("dab", half), F.Relu, scale=-8192.0, bias=8192.0)
            early.append(len(ops) - 1)
        if not TRI:
            E("g", "affine_select", out=A("eq", half), in_=A("eq", half), pattern=[[0, 4], [1, 128]], compare_op=O.is_gt, fill=0.0,
              base=0, channel_multiplier=-1)

    hits, turns = [], []

    def names(b, s=None):
        if b:
            act(col("fr", s), col("pri", s), F.Sign, scale=-1.0, bias=32.5)
        else:
            act(blk("fr", 0), A("pri"), F.Sign, scale=-1.0, bias=32.5)
        for n, m in (("nq", "Ib"), ("fr", "I64")):
            for k in range(2 - b):
                mm(blk("p5", k), A(n, c(s % 2 if b else k, 256, 2)), A(m), (n, k) == ("nq", 0), (n, k) == ("fr", 1 - b))
                behind(*made[1:])
        act(A("qq", c(256 * b, 256 + 128 * b)), A("p5", c(0, 256 - 128 * b)), bias=K_("qb"))

    def prepare(t, h):
        L = slots(t)
        mm(A("p6", c(384, 512)), A("Wb"), A(h), True, True)
        if UV and t:
            cp(A("i2"), A("p6", c(384, 512)))
            ts(A("i3"), A("i2"), 4095, O.bitwise_and)
            ts(A("l1"), A("i3"), K_("kp"), O.add)
            tt(A("v2"), A("l1"), A("l1"), O.mult)
        else:
            act(A("uq"), A("p6", c(384, 512)), scale=1.0 / 8192, bias=(OFF - 0.5 + 1.0 / 8192) / 2)
            group(A("p6", c(256, 384)), [(A("Wb"), A(h)), (A("nI8k"), A("uq"))])
            act(A("v2"), A("p6", c(256, 384)), F.Square, bias=K_("k8"))
        ts(A("i1"), A("v2"), 1.0 / 16, O.mult, A("Ac", c(0, 1)), O.add)
        ts(A("i3"), A("i1"), 3, O.arith_shift_right, 1, O.bitwise_and)
        ts(A("p6", c(128, 256)), A("i3"), K_("ev"), O.max)
        tt(A("i4"), A("i1"), A("p6", c(128, 256)), O.mult)
        if t == 0:
            names(0)
        if t != 1:
            mm(blk("pk", 3), A("oddI"), A("f1"), True, t == 0)
            behind(*made[1:])
        if t == 2:
            for k, n in enumerate(("I129", "Ib", "nI129", "nI")):
                mm(blk("pk", 3), blk("Ur", k), A(n), False, k == 3)
        tt(A("i2"), A("i4"), blk("pk", 3), O.add)
        ts(A("aI"), A("i2"), 8191, O.bitwise_and)
        if t:
            names(1, t - 1)
        scan(A("M0"), RS, A("pri"), O.min, O.max, 0.0)
        tt(A("eq0"), spread("M0"), A("pri"), O.is_equal)
        mm(A("p7", c(0, 256)), A("Ib"), A("TP"), True, False)
        mm(A("p7", c(0, 128)), A("I129"), nh, False, False)
        mm(A("p7", c(0, 128)), A("Ib"), nlo, False, False)
        mm(A("p7", c(0, 128)), A("I8k"), blk("fr", 0), False, False)
        mm(A("p7", c(0, 128)), A("I32k"), A("eq0"), False, False)
        mm(A("p7", c(128, 256)), A("I129"), A("eq0"), False, True)
        scan(A("N0"), A("RS", c(0, 256)), A("p7", c(0, 256)), O.min, O.max, 0.0)
        cp(col("tw", 0), col("N0", 15))
        tt(col("tw", 1), col("N0", 15), col("tw", 0), O.subtract)
        act(A("nn"), col("N0", 15), scale=-1.0)
        mm(A("p5", c(256, 384)), A("tw"), A("Ib"), True, True)
        act(A("nl"), A("p5", c(256, 384)))
        act(A("x2"), spread("M0"), F.Relu, scale=2048.0, bias=-2048.0 * (1024 - 32 * (t + 1)))
        twin_sums(0)
        twin_sums(1)
        mm(A("pk", c(0, 128)), A("Ib"), A("ib"), True, False)
        for a in range(0, len(L), 4):
            four = list(enumerate(L))[a:a + 4]
            for j, s in four:
                mm(blk("pn", j), blk("Sel2", s // 2), blk("qq", 2 if s == t - 1 else s % 2), True, True)
            for j, s in four:
                tt(blk("hit", j), A("aI"), blk("pn", j), O.is_equal)
                hits.append(len(ops) - 1)
                mm(A("pk", c(0, 128)), blk("KZ", s), blk("hit", j), False, j == len(L) - 1)

    def lists():
        tt(A("off"), A("aI"), A("pk", c(0, 128)), O.max)
        behind(*turns[:NR - OFFQ])
        cp(A("lst"), A("off"))
        for k in range(4):
            mm(A("pn", c(512 * k, 512 * k + 512)), A("hT"), A("Sel", c(2 * k, 2 * k + 2)), True, False)

    diag = lambda t: A("sgn", c(144 * t, 144 * t + 128))
    plain = lambda t: A("sgn", c(144 * t + 128, 144 * t + 136))
    over = lambda t: A("R8", c(16 * t, 16 * t + 8))

    def first_terms():
        mm(A("p6", c(0, 264)), ones, A("thc"), True, False)
        mm(A("p6", c(128, 256)), A("Ib"), A("cq"), False, False)
        mm(A("p6", c(0, 128)), A("nI"), A("x2"), False, False)
        mm(A("p5", c(0, 128)), A("nl"), A("nB3", c(0, 128)), True, False)
        mm(A("p5", c(0, 128)), A("Ib"), A("cq"), False, False)
        act(A("hiL"), A("off"), scale=1.0 / 128, bias=HI)
        mm(A("pk", c(0, 384)), A("Ib"), A("TK"), True, False)
        mm(A("pk", c(256, 384)), A("off"), A("I32"), False, False)
        mm(A("pk", c(128, 256)), A("hiL"), A("Ib"), False, False)
        mm(A("pk", c(256, 384)), A("hiL"), A("nI128"), False, False)

    def reads(t, h):
        win = A("W", c(0, VD))
        for a, b in zip(CUTS, CUTS[1:]):
            (act if a < NB else cp)(A("x", c(16 * a, 16 * b)), ind(win, A("lst", c(a, b))))
            if a == 0:
                behind(*early[len(early) - 2 + TWV:])
        fine = sorted(set(CUTS + [32, 64, 96]))
        for a, b in zip(fine, fine[1:]):
            mm(A("pn", c(16 * a, 16 * b)), A("Ib"), A("x", c(16 * a, 16 * b)), False, b % 32 == 0)
        for k in range(8):
            mm(A("p5", c(16 * k, 16 * k + 16)), blk("eq", k), A("m1"), False, False)
            behind(len(ops) - 2)
        for threads, ks in ABS:
            act(ad(threads, *ks), A("pn", c(*threads), c(*ks)), F.Abs, bias=-OFF)
        for a in range(2048 - NSC, -1, -NSC):
            scan(A("sh", c(a, a + NSC)), A("r1"), A("x", c(a, a + NSC)), O.min, O.max, 0.0)
            if a == 0:
                behind(len(ops) - 2)
        for a in range(0, 2048, NSC):
            scan(A("sl", c(a, a + NSC)), A("r2"), A("x", c(a, a + NSC)), O.max, O.min, 256.0)
            behind(len(ops) - 2)
        tt(A("sd"), ind(A("N0", c(128, 256)), A("xl")), A("dl"), O.mult)
        behind(len(ops) - 2)
        group(A("pn", c(528, 544)), [(A("Ib"), A("Cl")), (A("sd"), A("dc128"))])
        hi, lo = A("sh", c(15, None, 16)), A("sl", c(15, None, 16))
        mm(A("p6", c(0, 264)), hi, A("nB3"), False, False)
        mm(A("p6", c(0, 264)), lo, A("B3"), False, True)
        ranges = len(ops) - 1
        for k in range(16):
            mm(A("pk", c(k, 384, 16)), ad((0, 128), k), A("B16"), False, k == 15)
            if k == RK:
                behind(ranges)
        group(blk("p7", 0), [(A("Ib"), hi), (A("Ib"), lo)])
        scan(A("ME"), A("RS"), A("pk", c(0, 384)), O.min, O.max, 0.0)
        ts(A("vl"), A("pn", c(528, 544)), -128 * SLOT, O.add)
        behind(len(ops) - 2)
        turn = {"vl": len(ops) - 1}
        act(A("ng"), A("p6", c(0, 128)), F.Sign, bias=-0.5)
        act(A("OV", c(256, 384)), blk("p7", 0), scale=0.5, bias=-0.25)
        act(A("sgn", c(144 * t, 144 * t + 136)), A("p6", c(128, 264)), F.Sign, bias=-0.5, accum_out=A("Ac", c(2, 3)))
        if YF: behind(len(ops) - 2)
        mm(A("p5", c(0, 128)), A("nI8k"), A("ng"), False, False)
        for k in range(8):
            mm(A("p5", c(16 * k, 16 * k + 16)), blk("eq", k), A("ng", c(16 * k, 16 * k + 16)), False, k == 7)
        tt(A("e8"), A("ME", c(143, 384, 16)), A("ME", c(15, 256, 16)), O.subtract)
        behind(turn["vl"])
        turn["e8"] = len(ops) - 1
        act(A("l2"), A("p5", c(0, 128)), F.Relu, bias=K_("nbc"))
        act(over(t), A("e8", c(0, 8)), F.Relu, bias=-SLOT - POS[t])
        group(blk("pn", 13), [(A("I16k"), ones), (A("nI8k"), A("eq0")), (A("I8k"), A("ng"))])
        tt(A("ov"), ind(A("e8"), A("x8")), A("sd"), O.is_equal)
        cp(A("OV", c(0, 256)), ind(A("W", c(VB, VD)), A("vl")))
        behind(len(ops) - 2)
        turn["lm"] = len(ops) - 1
        group(A("pn", c(512, 520)), [(A("Ib"), A("Cl", c(0, 8))), (diag(t), A("dc64")), (A("ov"), A("dc128", c(0, 8)))])
        group(A("pn", c(0, 8)), [(A("Ib"), A("Cl", c(0, 8))), (A("l2"), A("ndc"))])
        ts(A("vl2"), A("pn", c(512, 520)), 1024.0, O.add)
        behind(turn["lm"])
        if t < STEPS - 1:
            cp(A("rv", t, rank, c(0, 128)), ind(A("OV"), A("vl2")))
        else:
            ts(A("rv", t, rank, c(0, 128)), ind(A("OV"), A("vl2")), -OFF, O.add)
        ts(A("rv", t, rank, c(128, 136)), A("pn", c(0, 8)), float(DUMP), O.add)
        behind(len(ops) - 2)
        made[:] = [len(ops) - 1, len(ops) - 4, len(ops) - 6]
        tt(A("pri"), A("pri"), blk("pn", 13), O.min)
        tt(A("lm"), ind(over(t), A("x8")), A("dl"), O.mult)
        behind(made[0])
        piece = T.rv[:, t, rank, :]

        def pass_on():
            g.remote_dma_fused([RemoteDMATransfer(dst_ids=[dst(topo, k, core) for k, _ in relay], dma_engine_mask=bits(e8 + loc),
                                                  remote_sem=T.sem["rl%d" % t], srcs=[piece], dsts=[piece for k in relay])],
                               local_sem=T.sem.lsD)
            g.remote_dma_fused([RemoteDMATransfer(dst_ids=[dst(topo, T.cores[q], core) for q in straight], dma_engine_mask=bits(e8),
                                                  remote_sem=T.sem["dr%d_%d" % (t, rank)], srcs=[piece], dsts=[piece for q in straight])],
                               local_sem=T.sem.lsD)

        send(A("rv", t, rank), "out%d" % t, pass_on)
        for q in range(NR):
            if q != rank:
                lands(A("rv", t, q), "out%d" % t, "dr%d_%d" % (t, q), len(e8), (NEAR if q in near else FAR) + LAG * (NR - 1 - q))

    def change(t, more=[]):
        old, new = first(t), lambda k, n=1: A("pn", c(1040 + 8 * k, 1040 + 8 * (k + n)))
        now = A("e8") if t == 1 else nslot(t)
        terms = [(new(0, 2), A("nI"), old), (new(2, 2), A("Ib"), old), (new(0, 2), A("Ib"), now), (new(2, 2), A("nI"), now)] \
            + [(new(k), A("I8k"), plain(t)) for k in range(4)] + [(new(k), A("nI8k"), over(t)) for k in range(4)] + more
        for k, (o, a, b) in enumerate(terms):
            mm(o, a, b, k == 0, k == len(terms) - 1)
        act(A("Ur", c(1, 512, 16)), new(0, 4), F.Relu, bias=-8192.0)

    def update(t, h, hn):
        yb = A("OV", c(256, 384))
        group(blk("p7", 0), [(A("Ib"), yb), (A("nI"), A(h))])
        act(A(hn), blk("p7", 0), F.Abs, bias=-OFF)
        ac = lambda k: A("Ac", c(k, k + 1))
        if t < STEPS - 1:
            tot = A("pn", c(1792, 1793))
            mm(tot, A("on32"), ac(2), True, True)
            behind(*made[1:])
            act(A("aq"), tot, scale=-1.0 / 256, bias=OFF - 52 - 63.0 / 128)
            act(ac(3), tot, scale=-0.25, bias=K_("kq"))
            act(ac(0), A("aq"), scale=-64.0, bias=ac(3))
        mm(A("pn", c(1024, 1032)), yb, A("B8th"), True, True)
        act(A("r8"), A("pn", c(1024, 1032)), scale=1.0 / 32, bias=(129 - 2 * OFF - 0.4375) / 32)
        if t < STEPS - 1:
            names(0)
        group(A("pn", c(512, 520)), [(A("Ib"), A("Cl", c(0, 8))), (diag(t), A("dcm")), (A("lm"), A("dc128", c(0, 8)))])
        ts(A("sl16"), A("pn", c(512, 520)), 128.0 * POS[t] - 14336, O.add)
        cp(ind(A("W", c(VB, WEND)), A("sl16")), yb)
        act(nslot(t), A("e8"))
        due = [(A("pn", c(1024, 1032)), a, b) for a, b in ((yb, A("Bm32")), (A("I8k"), plain(t)), (A("I8k"), A("r8")), (A("nI8k"), over(t)))]
        if t == 1:
            change(t, due)
        else:
            group(due[0][0], [d[1:] for d in due])
        act(col("pri", t), A("pn", c(1024, 1032)), F.Relu, bias=KEY[t] - 32.0 * (t + 1) + 512 * OFF - 256 * 129 - 8192)
        if t < STEPS - 1:
            mm(A("pn", c(1536, 1664)), A(hn), A("nI"), True, True)
            act(A("hT"), A("pn", c(1536, 1664)))

    def drains(t):
        turns[:] = range(len(ops), len(ops) + NR)
        for q in range(NR - 1, -1, -1):
            cp(ind(A("W", c(0, VB)), A("rv", t, q, c(128, 136))), A("rv", t, q, c(0, 128)))
            if q == HITS and t < STEPS - 1:
                behind(*hits)

    for s in range(16):
        act(blk("KZ", s), A("Ib"), scale=float(VB + 128 * (POS[s] + 1)))
        if s >= 16 - NV[2]:
            ts(vslot(s), A("vv", c(s, None, 16)), OFF, O.add)
        else:
            act(vslot(s), A("vv", c(s, None, 16)), bias=OFF)
    fill(A("TP", c(128, 256, 16)), SLOT - 129 + POS[0])
    fill(blk("TP", 0), -NOFF)
    fill(A("tw"), 0.0)
    fill(blk("fr", 1), 0.0)
    E("g", "iota", out=A("Ur"), pattern=[[0, 512]], base=0, **small)
    act(A("I32k"), A("Ib"), scale=32768.0)
    ts(A("Ih"), A("dI"), 0, O.is_equal)
    ts(own, A("ms"), OFF, O.add)
    fill(A("on32"), 1.0)
    cp(K_("tf"), A("tI"))
    act(A("aq"), K_("tf"))
    act(K_("t1"), A("aq"), scale=-1.0, bias=K_("tf"))
    act(K_("t2"), A("aq"), scale=A("oh16", c(0, 1)))
    act(K_("t3"), K_("t1"), scale=A("oh16", c(1, 2)), bias=K_("t2"))
    mm(A("p5", c(0, 128)), A(H[0]), A("nI"), True, True)
    act(A("hT"), A("p5", c(0, 128)))
    act(A("B3", c(128, 256)), B)
    act(A("B3", c(256, 264)), A("dc"))
    act(A("nB3"), A("B3"), scale=-1.0)
    act(A("thc"), A("B3"), scale=K_("t3"))
    act(A("cq"), A("dl"), scale=16384.0, bias=-16384.0)
    E("g", "iota", out=A("W", c(DUMP, VB)), pattern=[[0, 128]], base=0, **small)
    for k in range(3):
        act(A("B16", c(8 * k, 8 * k + 8)), A("dc"), scale=4096.0)
    cp(A("x8"), A("mI", c(0, 8)))
    for n, x in (("ndc", -1), ("B8th", 0.125), ("Bm32", -32), ("dc64", 64), ("dcm", -1024)):
        act(A(n), A("dc"), scale=float(x))
    prepare(0, H[0])
    lists()
    before = len(ops)
    for n, (_, j, q) in enumerate(units):
        if n == LAST:
            late_units = len(ops)
        unpack(n, j, q)
    late_units = range(late_units, len(ops))
    first_terms()
    for t in range(STEPS):
        h, hn = H[t % 2], H[1 - t % 2]
        reads(t, h)
        if t == 0:
            used = {made[0]}
            for k in range(made[0], -1, -1):
                if k in used:
                    used.update(ops[k]["pre"])
            for u in late_units:
                for k in used:
                    if k < before and ops[k]["q"] == ops[u]["q"]:
                        ops[u]["pre"].setdefault(k, ops[k]["busy"])
        update(t, h, hn)
        if t < STEPS - 1:
            prepare(t + 1, hn)
        else:
            act(own, own, bias=-OFF)
            for s in range(16):
                if s % 8 < 5:
                    ts(A("vv", c(s, None, 16)), vslot(s), -OFF, O.add)
                else:
                    act(A("vv", c(s, None, 16)), vslot(s), bias=-OFF)
            E("y", "dma_start", out=ext("yh"), in_=A(hn))
            E("y", "dma_start", out=ext("yval"), in_=A("vv"))
            for s in (1, 0, 2):
                if s != 1:
                    change(s)
                group(A("pn", c(1072, 1088)), [(A("Ib"), first(s)), (A("Ib"), A("Ur", c(1, 256, 16))),
                                               (A("nI"), A("Ur", c(257, 512, 16)))])
                act(nslot(s), A("pn", c(1072, 1088)))
            group(A("pn", c(0, 128)), [(nlo, A("Ib")), (nh, A("I129"))])
            ts(A("sI"), A("pri"), -0.03125, O.mult, 32.0 - 31.0 / 64, O.add)
            ts(A("off"), A("sI"), 31.0, O.min)
            tr(A("pn", c(512, 640)), A("off"))
            act(A("f1"), A("pn", c(0, 128)), bias=-128 * OFF)
            cp(A("l1"), A("pn", c(512, 640)))
            E("y", "dma_start", out=ext("ydue"), in_=A("l1"))
            E("y", "dma_start", out=ext("ypnd"), in_=A("f1"))
        drains(t)
        if t < STEPS - 1:
            lists()
            first_terms()
    E("y", "dma_start", out=ext("ymem"), in_=own)
    issue()
    g.wait_ge(T.sem.lsA, 2 * len(e8))
    g.wait_ge(T.sem.lsH, len(e8 + loc))
    g.wait_ge(T.sem.lsD, STEPS * (2 * len(e8) + len(loc)))
    for k in range(ndma[0]):
        if not any(seen[q].get("dm%d" % k, 0) for q in Q):
            g.sync.wait_ge(T.sem["dm%d" % k], 16)
    for q in "gvst":
        if cnt.get("q" + q, 0) > max(seen[o].get("q" + q, 0) for o in Q):
            g.sync.wait_ge(T.sem["q" + q], cnt["q" + q])
